import numpy as np, ml_dtypes
CORES = [10,34,74,98]
N = 4
import mx_ref
BF = ml_dtypes.bfloat16
def pick(q, e):
    c = np.concatenate([q[0].reshape(128, -1, 4), np.zeros((128, 1, 4), np.uint8)], axis=1); s = np.concatenate([q[1], np.ones((16, 1), np.uint8)], axis=1)
    return (np.ascontiguousarray(c[:, e].reshape(128, -1)), np.ascontiguousarray(s[:, e]))
def join(*qs):
    return (np.concatenate([q[0] for q in qs], axis=1), np.concatenate([q[1] for q in qs], axis=1))
def put(q, e, v):
    c, s = q[0].reshape(128, -1, 4).copy(), q[1].copy(); c[:, e] = v[0].reshape(128, -1, 4); s[:, e] = v[1]
    return (c.reshape(128, -1), s)
def pk(c, s):
    return (np.ascontiguousarray(c), mx_ref.live(s))
def emit(q):
    return q[0], q[1]
def decode(q):
    o = []
    for b in range(4):
        e = np.zeros((128, 128, 4), np.float32); e[np.arange(128), np.arange(128), b] = 1
        o.append(mx_ref.matmul(mx_ref.quantize(e.reshape(128, 512).astype(BF)), q))
    return np.stack(o, axis=2).reshape(128, -1)
def f(rng, *shape):
    return mx_ref.flush((rng.standard_normal(shape, dtype=np.float32) * np.exp2(rng.integers(-2, 3, shape[:-1] + (1,)))).astype(BF))
def wide(rng, *shape, cols=0):
    v = rng.standard_normal(shape, dtype=np.float32) * np.exp2(rng.integers(-12, 13, shape)).astype(np.float32)
    if cols: v *= np.repeat(np.exp2(rng.integers(-cols, cols + 1, shape[:-2] + (1, shape[-1] // 4))) * (rng.random(shape[:-2] + (1, shape[-1] // 4)) > 0.0625), 4, axis=-1).astype(np.float32)
    return mx_ref.flush(v.astype(BF))
I, B, K, M, R = 48, 384, 12, 8, 3
H = M + M // 2
def least(v):
    v = np.array(v)
    v[np.abs(v.astype(np.float32)) < np.float32(2.0 ** -12)] = 0
    return v
def plain(rng):
    return {"it": least(f(rng, N, 128, 4 * I)), "x": least(f(rng, N, 128, 4 * B)), "w": f(rng, N, 128, 512)}
def lay(m):
    return np.ascontiguousarray(m.reshape(N, 128, 4, -1).transpose(0, 1, 3, 2)).reshape(N, 128, -1).astype(np.float32).astype(BF)
def goods(at):
    m = np.zeros((N, 512, I))
    for q in range(N):
        e = at[I * q:I * q + I]
        m[q, e, np.arange(I)] = 16
        m[q, 256 + e, np.arange(I)] = 2.0 ** -7
    return m
def wishes(at, goal, size, fine):
    m = np.zeros((N, 512, B))
    for r in range(N):
        m[r, at[goal[r]], np.arange(B)] = size[r]
        m[r, 256 + at[goal[r]], np.arange(B)] = fine[r]
    return m
def hot(rng, owners):
    return np.concatenate([I * q + rng.permutation(I)[:H] for q in owners])
def setup_inputs(rng):
    return plain(rng)
def setup_inputs_again(rng):
    at, owners = rng.permutation(256), rng.permutation(N)
    goal = I * owners[rng.integers(0, 2, (N, B))] + rng.integers(0, I, (N, B))
    size = np.full((N, B), 2.0)
    s = np.tile(1 + (np.arange(H) < H // 2), 2)
    e = hot(rng, owners[:2])
    slots = np.concatenate([[0], 1 + rng.permutation(N * K - 1)[:4 * H - 1]])
    number = np.stack([np.concatenate([[0], 1 + rng.permutation(B - 1)[:K - 1]])] + [rng.permutation(B)[:K] for r in range(1, N)])[slots // K, slots % K]
    goal[slots // K, number] = np.concatenate([e, e])
    size[slots // K, number] = 16 * np.concatenate([8 * s, 7 * s])
    return {**plain(rng), "it": lay(goods(at)), "x": lay(wishes(at, goal, size, np.zeros((N, B))))}
def setup_inputs_below(rng):
    d = plain(rng)
    low = np.argsort(rng.random((N, 128, I)), axis=1) < 64
    half = np.argsort(rng.random((N, 128, B)), axis=1) < 64
    e = rng.permutation(np.concatenate([I * q + rng.permutation(I)[:K] for q in range(N)])).reshape(N, K)
    for r in range(N):
        b = rng.permutation(B)[:K]
        half[r][:, b] = low[e[r] // I, :, e[r] % I].T
    d["it"] = ((1 + 0.25 * rng.random((N, 128, 4 * I)) + np.where(np.repeat(low, 4, axis=2), 0.0, 0.75)) * 2.0 ** 29).astype(np.float32).astype(BF)
    d["x"] = (-(1 + rng.random((N, 128, 4 * B))) * 2.0 ** 29 * np.repeat(half, 4, axis=2)).astype(np.float32)
    d["x"][d["x"] == 0] = 0
    d["x"] = d["x"].astype(BF)
    return d
def setup_inputs_near(rng):
    at, o = rng.permutation(256), int(rng.integers(0, N - 1))
    pool = I * o + np.sort(rng.permutation(I)[:2 * K])
    goal, size, fine = rng.integers(0, N * I, (N, B)), np.full((N, B), 16.0), np.zeros((N, B))
    for r in range(1, N):
        b = K + rng.permutation(B - K)[:K]
        goal[r, b] = pool[K:] if r % 2 == (N - 1) % 2 else pool[:K]
        fine[r, b] = r * 2.0 ** -7
    m = wishes(at, goal, size, fine)
    q = I * ((o + 1) % N)
    i = rng.integers(0, I - 1, B)
    j = rng.integers(i + 1, I)
    n = rng.integers(1, 8, B)
    n[:K] = 1
    n[B - K:] = 8
    m[0] = 0
    m[0, at[q + i], np.arange(B)] = 16
    m[0, at[q + j], np.arange(B)] = 16
    m[0, 256 + at[q + j], np.arange(B)] = n * 2.0 ** -7
    return {**plain(rng), "it": lay(goods(at)), "x": lay(m)}
def setup_inputs_ties(rng):
    at, owners, z = rng.permutation(256), rng.permutation(N), int(rng.integers(0, N))
    goal = rng.integers(0, N * I, (N, B))
    e = np.resize(rng.permutation(hot(rng, owners[:2])), (N - 1) * K).reshape(N - 1, K)
    goal[np.arange(N) != z, :K] = rng.permuted(e, axis=1)
    m = wishes(at, goal, np.full((N, B), 16.0), np.zeros((N, B)))
    m[z] = 0
    for q in owners[2:4]:
        e = rng.integers(0, I, B)
        e[:2] = np.min(e[:K])
        m[z, at[I * q + e], np.arange(B)] = 16
    return {**plain(rng), "it": lay(goods(at)), "x": lay(m)}
def setup_inputs_spread(rng):
    return {**plain(rng), "it": least(wide(rng, N, 128, 4 * I, cols=4)), "x": least(wide(rng, N, 128, 4 * B, cols=4))}
def check_inputs(d):
    b = []
    for k, low in (("it", 2.0 ** -12), ("x", 2.0 ** -12), ("w", 2.0 ** -30)):
        v = np.abs(d[k].astype(np.float32))
        if not (np.isfinite(v).all() and ((v == 0) | (v >= low) & (v <= 2.0 ** 30)).all()): b.append("a value of " + k)
    return b
def values(xq, g, price):
    s = np.concatenate([mx_ref.matmul(pick(xq, np.arange(128 * i, 128 * i + 128)), g) for i in range(B // 128)])
    return s + np.float32(0) - price
def reference(it, x, w):
    xq = [mx_ref.quantize(np.ascontiguousarray(x[r])) for r in range(N)]
    g = join(*[mx_ref.quantize(np.ascontiguousarray(it[q])) for q in range(N)])
    price, holder, free = np.zeros(N * I, np.float32), np.full(N * I, -1), np.ones((N, B), bool)
    ho, pr = np.zeros((N, R, I), np.float32), np.zeros((N, R, I), np.float32)
    every = np.arange(B)
    for t in range(R):
        best, who = np.zeros(N * I, np.float32), np.full(N * I, -1)
        for r in range(N):
            v = values(xq[r], g, price)
            goal = np.argmax(v, axis=1)
            large = v[every, goal]
            v[every, goal] = -np.inf
            bid = large - np.max(v, axis=1)
            c = np.flatnonzero(free[r])
            for b in c[np.argsort(-bid[c], kind="stable")[:K]]:
                i = goal[b]
                if who[i] < 0 or bid[b] > best[i]: best[i], who[i] = bid[b], B * r + b
        sold = []
        for q in range(N):
            c = np.arange(I * q, I * q + I)
            c = c[who[c] >= 0]
            sold.extend(c[np.argsort(-best[c], kind="stable")[:M]].tolist())
        n = len(sold)
        buyers = join(*[pick(xq[who[i] // B], np.array([who[i] % B])) for i in sold])
        none = np.full(N * M - n, -1)
        old = decode(pick(g, np.concatenate([np.array(sold), none])))
        new = np.float32(0.5) * (old + decode(pick(buyers, np.concatenate([np.arange(n), none]))))
        g = put(g, np.array(sold), pick(mx_ref.quantize(np.ascontiguousarray(new.astype(BF))), np.arange(n)))
        for i in sold:
            if holder[i] >= 0: free[holder[i] // B, holder[i] % B] = True
            free[who[i] // B, who[i] % B] = False
            holder[i] = who[i]
            price[i] = price[i] + best[i]
        ho[:, t], pr[:, t] = holder.reshape(N, I), price.reshape(N, I)
    y = np.stack([mx_ref.matmul(mx_ref.quantize(np.ascontiguousarray(w[r])), g) for r in range(N)])
    own = [emit(pick(g, np.arange(I * q, I * q + I))) for q in range(N)]
    return {"y": y, "oc": np.stack([a for a, b in own]), "osc": np.stack([b for a, b in own]), "ho": ho, "pr": pr}

@@ -1,0 +1,495 @@
+from concourse.bass import DstId, RemoteDMATransfer
+from concourse.mybir import dt, AluOpType, AxisListType, ActivationFunctionType
+
+NI, NB, NK, NM, NR = 48, 384, 12, 8, 3
+C4, U8, F32, BF, U16, I32 = "float8_e4m3fn_x4", "uint8", "float32", "bfloat16", "uint16", "int32"
+PW = 464
+OWN = 336
+
+
+def _s(n, d):
+    return ("sbuf", [128, n], d)
+
+
+SCRATCH = {
+    "ti": _s(512, BF), "tx": _s(1536, BF), "tw": _s(512, BF), "te": _s(1040, BF), "tn": _s(512, BF),
+    "iq": _s(128, C4), "isc": _s(128, U8), "xq": _s(384, C4), "xs": _s(384, U8), "xpq": _s(384, C4), "xps": _s(384, U8),
+    "wq": _s(128, C4), "ws": _s(128, U8), "eq": _s(512, C4), "es": _s(512, U8),
+    "pq0": _s(PW, C4), "pz0": _s(PW, U8), "pq1": _s(PW, C4), "pz1": _s(PW, U8), "pq2": _s(PW, C4), "pz2": _s(PW, U8),
+    "pq3": _s(192, C4), "pz3": _s(192, U8),
+    "hdx": _s(1536, BF), "hdv": _s(768, BF), "gv": _s(64, F32),
+    "psS": ("psum", [128, 1536], F32), "psD": ("psum", [128, 2048], F32), "psY": ("psum", [128, 512], F32),
+    "pint": _s(8, I32), "bint": _s(8, I32), "bits": _s(8, F32), "row": _s(288, F32), "ep": _s(24, F32), "pf": _s(8, F32),
+    "cf": _s(64, F32), "co": _s(64, U16), "cu": _s(2, U16), "k": _s(48, F32), "neg": _s(192, F32), "pat": _s(64, F32),
+    "od1": _s(288, BF), "od2": _s(128, BF), "mv": _s(64, F32),
+    "v": _s(576, F32), "pm": _s(576, F32), "qm": _s(576, F32), "jk": _s(576, BF), "sg": _s(288, BF), "ee": _s(288, BF),
+    "g3": _s(8, F32), "a3": _s(8, F32), "x1": _s(96, F32), "r1": _s(96, F32),
+    "m1": _s(192, F32), "t1": _s(192, F32), "c8": _s(8, F32), "x2": _s(80, F32), "r2": _s(64, F32), "d2": _s(16, F32),
+    "m2": _s(192, F32), "t2": _s(192, F32), "land": _s(48, F32), "gl": _s(8, U16), "xl": _s(2, U16),
+    "xs3": _s(128, F32), "rs": _s(128, F32), "tt": _s(256, F32), "mb": _s(256, F32), "pb": _s(256, F32), "sm": _s(64, F32),
+    "zz": _s(8, F32), "xz": _s(64, F32), "rz": _s(64, F32), "g4": _s(8, U16), "of": _s(4, U16),
+    "wm": _s(288, F32), "tm": _s(224, F32), "ml": _s(48, U16), "xh": _s(192, F32),
+    "pp0": _s(384, F32), "pp1": _s(384, F32), "hp0": _s(384, F32), "hp1": _s(384, F32),
+    "fu": _s(144, F32), "fj": _s(144, BF), "fm": _s(8, F32), "fe": _s(96, F32), "cb": _s(32, F32), "yo": _s(192, F32),
+}
+POOLS = {"v": 44, "a": 36, "p": 10, "g": 6, "sd": 14, "ad": 8}
+SEMAPHORES = [q + str(i) for q in POOLS for i in range(POOLS[q])] + ["sent", "items"] + \
+    ["bids%d" % t for t in range(NR)] + ["cols%d" % t for t in range(NR)]
+MAGIC = 12582912.0
+BIG = 2.0 ** 80
+
+
+def rank_program(g, core, T, topo):
+    me = T.rank_of(core)
+    if me is None:
+        return
+    N = len(T.cores)
+    A, F = AluOpType, ActivationFunctionType
+    peers = [r for r in range(N) if r != me]
+    engs = [e for e in topo.engines(core, T.cores[peers[0]]) if all(e in topo.engines(core, T.cores[r]) for r in peers)]
+    ids = [DstId(rid=topo.addr(T.cores[r])[0], pnc=topo.addr(T.cores[r])[1]) for r in peers]
+
+    def bitmask(es):
+        return sum(1 << e for e in es)
+
+    ops = []
+
+    def V(name, a=0, b=None, step=1, p0=0, p1=128):
+        b = SCRATCH[name][1][1] if b is None else b
+        if SCRATCH[name][0] == "psum":
+            reg = (name, 0, 128, frozenset([a // 512]))
+        else:
+            reg = (name, p0, p1, frozenset(range(a, b, step)))
+        return (T[name][p0:p1, a:b:step] if step > 1 else T[name][p0:p1, a:b], [reg])
+
+    def col(name, a):
+        return V(name, a, a + 1)
+
+    def blk(name, n, j):
+        return V(name, n * j, n * j + n)
+
+    def ind(w, o):
+        return (w[0].indirect(o[0]), w[1] + o[1])
+
+    def b8(w):
+        return (w[0].bitcast(dt.uint8), w[1])
+
+    def b32(w):
+        return (w[0].bitcast(dt.uint32), w[1])
+
+    def ap(x):
+        return x[0] if isinstance(x, tuple) else x
+
+    def rec(q, fn, wr, rd, kind="c", ext=None):
+        r = [z for x in rd if isinstance(x, tuple) for z in x[1]]
+        w = [z for x in wr for z in x[1]]
+        w = w + [z for z in r if SCRATCH[z[0]][0] == "psum"]
+        ops.append({"q": q, "fn": fn, "w": w, "r": r, "kind": kind, "ext": ext})
+
+    vec, act, pe = g.vector, g.scalar, g.tensor
+
+    def ts(o, i, s1, op0, s2=None, op1=None):
+        if op1 is None:
+            rec("v", lambda: vec.tensor_scalar(o[0], i[0], ap(s1), None, op0), [o], [i, s1])
+        else:
+            rec("v", lambda: vec.tensor_scalar(o[0], i[0], ap(s1), ap(s2), op0, op1), [o], [i, s1, s2])
+
+    def tt(o, a, b, op):
+        rec("v", lambda: vec.tensor_tensor(o[0], a[0], b[0], op), [o], [a, b])
+
+    def cp(o, i):
+        rec("v", lambda: vec.tensor_copy(o[0], i[0]), [o], [i])
+
+    def ms(o, c):
+        rec("v", lambda: vec.memset(o[0], c), [o], [])
+
+    def tr(o, i):
+        rec("v", lambda: vec.transpose(o[0], i[0]), [o], [i])
+
+    def red(o, i, op):
+        rec("v", lambda: vec.tensor_reduce(o[0], i[0], AxisListType.X, op), [o], [i])
+
+    def scan(o, a, b, op0, op1):
+        rec("v", lambda: vec.tensor_tensor_scan(o[0], a[0], b[0], -1e29, op0, op1), [o], [a, b])
+
+    def quant(q, s, i):
+        rec("v", lambda: vec.quantize_mx(q[0], s[0], i[0]), [q, s], [i])
+
+    def ac(o, i, f, bias=None, scale=None, acc=None):
+        kw = {}
+        if bias is not None:
+            kw["bias"] = ap(bias)
+        if scale is not None:
+            kw["scale"] = ap(scale)
+        if acc is not None:
+            kw["accum_out"] = acc[0]
+        rec("a", lambda: act.activation(o[0], i[0], f, **kw), [o] + ([acc] if acc is not None else []), [i, bias, scale])
+
+    def mm(o, lq, ls, rq, rs):
+        rec("p", lambda: pe.matmul_mx(o[0], lq[0], ls[0], rq[0], rs[0], True, True), [o], [lq, ls, rq, rs])
+
+    def iota(o, pattern, cm, **kw):
+        rec("g", lambda: g.iota(o[0], pattern, 0, cm, **kw), [o], [])
+
+    def load(q, o, src):
+        e = g.sync if q == "s" else act
+        rec(q, lambda: e.dma_start(o[0], src), [o], [], kind="d")
+
+    def store(q, dst, i):
+        e = g.sync if q == "s" else act
+        rec(q, lambda: e.dma_start(dst, i[0]), [], [i], kind="o")
+
+    sent = [0]
+
+    def send(s, d, sem):
+        trs = [RemoteDMATransfer(dst_ids=ids, dma_engine_mask=bitmask(engs), remote_sem=T.sem[sem], srcs=[s[0]], dsts=[d(r)[0] for r in peers])]
+        sent[0] += len(engs)
+        rec("g", lambda: g.remote_dma_fused(trs, local_sem=T.sem.sent), [], [s], kind="r")
+
+    def arrive(sem, calls, views):
+        rec(None, None, views, [], kind="x", ext=(sem, calls * len(engs) * len(peers)))
+
+    def pick(oq, oz, wq, wz, lst):
+        ac(oz, ind(wz, lst), F.Copy)
+        cp(b32(oq), ind(b32(wq), lst))
+
+    def place(r, at):
+        return 192 + 48 * ((r - at - 1) % N)
+
+    load("s", V("ti", 0, 192), T.it[:])
+    load("a", V("tx"), T.x[:])
+    load("s", V("tw"), T.w[:])
+    iota(col("pint", 0), [[0, 1]], 1)
+    iota(V("row"), [[1, 288]], 0, allow_small_or_imprecise_dtypes=True)
+    iota(V("ep"), [[32, 3], [96, 4], [16, 2]], 0, allow_small_or_imprecise_dtypes=True)
+    ms(V("ti", 192, 512), 0.0)
+    ms(V("te"), 0.0)
+    for j, (sh, m) in enumerate([(4, 1), (4, 1), (5, 1), (6, 1), (0, 15), (0, 31), (0, 127)]):
+        ts(col("bint", j), col("pint", 0), sh, A.logical_shift_right, m, A.bitwise_and)
+    cp(V("bits", 0, 7), V("bint", 0, 7))
+    h, hh, q0, q1, s16, s32, pf = col("bits", 0), V("bits", 0, 2), col("bits", 2), col("bits", 3), col("bits", 4), col("bits", 5), col("bits", 6)
+    E_I, E_P, E_2, E_S, E_Z, E_H = 0, 4, 28, 40, 48, 52
+    KC, NG, CP, DM, GD, X0, SH, PAD = 0, 4, 8, 12, 16, 20, 24, 25
+    ms(V("cf", 0, 4), 0.0)
+    ts(V("cf", E_I, E_I + 3), V("row", 0, 48, 16), s16, A.add)
+    ts(V("cf", E_P, E_P + 24), V("ep"), s16, A.add)
+    ts(V("te", 2, 514, 4), V("row", 0, 128), pf, A.is_equal)
+    cp(V("co", 0, 28), V("cf", 0, 28))
+    ts(V("te", 523, 1035, 4), V("row", 0, 128), pf, A.is_equal)
+    quant(V("iq"), V("isc"), V("ti"))
+    send(b8(V("iq", 0, NI)), lambda r: b8(blk("pq0", NI, me)), "items")
+    send(V("isc", 0, NI), lambda r: blk("pz0", NI, me), "items")
+    for b, a in enumerate([2, 522, 0, 520]):
+        quant(blk("eq", 128, b), blk("es", 128, b), V("te", a, a + 512))
+    pick(blk("pq0", NI, me), blk("pz0", NI, me), V("iq"), V("isc"), V("co", E_I, E_I + 3))
+    quant(V("xq"), V("xs"), V("tx"))
+    ms(V("neg"), -1e29)
+    pick(V("xpq"), V("xps"), V("xq"), V("xs"), V("co", E_P, E_P + 24))
+    for b in range(4):
+        mm(V("psD", 512 * b, 512 * b + NB), blk("eq", 128, b), blk("es", 128, b), V("xq"), V("xs"))
+    for b in range(4):
+        ac(blk("hdx", NB, b), V("psD", 512 * b, 512 * b + NB), F.Copy, scale=0.5)
+    ts(col("k", 26), pf, s32, A.subtract, 3.0, A.mult)
+    ts(col("k", X0), q0, h, A.not_equal, 4.0, A.mult)
+    ts(V("pf", 0, 3), V("row", 0, 96, 32), s32, A.add)
+    ms(V("fe"), 0.0)
+    ts(col("k", 27), col("k", 26), s32, A.add)
+    ts(col("k", 32), q1, 2.0, A.mult, col("k", X0), A.add)
+    ts(col("k", 33), q1, -2.0, A.mult, col("k", X0), A.add)
+    for kk in range(3):
+        ts(blk("od1", 96, kk), V("row", 0, 96), col("pf", kk), A.is_ge, -0.5, A.add)
+    ts(V("k", KC, KC + 3), V("row", 0, 96, 32), col("k", 27), A.add, 320.0, A.add)
+    ts(col("k", 34), col("k", 33), 2.0, A.add)
+    ts(V("cf", E_2, E_2 + 2), hh, 0.0, A.mult, col("k", 32), A.add)
+    for b in range(2):
+        ts(blk("od2", 64, b), V("row", 0, 64), col("pf", b), A.is_ge, -0.5, A.add)
+    ts(V("cf", E_2 + 2, E_2 + 4), hh, 0.0, A.mult, col("k", 34), A.add)
+    ts(col("k", 35), col("k", 34), col("k", 32), A.subtract)
+    for j in range(2):
+        ts(blk("pat", 16, j), V("row", 0, 16), -2.0, A.mult, 96.0, A.add)
+    ts(col("k", 36), s16, 1.0, A.min, col("k", 35), A.mult)
+    ms(V("pat", 32, 64), 999.0)
+    ms(col("land", 4 * me + 3), 0.0)
+    ts(col("cf", E_2 + 4), col("k", 36), col("k", 32), A.add, 1.0, A.add)
+    for j in range(2):
+        ts(V("pat", 32 + 16 * j, 32 + 16 * j + NK), V("row", 0, NK), -2.0, A.mult, 64.0, A.add)
+    cp(V("co", E_2, E_2 + 5), V("cf", E_2, E_2 + 5))
+    ms(V("gl"), 0)
+    ms(V("tn"), 0.0)
+
+    def later():
+        ts(col("k", PAD), s16, float(NK), A.is_ge, 1000.0, A.mult)
+        ts(V("k", DM, DM + 4), V("row", 224, 288, 16), s16, A.add)
+        ts(col("k", SH), h, 16.0, A.mult, -16.0, A.add)
+        ts(col("k", 37), s16, h, A.subtract, 16.0, A.mult)
+        for b in range(2):
+            for f in range(2):
+                ts(V("cf", E_S + 4 * f + 2 * b, E_S + 4 * f + 2 * b + 2), hh, 4.0, A.mult, float(8 * b + f), A.add)
+            ts(V("cf", E_Z + 2 * b, E_Z + 2 * b + 2), hh, float(2 * b), A.add)
+        for b in range(6):
+            c = [4 * ((me + 1 + m // 3) % N) + 2 if m % 3 == 0 else 2 for m in (2 * b, 2 * b + 1)]
+            ts(V("cf", E_H + 2 * b, E_H + 2 * b + 2), hh, float(c[1] - c[0]), A.mult, float(c[0]), A.add)
+        ts(V("k", CP, CP + 4), V("row", 0, 64, 16), s16, A.add, col("k", PAD), A.add)
+        ts(V("k", 28, 32), V("k", DM, DM + 4), col("k", SH), A.add, 1.0, A.add)
+        ts(col("k", 38), col("k", 37), 16.0, A.add, 208.0, A.min)
+        cp(V("co", E_S, 64), V("cf", E_S, 64))
+        ts(V("k", GD, GD + 4), V("k", 28, 32), -1.0, A.mult)
+        cp(col("cu", 0), col("k", 38))
+        ms(V("zz", 4, 8), 0.0)
+        ms(V("pp0"), 0.0)
+        for r in range(N):
+            ts(blk("mv", 16, r), V("row", 0, 16), float(place(r, me)), A.add)
+        ms(V("hp0", 0, 192), -1.0)
+
+    def latest():
+        ts(V("k", NG, NG + 3), V("k", KC, KC + 3), -1.0, A.mult, 320.0 - NB * me, A.add)
+        ms(V("cb"), BIG)
+        ms(col("k", 40), -16 * BIG)
+        ms(col("k", 41), -48 * BIG)
+        ms(V("land", 16 + 4 * me + 3, 48, 16), 0.0)
+        ms(V("pp1", 192, 384), 0.0)
+
+    arrive("items", 2, [blk(n, NI, r) for n in ("pq0", "pz0") for r in peers])
+
+    for t in range(NR):
+        pq, pz, nq, nz = "pq%d" % t, "pz%d" % t, "pq%d" % (t + 1), "pz%d" % (t + 1)
+        pp, np_, hp, nh = "pp%d" % (t % 2), "pp%d" % (1 - t % 2), "hp%d" % (t % 2), "hp%d" % (1 - t % 2)
+        L = 16 * t
+        for kk in range(3):
+            mm(V("psS", 512 * kk, 512 * kk + 192), blk("xpq", 128, kk), blk("xps", 128, kk), V(pq, 0, 192), V(pz, 0, 192))
+        for b in range(4):
+            mm(V("psD", 512 * b, 512 * b + 192), blk("eq", 128, b), blk("es", 128, b), V(pq, 0, 192), V(pz, 0, 192))
+
+        def val(kk):
+            tt(blk("v", 192, kk), V("psS", 512 * kk, 512 * kk + 192), V(pp, 0, 192), A.subtract)
+
+        def src(kk, a):
+            return V("v", 192 * kk + a, 192 * kk + 192) if t else V("psS", 512 * kk + a, 512 * kk + 192)
+
+        def first(kk):
+            scan(blk("pm", 192, kk), src(kk, 0), src(kk, 0) if t else V("neg"), A.max, A.max)
+            ac(blk("jk", 192, kk), blk("pm", 192, kk), F.Sign, bias=col("pm", 192 * kk + 191), scale=-1.0, acc=col("g3", kk))
+
+        def second(kk):
+            scan(V("qm", 192 * kk, 192 * kk + 191), src(kk, 1), V("pm", 192 * kk, 192 * kk + 191), A.max, A.min)
+
+        def bid(kk):
+            ts(blk("x1", 32, kk), blk("fe", 32, kk), col("pm", 192 * kk + 191), A.add, col("qm", 192 * kk + 190), A.subtract)
+
+        if t:
+            val(0)
+            val(1)
+            first(0)
+            val(2)
+            first(1)
+            second(0)
+            first(2)
+        else:
+            first(0)
+            first(1)
+            first(2)
+            second(0)
+        second(1)
+        bid(0)
+        second(2)
+        bid(1)
+        tr(blk("r1", 32, 0), blk("x1", 32, 0))
+        bid(2)
+        tr(blk("r1", 32, 1), blk("x1", 32, 1))
+        tr(blk("r1", 32, 2), blk("x1", 32, 2))
+        for kk in range(3):
+            ac(col("g3", 4 + kk), col("g3", kk), F.Identity, bias=col("k", KC + kk), scale=512.0)
+        for kk in range(3):
+            ac(blk("sg", 96, kk), V("r1"), F.Sign, bias=col("x1", 32 * kk), scale=-1.0)
+        for kk in range(3):
+            tt(blk("ee", 96, kk), blk("sg", 96, kk), blk("od1", 96, kk), A.add)
+            ac(blk("jk", 96, kk), blk("ee", 96, kk), F.Sign, acc=col("a3", kk))
+        for kk in range(3):
+            ts(blk("m1", 32, kk), V("pat", 0, 32), col("a3", kk), A.is_equal, col("x1", 32 * kk), A.mult)
+            ts(blk("m1", 32, 3 + kk), V("pat", 0, 32), col("a3", kk), A.is_equal, col("g3", 4 + kk), A.mult)
+        for b in range(3):
+            ac(blk("hdv", 192, b), V("psD", 512 * b, 512 * b + 192), F.Copy, scale=0.5)
+        tr(V("t1", 0, 96), V("m1", 0, 96))
+        tr(V("t1", 96, 192), V("m1", 96, 192))
+        red(col("c8", 0), V("t1", 0, 96), A.add)
+        red(col("c8", 1), V("t1", 96, 192), A.add)
+        cp(V("c8", 2, 4, 1, 0, 64), V("c8", 0, 2, 1, 64, 128))
+        ac(V("c8", 2, 4, 1, 64, 128), V("c8", 0, 2, 1, 0, 64), F.Copy)
+        cp(V("c8", 4, 8, 1, 0, 32), V("c8", 0, 4, 1, 32, 64))
+        ac(V("c8", 4, 8, 1, 64, 96), V("c8", 0, 4, 1, 96, 128), F.Copy)
+        cp(V("c8", 4, 8, 1, 32, 64), V("c8", 0, 4, 1, 0, 32))
+        ac(V("c8", 4, 8, 1, 96, 128), V("c8", 0, 4, 1, 64, 96), F.Copy)
+        cp(V("x2"), ind(V("c8"), V("co", E_2, E_2 + 5)))
+        ac(blk("hdv", 192, 3), V("psD", 1536, 1536 + 192), F.Copy, scale=0.5)
+        tr(V("r2"), V("x2", 0, 64))
+        ts(V("d2", 0, 2), V("x2", 64, 66), 1.0 / 512, A.mult, MAGIC, A.add)
+        for b in range(2):
+            ac(blk("sg", 64, b), V("r2"), F.Sign, bias=col("x2", 32 * b), scale=-1.0)
+        ts(V("d2", 4, 6), V("d2", 0, 2), -MAGIC, A.add, -512.0, A.mult)
+        ts(V("d2", 2, 4), V("d2", 0, 2), -MAGIC, A.add)
+        for b in range(2):
+            tt(blk("ee", 64, b), blk("sg", 64, b), blk("od2", 64, b), A.add)
+            ac(blk("jk", 64, b), blk("ee", 64, b), F.Sign, acc=col("a3", 4 + b))
+        for b in range(2):
+            ts(col("d2", 6 + b), col("d2", 4 + b), col("x2", 64 + b), A.add, 192.0 + NB * me, A.add)
+        for b in range(2):
+            for f, fld in enumerate([col("x2", 32 * b), col("d2", 2 + b), col("d2", 6 + b)]):
+                ts(blk("m2", 32, 2 * f + b), V("pat", 32, 64), col("a3", 4 + b), A.is_equal, fld, A.mult)
+        for f in range(3):
+            tr(blk("t2", 64, f), blk("m2", 64, f))
+        for f in range(3):
+            red(col("land", L + 4 * me + f), blk("t2", 64, f), A.add)
+        mine = V("land", L + 4 * me, L + 4 * me + 4)
+        send(mine, lambda r: mine, "bids%d" % t)
+        ts(col("gl", 2 * t), col("land", L + 4 * me + 1), -1.0, A.add, 0.0, A.max)
+        ts(col("xl", 0), col("land", L + 4 * me + 2), -float(NB * me), A.add, 0.0, A.max)
+        for b in range(4):
+            ac(blk("gv", 16, b), ind(blk("hdv", 192, b), col("gl", 2 * t)), F.Copy)
+        for b in range(4):
+            tt(V("tn", b, 64, 4), ind(blk("hdx", NB, b), col("xl", 0)), blk("gv", 16, b), A.add)
+        quant(V(pq, OWN, PW), V(pz, OWN, PW), V("tn"))
+        send(b8(V(pq, OWN, OWN + NK)), lambda r: b8(V(pq, place(me, r), place(me, r) + NK)), "cols%d" % t)
+        send(V(pz, OWN, OWN + NK), lambda r: V(pz, place(me, r), place(me, r) + NK), "cols%d" % t)
+        if t == 0:
+            later()
+            latest()
+        if t == 1:
+            quant(V("wq"), V("ws"), V("tw"))
+        ac(V("wm"), V("row"), F.Relu, bias=col("k", SH))
+        arrive("bids%d" % t, 1, [V("land", L + 4 * r, L + 4 * r + 4) for r in peers])
+        lw, goal = V("land", L, L + 16), V("land", L + 1, L + 16, 4)
+        cp(V("xs3", 64, 128), ind(lw, V("co", E_S + 4, E_S + 8)))
+        ac(V("xs3", 0, 64), ind(lw, V("co", E_S, E_S + 4)), F.Copy)
+        ac(V("sm", 0, 4), goal, F.Copy, scale=-BIG)
+        tr(V("rs", 64, 128), V("xs3", 64, 128))
+        tr(V("rs", 0, 64), V("xs3", 0, 64))
+        for r in range(N):
+            ac(blk("tt", 64, r), V("rs", 64, 128), F.Abs, bias=col("sm", r), scale=BIG)
+        ts(V("sm", 4, 8), goal, -24.5, A.add, 1.0 / NI, A.mult)
+        for r in range(N):
+            ac(blk("jk", 64, r), V("rs", 0, 64), F.Sign, bias=col("land", L + 4 * r), scale=-1.0, acc=col("sm", 24 + r))
+
+        def masked(r):
+            tt(blk("mb", 64, r), V("rs", 0, 64), blk("tt", 64, r), A.subtract)
+
+        def best(r):
+            scan(blk("pb", 64, r), blk("mb", 64, r), blk("mb", 64, r), A.max, A.max)
+            ac(blk("jk", 64, 4 + r), blk("pb", 64, r), F.Sign, bias=col("pb", 64 * r + 63), scale=-1.0, acc=col("sm", 32 + r))
+
+        masked(0)
+        masked(1)
+        best(0)
+        masked(2)
+        best(1)
+        masked(3)
+        best(2)
+        ts(V("sm", 8, 12), V("sm", 4, 8), MAGIC, A.add)
+        best(3)
+        ts(V("sm", 12, 16), goal, 2.0 ** -20, A.mult, 2.0 ** -6, A.add)
+        ts(V("sm", 16, 20), V("sm", 8, 12), -MAGIC, A.add, 1.0 / 16, A.mult)
+        ts(V("sm", 28, 32), V("sm", 24, 28), -2.0 ** -12, A.mult)
+        tt(V("sm", 20, 24), V("sm", 12, 16), V("sm", 16, 20), A.add)
+        ts(V("sm", 40, 44), V("sm", 16, 20), -2.0 ** -21, A.add)
+        tt(V("sm", 36, 40), V("sm", 20, 24), V("sm", 28, 32), A.add)
+        ts(V("g4", 0, 7, 2), goal, -1.0, A.add, 0.0, A.max)
+        for r in range(N):
+            ts(col("zz", r), col("sm", 32 + r), col("k", CP + r), A.not_equal, col("sm", 36 + r), A.add)
+        cp(V("xz"), ind(V("zz"), V("co", E_Z, E_Z + 4)))
+        ac(V("xh"), ind(lw, V("co", E_H, E_H + 12)), F.Copy)
+        tt(V("sm", 44, 48), goal, V("k", GD, GD + 4), A.add)
+        tr(V("rz"), V("xz"))
+        for r in range(N):
+            ac(blk("jk", 64, r), V("rz"), F.Sign, bias=col("zz", r), scale=-1.0, acc=col("sm", 48 + r))
+            ac(blk("jk", 64, 4 + r), V("rz"), F.Sign, bias=col("sm", 40 + r), scale=-1.0, acc=col("sm", 52 + r))
+        for r in range(N):
+            ts(col("sm", 56 + r), col("sm", 32 + r), col("k", CP + r), A.is_equal, 2.0 * NM, A.mult)
+        for r in range(N):
+            if r == 0 or r == 2:
+                for u in (r, r + 1):
+                    tt(V(pp, place(u, me), place(u, me) + 16), ind(V(pp, 0, 192), col("g4", 2 * u)), blk("rs", 16, u), A.add)
+            ts(col("sm", 60 + r), col("sm", 48 + r), col("sm", 52 + r), A.subtract, col("sm", 56 + r), A.is_lt)
+            if r:
+                ts(col("of", r - 1), col("sm", 59 + r), col("sm", 43 + r), A.mult, col("k", DM + r - 1), A.add)
+        ts(col("of", 3), col("sm", 63), col("sm", 47), A.mult, col("k", DM + 3), A.add)
+        cp(ind(V("wm"), V("of")), V("mv"))
+        tr(V("tm"), V("wm", 0, 224))
+        cp(blk("ml", 16, t), ind(V("tm"), col("cu", 0)))
+        arrive("cols%d" % t, 2, [V(n, place(r, me), place(r, me) + NK) for r in peers for n in (pq, pz)])
+        lst = V("ml", 16 * t, 16 * t + 12)
+        pick(V(nq, 0, 192), V(nz, 0, 192), V(pq), V(pz), lst)
+        tr(V(hp, 192, 384), V("xh"))
+        own = (NI * me, NI * me + NI)
+        if t == NR - 1:
+            mm(V("psY", 0, 192), V("wq"), V("ws"), V(nq), V(nz))
+            store("s", T.oc[:], b8(V(nq, *own)))
+            cp(V("yo"), V("psY", 0, 192))
+            for u in range(4):
+                store("s" if u < 2 else "a", T.osc[4 * u:4 * u + 4, :], V(nz, own[0], own[1], 1, 32 * u, 32 * u + 4))
+            store("s", T.y[:], V("yo"))
+        ac(V(np_, 0, 192), ind(V(pp), lst), F.Copy)
+        ac(V(nh, 0, 192), ind(V(hp), lst), F.Copy)
+        q = "s" if t < NR - 1 else "a"
+        store(q, T.pr[t:t + 1, :], V(np_, own[0], own[1], 1, 0, 1))
+        store(q, T.ho[t:t + 1, :], V(nh, own[0], own[1], 1, 0, 1))
+        if t < NR - 1:
+            n = 16 * (2 * t + 1)
+            for kk in range(3):
+                ac(V("fu", 48 * kk, 48 * kk + n), ind(V(nh, 0, 192), V("gl", 0, 2 * t + 1)), F.Abs, bias=col("k", NG + kk))
+            for kk in range(3):
+                ac(V("fj", 48 * kk, 48 * kk + n), V("fu", 48 * kk, 48 * kk + n), F.Sign, acc=col("fm", kk))
+            for kk in range(3):
+                ac(blk("fe", 32, kk), V("cb"), F.Identity, bias=col("k", 40 + t), scale=col("fm", kk))
+
+    emit(g, T, ops, sent[0])
+
+
+def clash(a, b):
+    return a[0] == b[0] and a[1] < b[2] and b[1] < a[2] and not a[3].isdisjoint(b[3])
+
+
+def emit(g, T, ops, sent):
+    n = len(ops)
+    hist, known, waits, done = {}, {}, [], []
+    for i, o in enumerate(ops):
+        deps = set()
+        if o["kind"] != "x":
+            for z in o["r"]:
+                deps.update(j for j, y, w in hist.get(z[0], []) if w and clash(z, y))
+            for z in o["w"]:
+                deps.update(j for j, y, w in hist.get(z[0], []) if clash(z, y) and ops[j]["kind"] != "r")
+        for z in o["r"]:
+            hist.setdefault(z[0], []).append((i, z, False))
+        for z in o["w"]:
+            hist.setdefault(z[0], []).append((i, z, True))
+        kn = known.setdefault(o["q"], set())
+        ws = []
+        for j in sorted(deps, reverse=True):
+            if j != i and j not in kn:
+                ws.append(j)
+                kn.add(j)
+                kn.update(done[j])
+        waits.append(ws)
+        done.append(set(kn) if o["kind"] != "x" else set())
+    need = set(j for ws in waits for j in ws)
+    last = [i for i in range(n) if ops[i]["kind"] == "o" and i not in need]
+    need.update(i for i in range(n) if ops[i]["kind"] in "do")
+    queue = {"v": g.vector, "a": g.scalar, "p": g.tensor, "g": g, "s": g.sync}
+    user, count, sig = {}, {}, {}
+    for i, o in enumerate(ops):
+        if o["kind"] == "x":
+            sig[i] = o["ext"]
+            continue
+        for j in waits[i]:
+            queue[o["q"]].wait_ge(T.sem[sig[j][0]], sig[j][1])
+        ins = o["fn"]()
+        if i in need:
+            dma = o["kind"] in "do"
+            pool = o["q"] + "d" if dma else o["q"]
+            s = [pool + str(u) for u in range(POOLS[pool]) if user.get(pool + str(u), -1) in done[i] or pool + str(u) not in user][0]
+            user[s] = i
+            count[s] = count.get(s, 0) + (16 if dma else 1)
+            sig[i] = (s, count[s])
+            ins.then_inc(T.sem[s], 16 if dma else 1)
+    for i in last:
+        queue[ops[i]["q"]].wait_ge(T.sem[sig[i][0]], sig[i][1])
+    g.wait_ge(T.sem.sent, sent)

@@ -19,16 +19,16 @@ SCRATCH = {
     "pq3": _s(192, C4), "pz3": _s(192, U8),
     "hdx": _s(1536, BF), "hdv": _s(768, BF), "gv": _s(64, F32),
     "psS": ("psum", [128, 1536], F32), "psD": ("psum", [128, 2048], F32), "psY": ("psum", [128, 512], F32),
-    "pint": _s(8, I32), "bint": _s(8, I32), "bits": _s(8, F32), "row": _s(288, F32), "ep": _s(24, F32), "pf": _s(8, F32),
-    "cf": _s(64, F32), "co": _s(64, U16), "cu": _s(2, U16), "k": _s(48, F32), "neg": _s(192, F32), "pat": _s(64, F32),
-    "od1": _s(288, BF), "od2": _s(128, BF), "mv": _s(64, F32),
-    "v": _s(576, F32), "pm": _s(576, F32), "qm": _s(576, F32), "jk": _s(576, BF), "sg": _s(288, BF), "ee": _s(288, BF),
+    "pint": _s(8, I32), "bint": _s(8, I32), "bits": _s(8, F32), "row": _s(96, F32), "r128": _s(128, BF), "ep": _s(24, F32), "pf": _s(8, F32),
+    "cf": _s(64, F32), "co": _s(64, U16), "k": _s(48, F32), "neg": _s(192, F32), "pat": _s(64, F32),
+    "od1": _s(32, BF), "od2": _s(128, BF), "mv": _s(32, BF), "ce": _s(64, F32),
+    "v": _s(576, F32), "pm": _s(576, F32), "qm": _s(576, F32), "jk": _s(576, BF), "sg": _s(128, BF), "ee": _s(288, BF),
     "g3": _s(8, F32), "a3": _s(8, F32), "x1": _s(96, F32), "r1": _s(96, F32),
     "m1": _s(192, F32), "t1": _s(192, F32), "c8": _s(8, F32), "x2": _s(80, F32), "r2": _s(64, F32), "d2": _s(16, F32),
     "m2": _s(192, F32), "t2": _s(192, F32), "land": _s(48, F32), "gl": _s(8, U16), "xl": _s(2, U16),
-    "xs3": _s(128, F32), "rs": _s(128, F32), "tt": _s(256, F32), "mb": _s(256, F32), "pb": _s(256, F32), "sm": _s(64, F32),
-    "zz": _s(8, F32), "xz": _s(64, F32), "rz": _s(64, F32), "g4": _s(8, U16), "of": _s(4, U16),
-    "wm": _s(288, F32), "tm": _s(224, F32), "ml": _s(48, U16), "xh": _s(192, F32),
+    "xs3": _s(128, F32), "rs": _s(128, F32), "tt": _s(128, F32), "mb": _s(128, F32), "pb": _s(128, F32), "sm": _s(64, F32),
+    "xz": _s(64, F32), "rz": _s(64, F32), "g4": _s(8, U16), "of": _s(2, U16),
+    "wc": _s(432, BF), "wm": _s(432, BF), "tm": _s(384, BF), "mx": _s(12, F32), "ml": _s(48, U16), "xh": _s(192, F32),
     "pp0": _s(384, F32), "pp1": _s(384, F32), "hp0": _s(384, F32), "hp1": _s(384, F32),
     "fu": _s(144, F32), "fj": _s(144, BF), "fm": _s(8, F32), "fe": _s(96, F32), "cb": _s(32, F32), "yo": _s(192, F32),
 }
@@ -128,8 +128,8 @@ def rank_program(g, core, T, topo):
     def mm(o, lq, ls, rq, rs):
         rec("p", lambda: pe.matmul_mx(o[0], lq[0], ls[0], rq[0], rs[0], True, True), [o], [lq, ls, rq, rs])
 
-    def iota(o, pattern, cm, **kw):
-        rec("g", lambda: g.iota(o[0], pattern, 0, cm, **kw), [o], [])
+    def iota(o, pattern, base, cm, **kw):
+        rec("g", lambda: g.iota(o[0], pattern, base, cm, **kw), [o], [])
 
     def load(q, o, src):
         e = g.sync if q == "s" else act
@@ -157,47 +157,48 @@ def rank_program(g, core, T, topo):
         return 192 + 48 * ((r - at - 1) % N)
 
     load("s", V("ti", 0, 192), T.it[:])
-    load("a", V("tx"), T.x[:])
-    load("s", V("tw"), T.w[:])
-    iota(col("pint", 0), [[0, 1]], 1)
-    iota(V("row"), [[1, 288]], 0, allow_small_or_imprecise_dtypes=True)
-    iota(V("ep"), [[32, 3], [96, 4], [16, 2]], 0, allow_small_or_imprecise_dtypes=True)
+    load("s", V("tx"), T.x[:])
+    loose = {"allow_small_or_imprecise_dtypes": True}
+    iota(col("pint", 0), [[0, 1]], 0, 1)
+    iota(V("row"), [[1, 96]], 0, 0, **loose)
+    iota(V("r128"), [[1, 128]], 0, 0, **loose)
+    iota(V("ep"), [[32, 3], [96, 4], [16, 2]], 0, 0, **loose)
     ms(V("ti", 192, 512), 0.0)
     ms(V("te"), 0.0)
     for j, (sh, m) in enumerate([(4, 1), (4, 1), (5, 1), (6, 1), (0, 15), (0, 31), (0, 127)]):
         ts(col("bint", j), col("pint", 0), sh, A.logical_shift_right, m, A.bitwise_and)
     cp(V("bits", 0, 7), V("bint", 0, 7))
     h, hh, q0, q1, s16, s32, pf = col("bits", 0), V("bits", 0, 2), col("bits", 2), col("bits", 3), col("bits", 4), col("bits", 5), col("bits", 6)
-    E_I, E_P, E_2, E_S, E_Z, E_H = 0, 4, 28, 40, 48, 52
-    KC, NG, CP, DM, GD, X0, SH, PAD = 0, 4, 8, 12, 16, 20, 24, 25
+    E_I, E_P, E_2, E_S, E_H = 0, 4, 28, 40, 52
+    KC, NG, CP, DM, GD, X0, PAD = 0, 4, 8, 12, 16, 20, 25
     ms(V("cf", 0, 4), 0.0)
     ts(V("cf", E_I, E_I + 3), V("row", 0, 48, 16), s16, A.add)
     ts(V("cf", E_P, E_P + 24), V("ep"), s16, A.add)
-    ts(V("te", 2, 514, 4), V("row", 0, 128), pf, A.is_equal)
+    ts(V("te", 2, 514, 4), V("r128"), pf, A.is_equal)
     cp(V("co", 0, 28), V("cf", 0, 28))
-    ts(V("te", 523, 1035, 4), V("row", 0, 128), pf, A.is_equal)
+    ts(V("te", 523, 1035, 4), V("r128"), pf, A.is_equal)
     quant(V("iq"), V("isc"), V("ti"))
     send(b8(V("iq", 0, NI)), lambda r: b8(blk("pq0", NI, me)), "items")
     send(V("isc", 0, NI), lambda r: blk("pz0", NI, me), "items")
+    iota(V("wc", 0, 384), [[16, 12], [0, 2], [1, 16]], -128, 0, **loose)
     for b, a in enumerate([2, 522, 0, 520]):
         quant(blk("eq", 128, b), blk("es", 128, b), V("te", a, a + 512))
     pick(blk("pq0", NI, me), blk("pz0", NI, me), V("iq"), V("isc"), V("co", E_I, E_I + 3))
-    quant(V("xq"), V("xs"), V("tx"))
     ms(V("neg"), -1e29)
+    ts(col("k", 26), pf, s32, A.subtract, 3.0, A.mult)
+    ts(col("k", X0), q0, h, A.not_equal, 4.0, A.mult)
+    ts(V("pf", 0, 3), V("row", 0, 96, 32), s32, A.add)
+    ms(V("fe"), 0.0)
+    quant(V("xq"), V("xs"), V("tx"))
+    ts(col("k", 27), col("k", 26), s32, A.add)
     pick(V("xpq"), V("xps"), V("xq"), V("xs"), V("co", E_P, E_P + 24))
     for b in range(4):
         mm(V("psD", 512 * b, 512 * b + NB), blk("eq", 128, b), blk("es", 128, b), V("xq"), V("xs"))
     for b in range(4):
         ac(blk("hdx", NB, b), V("psD", 512 * b, 512 * b + NB), F.Copy, scale=0.5)
-    ts(col("k", 26), pf, s32, A.subtract, 3.0, A.mult)
-    ts(col("k", X0), q0, h, A.not_equal, 4.0, A.mult)
-    ts(V("pf", 0, 3), V("row", 0, 96, 32), s32, A.add)
-    ms(V("fe"), 0.0)
-    ts(col("k", 27), col("k", 26), s32, A.add)
     ts(col("k", 32), q1, 2.0, A.mult, col("k", X0), A.add)
     ts(col("k", 33), q1, -2.0, A.mult, col("k", X0), A.add)
-    for kk in range(3):
-        ts(blk("od1", 96, kk), V("row", 0, 96), col("pf", kk), A.is_ge, -0.5, A.add)
+    ts(V("od1"), V("row", 0, 32), s32, A.is_ge, -0.5, A.add)
     ts(V("k", KC, KC + 3), V("row", 0, 96, 32), col("k", 27), A.add, 320.0, A.add)
     ts(col("k", 34), col("k", 33), 2.0, A.add)
     ts(V("cf", E_2, E_2 + 2), hh, 0.0, A.mult, col("k", 32), A.add)
@@ -218,27 +219,26 @@ def rank_program(g, core, T, topo):
     ms(V("tn"), 0.0)
 
     def later():
+        load("s", V("tw"), T.w[:])
         ts(col("k", PAD), s16, float(NK), A.is_ge, 1000.0, A.mult)
-        ts(V("k", DM, DM + 4), V("row", 224, 288, 16), s16, A.add)
-        ts(col("k", SH), h, 16.0, A.mult, -16.0, A.add)
-        ts(col("k", 37), s16, h, A.subtract, 16.0, A.mult)
+        ts(V("k", DM, DM + 2), V("row", 0, 32, 16), s16, A.add, 384.0, A.add)
         for b in range(2):
             for f in range(2):
                 ts(V("cf", E_S + 4 * f + 2 * b, E_S + 4 * f + 2 * b + 2), hh, 4.0, A.mult, float(8 * b + f), A.add)
-            ts(V("cf", E_Z + 2 * b, E_Z + 2 * b + 2), hh, float(2 * b), A.add)
+            c = [place(2 * b, me), place(2 * b + 1, me)]
+            ts(col("k", 28 + b), h, float(c[1] - c[0]), A.mult, float(c[0] - 128), A.add)
         for b in range(6):
             c = [4 * ((me + 1 + m // 3) % N) + 2 if m % 3 == 0 else 2 for m in (2 * b, 2 * b + 1)]
             ts(V("cf", E_H + 2 * b, E_H + 2 * b + 2), hh, float(c[1] - c[0]), A.mult, float(c[0]), A.add)
-        ts(V("k", CP, CP + 4), V("row", 0, 64, 16), s16, A.add, col("k", PAD), A.add)
-        ts(V("k", 28, 32), V("k", DM, DM + 4), col("k", SH), A.add, 1.0, A.add)
-        ts(col("k", 38), col("k", 37), 16.0, A.add, 208.0, A.min)
-        cp(V("co", E_S, 64), V("cf", E_S, 64))
-        ts(V("k", GD, GD + 4), V("k", 28, 32), -1.0, A.mult)
-        cp(col("cu", 0), col("k", 38))
-        ms(V("zz", 4, 8), 0.0)
+        ts(V("k", CP, CP + 2), V("pf", 0, 2), col("k", PAD), A.add)
+        ts(V("k", GD, GD + 2), V("k", DM, DM + 2), -1.0, A.mult, -1.0, A.add)
+        cp(V("co", E_S, E_S + 8), V("cf", E_S, E_S + 8))
+        cp(V("co", E_H, 64), V("cf", E_H, 64))
+        for b in range(2):
+            ts(blk("ce", 32, b), V("row", 0, 32), 0.0, A.mult, col("k", CP + b), A.add)
+            ts(blk("mv", 16, b), V("row", 0, 16), col("k", 28 + b), A.add)
+        ms(V("wm", 384, 432), 0.0)
         ms(V("pp0"), 0.0)
-        for r in range(N):
-            ts(blk("mv", 16, r), V("row", 0, 16), float(place(r, me)), A.add)
         ms(V("hp0", 0, 192), -1.0)
 
     def latest():
@@ -276,6 +276,19 @@ def rank_program(g, core, T, topo):
         def bid(kk):
             ts(blk("x1", 32, kk), blk("fe", 32, kk), col("pm", 192 * kk + 191), A.add, col("qm", 192 * kk + 190), A.subtract)
 
+        def turn(kk):
+            tr(blk("r1", 32, kk), blk("x1", 32, kk))
+            ac(blk("sg", 32, kk), blk("r1", 32, kk), F.Sign, bias=col("x1", 32 * kk), scale=-1.0)
+
+        def count(kk):
+            ac(blk("jk", 96, kk), blk("ee", 96, kk), F.Sign, acc=col("a3", kk))
+
+        def near(kk):
+            tt(blk("ee", 32, 4 * kk), blk("sg", 32, kk), V("od1"), A.add)
+
+        def far(kk, a, b, op):
+            ts(V("ee", 96 * kk + 32 * a, 96 * kk + 32 * b), V("r1", 32 * a, 32 * b), col("x1", 32 * kk), op, -0.5, A.add)
+
         if t:
             val(0)
             val(1)
@@ -293,17 +306,22 @@ def rank_program(g, core, T, topo):
         bid(0)
         second(2)
         bid(1)
-        tr(blk("r1", 32, 0), blk("x1", 32, 0))
+        turn(0)
         bid(2)
-        tr(blk("r1", 32, 1), blk("x1", 32, 1))
-        tr(blk("r1", 32, 2), blk("x1", 32, 2))
+        turn(1)
+        turn(2)
+        far(2, 0, 2, A.is_lt)
+        near(0)
+        far(0, 1, 3, A.is_le)
+        count(0)
+        near(1)
+        far(1, 0, 1, A.is_lt)
+        far(1, 2, 3, A.is_le)
+        count(1)
+        near(2)
+        count(2)
         for kk in range(3):
-            ac(col("g3", 4 + kk), col("g3", kk), F.Identity, bias=col("k", KC + kk), scale=512.0)
-        for kk in range(3):
-            ac(blk("sg", 96, kk), V("r1"), F.Sign, bias=col("x1", 32 * kk), scale=-1.0)
-        for kk in range(3):
-            tt(blk("ee", 96, kk), blk("sg", 96, kk), blk("od1", 96, kk), A.add)
-            ac(blk("jk", 96, kk), blk("ee", 96, kk), F.Sign, acc=col("a3", kk))
+            ts(col("g3", 4 + kk), col("g3", kk), 512.0, A.mult, col("k", KC + kk), A.add)
         for kk in range(3):
             ts(blk("m1", 32, kk), V("pat", 0, 32), col("a3", kk), A.is_equal, col("x1", 32 * kk), A.mult)
             ts(blk("m1", 32, 3 + kk), V("pat", 0, 32), col("a3", kk), A.is_equal, col("g3", 4 + kk), A.mult)
@@ -355,67 +373,65 @@ def rank_program(g, core, T, topo):
             latest()
         if t == 1:
             quant(V("wq"), V("ws"), V("tw"))
-        ac(V("wm"), V("row"), F.Relu, bias=col("k", SH))
+        ac(V("wm", 0, 384), V("wc", 0, 384), F.Copy)
         arrive("bids%d" % t, 1, [V("land", L + 4 * r, L + 4 * r + 4) for r in peers])
-        lw, goal = V("land", L, L + 16), V("land", L + 1, L + 16, 4)
+        lw, goal = V("land", L, L + 16), V("xs3", 64, 128, 32)
         cp(V("xs3", 64, 128), ind(lw, V("co", E_S + 4, E_S + 8)))
         ac(V("xs3", 0, 64), ind(lw, V("co", E_S, E_S + 4)), F.Copy)
-        ac(V("sm", 0, 4), goal, F.Copy, scale=-BIG)
+        ac(V("sm", 0, 2), goal, F.Copy, scale=-BIG)
         tr(V("rs", 64, 128), V("xs3", 64, 128))
+        ts(V("sm", 4, 6), goal, -24.5, A.add, 1.0 / NI, A.mult)
         tr(V("rs", 0, 64), V("xs3", 0, 64))
-        for r in range(N):
-            ac(blk("tt", 64, r), V("rs", 64, 128), F.Abs, bias=col("sm", r), scale=BIG)
-        ts(V("sm", 4, 8), goal, -24.5, A.add, 1.0 / NI, A.mult)
-        for r in range(N):
-            ac(blk("jk", 64, r), V("rs", 0, 64), F.Sign, bias=col("land", L + 4 * r), scale=-1.0, acc=col("sm", 24 + r))
+        ts(V("sm", 8, 10), V("sm", 4, 6), MAGIC, A.add)
+        for b in range(2):
+            ac(blk("tt", 64, b), V("rs", 64, 128), F.Abs, bias=col("sm", b), scale=BIG)
+        for b in range(2):
+            ac(blk("jk", 64, b), V("rs", 0, 64), F.Sign, bias=col("xs3", 32 * b), scale=-1.0, acc=col("sm", 24 + b))
+        tt(blk("mb", 64, 0), V("rs", 0, 64), blk("tt", 64, 0), A.subtract)
+        ts(V("sm", 16, 18), V("sm", 8, 10), -MAGIC, A.add, 1.0 / 16, A.mult)
+        tt(blk("mb", 64, 1), V("rs", 0, 64), blk("tt", 64, 1), A.subtract)
+        for b in range(2):
+            ac(col("sm", 20 + b), col("xs3", 64 + 32 * b), F.Identity, bias=col("sm", 16 + b), scale=2.0 ** -20)
+        for b in range(2):
+            ac(col("sm", 36 + b), col("sm", 24 + b), F.Identity, bias=col("sm", 20 + b), scale=-2.0 ** -12)
+        for b in range(2):
+            scan(blk("pb", 64, b), blk("mb", 64, b), blk("mb", 64, b), A.max, A.max)
+            ac(blk("jk", 64, 4 + b), blk("pb", 64, b), F.Sign, bias=col("pb", 64 * b + 63), scale=-1.0, acc=col("sm", 32 + b))
+        ts(V("g4", 0, 7, 2), V("land", L + 1, L + 16, 4), -1.0, A.add, 0.0, A.max)
+        ts(V("sm", 6, 8), goal, -8.5, A.add, 1.0 / 16, A.mult)
+        ts(V("sm", 40, 42), V("sm", 16, 18), -2.0 ** -5, A.add)
 
-        def masked(r):
-            tt(blk("mb", 64, r), V("rs", 0, 64), blk("tt", 64, r), A.subtract)
+        def offer(u):
+            tt(V(pp, place(u, me), place(u, me) + 16), ind(V(pp, 0, 192), col("g4", 2 * u)), blk("rs", 16, u), A.add)
 
-        def best(r):
-            scan(blk("pb", 64, r), blk("mb", 64, r), blk("mb", 64, r), A.max, A.max)
-            ac(blk("jk", 64, 4 + r), blk("pb", 64, r), F.Sign, bias=col("pb", 64 * r + 63), scale=-1.0, acc=col("sm", 32 + r))
-
-        masked(0)
-        masked(1)
-        best(0)
-        masked(2)
-        best(1)
-        masked(3)
-        best(2)
-        ts(V("sm", 8, 12), V("sm", 4, 8), MAGIC, A.add)
-        best(3)
-        ts(V("sm", 12, 16), goal, 2.0 ** -20, A.mult, 2.0 ** -6, A.add)
-        ts(V("sm", 16, 20), V("sm", 8, 12), -MAGIC, A.add, 1.0 / 16, A.mult)
-        ts(V("sm", 28, 32), V("sm", 24, 28), -2.0 ** -12, A.mult)
-        tt(V("sm", 20, 24), V("sm", 12, 16), V("sm", 16, 20), A.add)
-        ts(V("sm", 40, 44), V("sm", 16, 20), -2.0 ** -21, A.add)
-        tt(V("sm", 36, 40), V("sm", 20, 24), V("sm", 28, 32), A.add)
-        ts(V("g4", 0, 7, 2), goal, -1.0, A.add, 0.0, A.max)
-        for r in range(N):
-            ts(col("zz", r), col("sm", 32 + r), col("k", CP + r), A.not_equal, col("sm", 36 + r), A.add)
-        cp(V("xz"), ind(V("zz"), V("co", E_Z, E_Z + 4)))
-        ac(V("xh"), ind(lw, V("co", E_H, E_H + 12)), F.Copy)
-        tt(V("sm", 44, 48), goal, V("k", GD, GD + 4), A.add)
+        for b in range(2):
+            ts(blk("xz", 32, b), blk("ce", 32, b), col("sm", 32 + b), A.not_equal, col("sm", 36 + b), A.add)
+        ts(V("sm", 10, 12), V("sm", 6, 8), MAGIC, A.add)
         tr(V("rz"), V("xz"))
-        for r in range(N):
-            ac(blk("jk", 64, r), V("rz"), F.Sign, bias=col("zz", r), scale=-1.0, acc=col("sm", 48 + r))
-            ac(blk("jk", 64, 4 + r), V("rz"), F.Sign, bias=col("sm", 40 + r), scale=-1.0, acc=col("sm", 52 + r))
-        for r in range(N):
-            ts(col("sm", 56 + r), col("sm", 32 + r), col("k", CP + r), A.is_equal, 2.0 * NM, A.mult)
-        for r in range(N):
-            if r == 0 or r == 2:
-                for u in (r, r + 1):
-                    tt(V(pp, place(u, me), place(u, me) + 16), ind(V(pp, 0, 192), col("g4", 2 * u)), blk("rs", 16, u), A.add)
-            ts(col("sm", 60 + r), col("sm", 48 + r), col("sm", 52 + r), A.subtract, col("sm", 56 + r), A.is_lt)
-            if r:
-                ts(col("of", r - 1), col("sm", 59 + r), col("sm", 43 + r), A.mult, col("k", DM + r - 1), A.add)
-        ts(col("of", 3), col("sm", 63), col("sm", 47), A.mult, col("k", DM + 3), A.add)
-        cp(ind(V("wm"), V("of")), V("mv"))
-        tr(V("tm"), V("wm", 0, 224))
-        cp(blk("ml", 16, t), ind(V("tm"), col("cu", 0)))
-        arrive("cols%d" % t, 2, [V(n, place(r, me), place(r, me) + NK) for r in peers for n in (pq, pz)])
+        for b in range(2):
+            ac(blk("jk", 64, b), V("rz"), F.Sign, bias=col("xz", 32 * b), scale=-1.0, acc=col("sm", 48 + b))
+            ac(blk("jk", 64, 4 + b), V("rz"), F.Sign, bias=col("sm", 40 + b), scale=-1.0, acc=col("sm", 52 + b))
+        ac(V("xh"), ind(lw, V("co", E_H, E_H + 12)), F.Copy)
+        ts(V("sm", 12, 14), V("sm", 10, 12), -MAGIC, A.add, 16.0, A.mult)
+        tt(V("sm", 14, 16), goal, V("k", GD, GD + 2), A.add)
+        for b in range(2):
+            ts(col("sm", 56 + b), col("sm", 32 + b), col("k", CP + b), A.is_equal, 2.0 * NM, A.mult)
+        tt(V("sm", 44, 46), V("sm", 12, 14), V("sm", 14, 16), A.add)
+        for b in range(2):
+            ts(col("sm", 60 + b), col("sm", 48 + b), col("sm", 52 + b), A.subtract, col("sm", 56 + b), A.is_lt)
+        for b in range(2):
+            ts(col("of", b), col("sm", 60 + b), col("sm", 44 + b), A.mult, col("k", DM + b), A.add)
+        offer(0)
+        cp(ind(V("wm", 0, 416), V("of")), V("mv"))
+        offer(1)
+        cp(ind(V("wm", 16, 432), V("of")), V("mv"))
+        offer(2)
+        tr(V("tm"), V("wm", 0, 384))
+        offer(3)
+        tt(V("mx"), V("tm", 0, 384, 32), V("tm", 16, 384, 32), A.max)
         lst = V("ml", 16 * t, 16 * t + 12)
+        ts(lst, V("mx"), 128.0, A.add)
+        arrive("cols%d" % t, 2, [V(n, place(r, me), place(r, me) + NK) for r in peers for n in (pq, pz)])
         pick(V(nq, 0, 192), V(nz, 0, 192), V(pq), V(pz), lst)
         tr(V(hp, 192, 384), V("xh"))
         own = (NI * me, NI * me + NI)

@@ -3,8 +3,7 @@ from concourse.mybir import dt, AluOpType, AxisListType, ActivationFunctionType
 
 NI, NB, NK, NM, NR = 48, 384, 12, 8, 3
 C4, U8, F32, BF, U16, I32 = "float8_e4m3fn_x4", "uint8", "float32", "bfloat16", "uint16", "int32"
-PW = 464
-OWN = 336
+PW = 384
 
 
 def _s(n, d):
@@ -15,28 +14,25 @@ SCRATCH = {
     "ti": _s(512, BF), "tx": _s(1536, BF), "tw": _s(512, BF), "te": _s(1040, BF), "tn": _s(512, BF),
     "iq": _s(128, C4), "isc": _s(128, U8), "xq": _s(384, C4), "xs": _s(384, U8), "xpq": _s(384, C4), "xps": _s(384, U8),
     "wq": _s(128, C4), "ws": _s(128, U8), "eq": _s(512, C4), "es": _s(512, U8),
-    "pq0": _s(PW, C4), "pz0": _s(PW, U8), "pq1": _s(PW, C4), "pz1": _s(PW, U8), "pq2": _s(PW, C4), "pz2": _s(PW, U8),
-    "pq3": _s(192, C4), "pz3": _s(192, U8),
-    "hdx": _s(1536, BF), "hdv": _s(768, BF), "gv": _s(64, F32),
+    "pq": _s(PW, C4), "pz": _s(PW, U8), "nq": _s(48, C4), "nz": _s(48, U8),
+    "oq0": _s(128, C4), "oz0": _s(128, U8), "oq1": _s(128, C4), "oz1": _s(128, U8), "oq2": _s(128, C4), "oz2": _s(128, U8),
+    "hdx": _s(1536, BF), "hdv": _s(4 * PW, BF), "gv": _s(64, F32),
     "psS": ("psum", [128, 1536], F32), "psD": ("psum", [128, 2048], F32), "psY": ("psum", [128, 512], F32),
-    "pint": _s(8, I32), "bint": _s(8, I32), "bits": _s(8, F32), "row": _s(96, F32), "r128": _s(128, BF), "ep": _s(24, F32), "pf": _s(8, F32),
-    "cf": _s(64, F32), "co": _s(64, U16), "k": _s(48, F32), "neg": _s(192, F32), "pat": _s(64, F32),
-    "od1": _s(32, BF), "od2": _s(128, BF), "mv": _s(32, BF), "ce": _s(64, F32),
-    "v": _s(576, F32), "pm": _s(576, F32), "qm": _s(576, F32), "jk": _s(576, BF), "sg": _s(128, BF), "ee": _s(288, BF),
-    "g3": _s(8, F32), "a3": _s(8, F32), "x1": _s(96, F32), "r1": _s(96, F32),
-    "m1": _s(192, F32), "t1": _s(192, F32), "c8": _s(8, F32), "x2": _s(80, F32), "r2": _s(64, F32), "d2": _s(16, F32),
-    "m2": _s(192, F32), "t2": _s(192, F32), "land": _s(48, F32), "gl": _s(8, U16), "xl": _s(2, U16),
-    "xs3": _s(128, F32), "rs": _s(128, F32), "tt": _s(128, F32), "mb": _s(128, F32), "pb": _s(128, F32), "sm": _s(64, F32),
-    "xz": _s(64, F32), "rz": _s(64, F32), "g4": _s(8, U16), "of": _s(2, U16),
-    "wc": _s(432, BF), "wm": _s(432, BF), "tm": _s(384, BF), "mx": _s(12, F32), "ml": _s(48, U16), "xh": _s(192, F32),
-    "pp0": _s(384, F32), "pp1": _s(384, F32), "hp0": _s(384, F32), "hp1": _s(384, F32),
-    "fu": _s(144, F32), "fj": _s(144, BF), "fm": _s(8, F32), "fe": _s(96, F32), "cb": _s(32, F32), "yo": _s(192, F32),
+    "pint": _s(8, I32), "bint": _s(8, I32), "bits": _s(8, F32), "r128": _s(128, BF), "oi": _s(16, I32),
+    "land": _s(48, F32), "v": _s(768, F32), "pm": _s(600, F32), "qm": _s(576, F32), "yo": _s(256, F32),
+    "pp": _s(256, F32), "hp": _s(256, F32), "wm": _s(256, BF),
+    "tf": _s(12288, F32), "tb": _s(16384, BF), "tu": _s(512, U16),
 }
-POOLS = {"v": 44, "a": 36, "p": 10, "g": 6, "sd": 14, "ad": 8}
+POOLS = {"v": 56, "a": 44, "p": 10, "g": 8, "sd": 14, "ad": 8}
 SEMAPHORES = [q + str(i) for q in POOLS for i in range(POOLS[q])] + ["sent", "items"] + \
     ["bids%d" % t for t in range(NR)] + ["cols%d" % t for t in range(NR)]
 MAGIC = 12582912.0
-BIG = 2.0 ** 80
+HELD = 2.0 ** 88
+TINY = 2.0 ** -120
+KEY, MID = 2048.0, 768.0
+CYC, WAKE, GATH, SCAT, FLY, ROWS, LOCAL = 0.00085, 0.2, 1.5, 3.5, 1.2, 0.9, 1.5
+OTHER = [(0.12, 1.0, 0.9), (0.2, 1.3, 1.2)]
+TRIES, MUT = 2000, 10
 
 
 def rank_program(g, core, T, topo):
@@ -48,74 +44,72 @@ def rank_program(g, core, T, topo):
     peers = [r for r in range(N) if r != me]
     engs = [e for e in topo.engines(core, T.cores[peers[0]]) if all(e in topo.engines(core, T.cores[r]) for r in peers)]
     ids = [DstId(rid=topo.addr(T.cores[r])[0], pnc=topo.addr(T.cores[r])[1]) for r in peers]
-
-    def bitmask(es):
-        return sum(1 << e for e in es)
-
     ops = []
 
     def V(name, a=0, b=None, step=1, p0=0, p1=128):
         b = SCRATCH[name][1][1] if b is None else b
+        cols = range(a, b, step)
         if SCRATCH[name][0] == "psum":
-            reg = (name, 0, 128, frozenset([a // 512]))
+            reg = (name, 0, 128, a // 512, a // 512, frozenset([a // 512]))
         else:
-            reg = (name, p0, p1, frozenset(range(a, b, step)))
-        return (T[name][p0:p1, a:b:step] if step > 1 else T[name][p0:p1, a:b], [reg])
+            reg = (name, p0, p1, a, b - 1, frozenset(cols))
+        kind = "p" if SCRATCH[name][0] == "psum" else "h" if SCRATCH[name][2] in (BF, U16) else "s"
+        return (T[name][p0:p1, a:b:step] if step > 1 else T[name][p0:p1, a:b], [reg], len(cols), kind)
 
-    def col(name, a):
-        return V(name, a, a + 1)
+    used = {"tf": 0, "tb": 0, "tu": 0}
 
-    def blk(name, n, j):
-        return V(name, n * j, n * j + n)
+    def tmp(n, pool="tf"):
+        base = used[pool]
+        al = 2 if pool == "tu" else 16
+        used[pool] += (n + al - 1) // al * al
+        assert used[pool] <= SCRATCH[pool][1][1]
+
+        def view(a=0, b=None, step=1, p0=0, p1=128):
+            return V(pool, base + a, base + (n if b is None else b), step, p0, p1)
+        return view
+
+    def col(w, a, p0=0, p1=128):
+        return V(w, a, a + 1, 1, p0, p1) if isinstance(w, str) else w(a, a + 1, 1, p0, p1)
+
+    def blk(w, n, j):
+        return V(w, n * j, n * j + n) if isinstance(w, str) else w(n * j, n * j + n)
 
     def ind(w, o):
-        return (w[0].indirect(o[0]), w[1] + o[1])
+        return (w[0].indirect(o[0]), w[1] + o[1], 16 * o[2], "i")
 
     def b8(w):
-        return (w[0].bitcast(dt.uint8), w[1])
+        return (w[0].bitcast(dt.uint8),) + w[1:]
 
     def b32(w):
-        return (w[0].bitcast(dt.uint32), w[1])
+        return (w[0].bitcast(dt.uint32),) + w[1:]
 
     def ap(x):
         return x[0] if isinstance(x, tuple) else x
 
-    def rec(q, fn, wr, rd, kind="c", ext=None):
-        r = [z for x in rd if isinstance(x, tuple) for z in x[1]]
-        w = [z for x in wr for z in x[1]]
+    def rec(alts, wr, rd, kind="c", ext=None):
+        r = [z for x in rd if isinstance(x, tuple) for z in x[1]] + [z for x in wr for z in x[1][1:]]
+        w = [x[1][0] for x in wr]
         w = w + [z for z in r if SCRATCH[z[0]][0] == "psum"]
-        ops.append({"q": q, "fn": fn, "w": w, "r": r, "kind": kind, "ext": ext})
+        ops.append({"alts": alts, "w": w, "r": r, "kind": kind, "ext": ext})
+        return len(ops) - 1
+
+    def cost(o, i, mul=None, base=0.05):
+        if o[3] == "i":
+            return base + SCAT * CYC * o[2]
+        if i[3] == "i":
+            return base + GATH * CYC * o[2]
+        if mul is None:
+            mul = 0.5 if o[3] == i[3] == "h" else 1.0
+        return CYC * max(64, mul * i[2])
 
     vec, act, pe = g.vector, g.scalar, g.tensor
 
-    def ts(o, i, s1, op0, s2=None, op1=None):
+    def vts(o, i, s1, op0, s2=None, op1=None):
         if op1 is None:
-            rec("v", lambda: vec.tensor_scalar(o[0], i[0], ap(s1), None, op0), [o], [i, s1])
-        else:
-            rec("v", lambda: vec.tensor_scalar(o[0], i[0], ap(s1), ap(s2), op0, op1), [o], [i, s1, s2])
+            return ("v", lambda: vec.tensor_scalar(o[0], i[0], ap(s1), None, op0), cost(o, i))
+        return ("v", lambda: vec.tensor_scalar(o[0], i[0], ap(s1), ap(s2), op0, op1), cost(o, i))
 
-    def tt(o, a, b, op):
-        rec("v", lambda: vec.tensor_tensor(o[0], a[0], b[0], op), [o], [a, b])
-
-    def cp(o, i):
-        rec("v", lambda: vec.tensor_copy(o[0], i[0]), [o], [i])
-
-    def ms(o, c):
-        rec("v", lambda: vec.memset(o[0], c), [o], [])
-
-    def tr(o, i):
-        rec("v", lambda: vec.transpose(o[0], i[0]), [o], [i])
-
-    def red(o, i, op):
-        rec("v", lambda: vec.tensor_reduce(o[0], i[0], AxisListType.X, op), [o], [i])
-
-    def scan(o, a, b, op0, op1):
-        rec("v", lambda: vec.tensor_tensor_scan(o[0], a[0], b[0], -1e29, op0, op1), [o], [a, b])
-
-    def quant(q, s, i):
-        rec("v", lambda: vec.quantize_mx(q[0], s[0], i[0]), [q, s], [i])
-
-    def ac(o, i, f, bias=None, scale=None, acc=None):
+    def aac(o, i, f, bias=None, scale=None, acc=None):
         kw = {}
         if bias is not None:
             kw["bias"] = ap(bias)
@@ -123,389 +117,465 @@ def rank_program(g, core, T, topo):
             kw["scale"] = ap(scale)
         if acc is not None:
             kw["accum_out"] = acc[0]
-        rec("a", lambda: act.activation(o[0], i[0], f, **kw), [o] + ([acc] if acc is not None else []), [i, bias, scale])
+        return ("a", lambda: act.activation(o[0], i[0], f, **kw), cost(o, i, 1.0, 0.065) + (0.02 if acc is not None else 0))
+
+    def ts(o, i, s1, op0, s2=None, op1=None):
+        rec([vts(o, i, s1, op0, s2, op1)], [o], [i, s1, s2])
+
+    def ac(o, i, f, bias=None, scale=None, acc=None):
+        rec([aac(o, i, f, bias, scale, acc)], [o] + ([acc] if acc is not None else []), [i, bias, scale])
+
+    def count(acc, i, f, bias=None, scale=None):
+        ac(tmp(i[2], "tb")(), i, f, bias, scale, acc)
+
+    def axb(o, i, a, b):
+        rec([aac(o, i, F.Identity, b, a), vts(o, i, a, A.mult, b, A.add)], [o], [i, a, b])
+
+    def times(o, i, c):
+        rec([aac(o, i, F.Copy, None, c), vts(o, i, c, A.mult)], [o], [i])
+
+    def tt(o, a, b, op):
+        rec([("v", lambda: vec.tensor_tensor(o[0], a[0], b[0], op), cost(o, a, 1.0 if "p" in (a[3], b[3]) else 2.0))], [o], [a, b])
+
+    def cp(o, i):
+        rec([("v", lambda: vec.tensor_copy(o[0], i[0]), cost(o, i))], [o], [i])
+
+    def cp2(o, i):
+        rec([aac(o, i, F.Copy), ("v", lambda: vec.tensor_copy(o[0], i[0]), cost(o, i))], [o], [i])
+
+    def ms(o, c):
+        rec([("v", lambda: vec.memset(o[0], c), cost(o, o))], [o], [])
+
+    def tr(o, i):
+        rec([("v", lambda: vec.transpose(o[0], i[0]), cost(o, i))], [o], [i])
+
+    def total(o, i):
+        j = tmp(i[2])()
+        rec([("v", lambda: vec.tensor_reduce(o[0], i[0], AxisListType.X, A.add), cost(o, i, 1.0)), aac(j, i, F.Identity, None, None, o)], [o, j], [i])
+
+    def scan(o, a, b, op0, op1, init):
+        rec([("v", lambda: vec.tensor_tensor_scan(o[0], a[0], b[0], init, op0, op1), cost(o, a))], [o], [a, b])
+
+    def quant(q, s, i):
+        rec([("v", lambda: vec.quantize_mx(q[0], s[0], i[0]), 0.012 + 0.00022 * i[2])], [q, s], [i])
 
     def mm(o, lq, ls, rq, rs):
-        rec("p", lambda: pe.matmul_mx(o[0], lq[0], ls[0], rq[0], rs[0], True, True), [o], [lq, ls, rq, rs])
+        rec([("p", lambda: pe.matmul_mx(o[0], lq[0], ls[0], rq[0], rs[0], True, True), 1.5 * CYC * (rq[2] + 16))], [o], [lq, ls, rq, rs])
 
-    def iota(o, pattern, base, cm, **kw):
-        rec("g", lambda: g.iota(o[0], pattern, base, cm, **kw), [o], [])
+    def iota(o, pattern, base, cm):
+        kw = {} if o[1][0][0] == "pint" else {"allow_small_or_imprecise_dtypes": True}
+        rec([("g", lambda: g.iota(o[0], pattern, base, cm, **kw), 0.13 + 2 * CYC * o[2])], [o], [])
 
-    def load(q, o, src):
-        e = g.sync if q == "s" else act
-        rec(q, lambda: e.dma_start(o[0], src), [o], [], kind="d")
+    def load(o, src, behind=()):
+        rec([("s", lambda: g.sync.dma_start(o[0], src), 0.05)], [o], list(behind), kind="d")
 
     def store(q, dst, i):
         e = g.sync if q == "s" else act
-        rec(q, lambda: e.dma_start(dst, i[0]), [], [i], kind="o")
+        rec([(q, lambda: e.dma_start(dst, i[0]), 0.05)], [], [i], kind="o")
 
     sent = [0]
 
     def send(s, d, sem):
-        trs = [RemoteDMATransfer(dst_ids=ids, dma_engine_mask=bitmask(engs), remote_sem=T.sem[sem], srcs=[s[0]], dsts=[d(r)[0] for r in peers])]
+        trs = [RemoteDMATransfer(dst_ids=ids, dma_engine_mask=sum(1 << e for e in engs), remote_sem=T.sem[sem], srcs=[s[0]], dsts=[d[0] for r in peers])]
         sent[0] += len(engs)
-        rec("g", lambda: g.remote_dma_fused(trs, local_sem=T.sem.sent), [], [s], kind="r")
+        return rec([("g", lambda: g.remote_dma_fused(trs, local_sem=T.sem.sent), 0.3)], [], [s], kind="r")
 
     def arrive(sem, calls, views):
-        rec(None, None, views, [], kind="x", ext=(sem, calls * len(engs) * len(peers)))
+        rec([(None, None, FLY + ROWS * len(calls))], views, [], kind="x", ext=(sem, len(calls) * len(engs) * len(peers), calls))
 
     def pick(oq, oz, wq, wz, lst):
         ac(oz, ind(wz, lst), F.Copy)
         cp(b32(oq), ind(b32(wq), lst))
 
-    def place(r, at):
-        return 192 + 48 * ((r - at - 1) % N)
+    def const(n, c, pool="tf"):
+        w = tmp(n, pool)
+        ms(w(), c)
+        return w
 
-    load("s", V("ti", 0, 192), T.it[:])
-    load("s", V("tx"), T.x[:])
-    loose = {"allow_small_or_imprecise_dtypes": True}
+    def decode(a, n, skip):
+        for b in range(4):
+            mm(V("psD", 512 * b, 512 * b + n), blk("eq", 128, b), blk("es", 128, b), V("pq", a, a + n), V("pz", a, a + n))
+            times(V("hdv", PW * b + a + skip, PW * b + a + n), V("psD", 512 * b + skip, 512 * b + n), 0.5)
+
+    load(V("ti", 0, 192), T.it[:])
+    load(V("tx"), T.x[:])
+    row, ep, dup, wc = tmp(96), tmp(24), tmp(6), tmp(PW, "tb")
     iota(col("pint", 0), [[0, 1]], 0, 1)
-    iota(V("row"), [[1, 96]], 0, 0, **loose)
-    iota(V("r128"), [[1, 128]], 0, 0, **loose)
-    iota(V("ep"), [[32, 3], [96, 4], [16, 2]], 0, 0, **loose)
+    iota(row(), [[1, 96]], 0, 0)
+    iota(V("r128"), [[1, 128]], 0, 0)
+    iota(ep(), [[32, 3], [96, 4], [16, 2]], 0, 0)
+    iota(dup(), [[16, 3], [0, 2]], NI * me, 0)
+    iota(wc(), [[1, PW]], -128, 0)
     ms(V("ti", 192, 512), 0.0)
     ms(V("te"), 0.0)
-    for j, (sh, m) in enumerate([(4, 1), (4, 1), (5, 1), (6, 1), (0, 15), (0, 31), (0, 127)]):
+    for j, (sh, m) in enumerate([(4, 1), (4, 1), (5, 1), (0, 15), (0, 31), (0, 127)]):
         ts(col("bint", j), col("pint", 0), sh, A.logical_shift_right, m, A.bitwise_and)
-    cp(V("bits", 0, 7), V("bint", 0, 7))
-    h, hh, q0, q1, s16, s32, pf = col("bits", 0), V("bits", 0, 2), col("bits", 2), col("bits", 3), col("bits", 4), col("bits", 5), col("bits", 6)
-    E_I, E_P, E_2, E_S, E_H = 0, 4, 28, 40, 52
-    KC, NG, CP, DM, GD, X0, PAD = 0, 4, 8, 12, 16, 20, 25
-    ms(V("cf", 0, 4), 0.0)
-    ts(V("cf", E_I, E_I + 3), V("row", 0, 48, 16), s16, A.add)
-    ts(V("cf", E_P, E_P + 24), V("ep"), s16, A.add)
+    cp(V("bits", 0, 6), V("bint", 0, 6))
+    h, hh, q0, s16, s32, pf = col("bits", 0), V("bits", 0, 2), col("bits", 2), col("bits", 3), col("bits", 4), col("bits", 5)
+    l_i, l_p, l_d, l_s = tmp(3, "tu"), tmp(24, "tu"), tmp(6, "tu"), tmp(8, "tu")
+    ts(l_i(), row(0, 48, 16), s16, A.add)
+    ts(l_p(), ep(), s16, A.add)
+    ts(l_d(), dup(), s16, A.add)
+    for b in range(2):
+        for f in range(2):
+            ts(l_s(4 * f + 2 * b, 4 * f + 2 * b + 2), hh, 4.0, A.mult, float(8 * b + f), A.add)
     ts(V("te", 2, 514, 4), V("r128"), pf, A.is_equal)
-    cp(V("co", 0, 28), V("cf", 0, 28))
     ts(V("te", 523, 1035, 4), V("r128"), pf, A.is_equal)
     quant(V("iq"), V("isc"), V("ti"))
-    send(b8(V("iq", 0, NI)), lambda r: b8(blk("pq0", NI, me)), "items")
-    send(V("isc", 0, NI), lambda r: blk("pz0", NI, me), "items")
-    iota(V("wc", 0, 384), [[16, 12], [0, 2], [1, 16]], -128, 0, **loose)
+    first = [send(b8(V("iq", 0, NI)), b8(blk("pq", NI, me)), "items"), send(V("isc", 0, NI), blk("pz", NI, me), "items")]
     for b, a in enumerate([2, 522, 0, 520]):
         quant(blk("eq", 128, b), blk("es", 128, b), V("te", a, a + 512))
-    pick(blk("pq0", NI, me), blk("pz0", NI, me), V("iq"), V("isc"), V("co", E_I, E_I + 3))
-    ms(V("neg"), -1e29)
-    ts(col("k", 26), pf, s32, A.subtract, 3.0, A.mult)
-    ts(col("k", X0), q0, h, A.not_equal, 4.0, A.mult)
-    ts(V("pf", 0, 3), V("row", 0, 96, 32), s32, A.add)
-    ms(V("fe"), 0.0)
+    pick(blk("pq", NI, me), blk("pz", NI, me), V("iq"), V("isc"), l_i())
     quant(V("xq"), V("xs"), V("tx"))
-    ts(col("k", 27), col("k", 26), s32, A.add)
-    pick(V("xpq"), V("xps"), V("xq"), V("xs"), V("co", E_P, E_P + 24))
+    pick(V("xpq"), V("xps"), V("xq"), V("xs"), l_p())
     for b in range(4):
         mm(V("psD", 512 * b, 512 * b + NB), blk("eq", 128, b), blk("es", 128, b), V("xq"), V("xs"))
-    for b in range(4):
-        ac(blk("hdx", NB, b), V("psD", 512 * b, 512 * b + NB), F.Copy, scale=0.5)
-    ts(col("k", 32), q1, 2.0, A.mult, col("k", X0), A.add)
-    ts(col("k", 33), q1, -2.0, A.mult, col("k", X0), A.add)
-    ts(V("od1"), V("row", 0, 32), s32, A.is_ge, -0.5, A.add)
-    ts(V("k", KC, KC + 3), V("row", 0, 96, 32), col("k", 27), A.add, 320.0, A.add)
-    ts(col("k", 34), col("k", 33), 2.0, A.add)
-    ts(V("cf", E_2, E_2 + 2), hh, 0.0, A.mult, col("k", 32), A.add)
-    for b in range(2):
-        ts(blk("od2", 64, b), V("row", 0, 64), col("pf", b), A.is_ge, -0.5, A.add)
-    ts(V("cf", E_2 + 2, E_2 + 4), hh, 0.0, A.mult, col("k", 34), A.add)
-    ts(col("k", 35), col("k", 34), col("k", 32), A.subtract)
+        times(blk("hdx", NB, b), V("psD", 512 * b, 512 * b + NB), 0.5)
+    neg, zero, one, four, low = const(192, -1e29), const(32, 0.0), const(32, 1.0), const(1, -4.0), const(1, -HELD / 8)
+    up, down, lose, two = const(1, MAGIC), const(1, -MAGIC), const(1, -2.0 ** 17), const(2, -KEY)
+    mid, shift, far, minus = const(1, MID), const(1, 128.0), const(32, -HELD / 2), const(32, -1.0)
+    k, od0, od1, pat1, pat2, bm, rz, cb = tmp(48), tmp(32), tmp(32), tmp(32), tmp(32), tmp(256, "tb"), tmp(80), tmp(320, "tb")
+    ts(col(k, 0), pf, s32, A.subtract, 3.0, A.mult)
+    ts(col(k, 1), col(k, 0), s32, A.add, NB * me - MID, A.add)
+    ts(k(4, 7), row(0, 96, 32), col(k, 1), A.add)
+    ts(od0(), row(0, 32), s32, A.is_lt, -2.0 ** -24, A.mult)
+    ts(od1(), od0(), 1.0, A.add)
+    ts(col(k, 8), q0, 1000.0, A.mult)
+    ts(col(k, 9), q0, -1000.0, A.mult, 1000.0, A.add)
     for j in range(2):
-        ts(blk("pat", 16, j), V("row", 0, 16), -2.0, A.mult, 96.0, A.add)
-    ts(col("k", 36), s16, 1.0, A.min, col("k", 35), A.mult)
-    ms(V("pat", 32, 64), 999.0)
-    ms(col("land", 4 * me + 3), 0.0)
-    ts(col("cf", E_2 + 4), col("k", 36), col("k", 32), A.add, 1.0, A.add)
-    for j in range(2):
-        ts(V("pat", 32 + 16 * j, 32 + 16 * j + NK), V("row", 0, NK), -2.0, A.mult, 64.0, A.add)
-    cp(V("co", E_2, E_2 + 5), V("cf", E_2, E_2 + 5))
-    ms(V("gl"), 0)
+        ts(blk(pat1, 16, j), row(0, 16), col(k, 8 + j), A.add)
+        ts(pat2(16 * j, 16 * j + NK), row(0, NK), s16, A.subtract)
+        ms(pat2(16 * j + NK, 16 * j + 16), 999.0)
+    ts(col(k, 10), h, -1.0, A.mult, 1.0, A.add)
+    ts(col(k, 11), s16, float(NK), A.is_lt)
+    ts(k(16, 20), row(0, 64, 16), s16, A.add, 192.0, A.add)
+    ts(k(20, 24), k(16, 20), 1.0, A.add, col(k, 11), A.mult)
+    ts(k(24, 28), row(0, 4), PW * KEY, A.mult, -KEY, A.add)
+    for r in range(N):
+        ts(bm(80 * r, 80 * r + 16), row(0, 16), s16, A.is_lt)
+    ms(cb(64, 320, 80), -64.0)
+    ms(rz(64, 80), 8192.0)
+    ms(V("pm", 7, 600, 200), -1e29)
     ms(V("tn"), 0.0)
-
-    def later():
-        load("s", V("tw"), T.w[:])
-        ts(col("k", PAD), s16, float(NK), A.is_ge, 1000.0, A.mult)
-        ts(V("k", DM, DM + 2), V("row", 0, 32, 16), s16, A.add, 384.0, A.add)
-        for b in range(2):
-            for f in range(2):
-                ts(V("cf", E_S + 4 * f + 2 * b, E_S + 4 * f + 2 * b + 2), hh, 4.0, A.mult, float(8 * b + f), A.add)
-            c = [place(2 * b, me), place(2 * b + 1, me)]
-            ts(col("k", 28 + b), h, float(c[1] - c[0]), A.mult, float(c[0] - 128), A.add)
-        for b in range(6):
-            c = [4 * ((me + 1 + m // 3) % N) + 2 if m % 3 == 0 else 2 for m in (2 * b, 2 * b + 1)]
-            ts(V("cf", E_H + 2 * b, E_H + 2 * b + 2), hh, float(c[1] - c[0]), A.mult, float(c[0]), A.add)
-        ts(V("k", CP, CP + 2), V("pf", 0, 2), col("k", PAD), A.add)
-        ts(V("k", GD, GD + 2), V("k", DM, DM + 2), -1.0, A.mult, -1.0, A.add)
-        cp(V("co", E_S, E_S + 8), V("cf", E_S, E_S + 8))
-        cp(V("co", E_H, 64), V("cf", E_H, 64))
-        for b in range(2):
-            ts(blk("ce", 32, b), V("row", 0, 32), 0.0, A.mult, col("k", CP + b), A.add)
-            ts(blk("mv", 16, b), V("row", 0, 16), col("k", 28 + b), A.add)
-        ms(V("wm", 384, 432), 0.0)
-        ms(V("pp0"), 0.0)
-        ms(V("hp0", 0, 192), -1.0)
-
-    def latest():
-        ts(V("k", NG, NG + 3), V("k", KC, KC + 3), -1.0, A.mult, 320.0 - NB * me, A.add)
-        ms(V("cb"), BIG)
-        ms(col("k", 40), -16 * BIG)
-        ms(col("k", 41), -48 * BIG)
-        ms(V("land", 16 + 4 * me + 3, 48, 16), 0.0)
-        ms(V("pp1", 192, 384), 0.0)
-
-    arrive("items", 2, [blk(n, NI, r) for n in ("pq0", "pz0") for r in peers])
+    ms(V("hdv"), 0.0)
+    ms(V("land", 4 * me + 2, 48, 16), 0.0)
+    ms(V("land", 4 * me + 3, 48, 16), 0.0)
+    ms(V("pp"), 0.0)
+    ms(V("hp"), -1.0)
+    cp2(V("wm"), wc(0, 256))
+    for kk in range(3):
+        ms(V("v", 256 * kk + 192, 256 * kk + 256), 0.0)
+    ms(V("yo", 192, 256), 0.0)
+    arrive("items", first, [blk(n, NI, r) for n in ("pq", "pz") for r in peers])
+    decode(0, 192, 0)
 
     for t in range(NR):
-        pq, pz, nq, nz = "pq%d" % t, "pz%d" % t, "pq%d" % (t + 1), "pz%d" % (t + 1)
-        pp, np_, hp, nh = "pp%d" % (t % 2), "pp%d" % (1 - t % 2), "hp%d" % (t % 2), "hp%d" % (1 - t % 2)
-        L = 16 * t
+        last = t == NR - 1
+        oq, oz, L, O = "oq%d" % t, "oz%d" % t, 16 * t, 192 + 64 * t
+        g1, x1, r1, a3, kb, fe = tmp(3), tmp(96), tmp(96), tmp(3), tmp(3), tmp(6)
+        u, w, sign = (A.min, A.max, -1.0) if t else (A.max, A.min, 1.0)
         for kk in range(3):
-            mm(V("psS", 512 * kk, 512 * kk + 192), blk("xpq", 128, kk), blk("xps", 128, kk), V(pq, 0, 192), V(pz, 0, 192))
-        for b in range(4):
-            mm(V("psD", 512 * b, 512 * b + 192), blk("eq", 128, b), blk("es", 128, b), V(pq, 0, 192), V(pz, 0, 192))
-
-        def val(kk):
-            tt(blk("v", 192, kk), V("psS", 512 * kk, 512 * kk + 192), V(pp, 0, 192), A.subtract)
-
-        def src(kk, a):
-            return V("v", 192 * kk + a, 192 * kk + 192) if t else V("psS", 512 * kk + a, 512 * kk + 192)
-
-        def first(kk):
-            scan(blk("pm", 192, kk), src(kk, 0), src(kk, 0) if t else V("neg"), A.max, A.max)
-            ac(blk("jk", 192, kk), blk("pm", 192, kk), F.Sign, bias=col("pm", 192 * kk + 191), scale=-1.0, acc=col("g3", kk))
-
-        def second(kk):
-            scan(V("qm", 192 * kk, 192 * kk + 191), src(kk, 1), V("pm", 192 * kk, 192 * kk + 191), A.max, A.min)
-
-        def bid(kk):
-            ts(blk("x1", 32, kk), blk("fe", 32, kk), col("pm", 192 * kk + 191), A.add, col("qm", 192 * kk + 190), A.subtract)
-
-        def turn(kk):
-            tr(blk("r1", 32, kk), blk("x1", 32, kk))
-            ac(blk("sg", 32, kk), blk("r1", 32, kk), F.Sign, bias=col("x1", 32 * kk), scale=-1.0)
-
-        def count(kk):
-            ac(blk("jk", 96, kk), blk("ee", 96, kk), F.Sign, acc=col("a3", kk))
-
-        def near(kk):
-            tt(blk("ee", 32, 4 * kk), blk("sg", 32, kk), V("od1"), A.add)
-
-        def far(kk, a, b, op):
-            ts(V("ee", 96 * kk + 32 * a, 96 * kk + 32 * b), V("r1", 32 * a, 32 * b), col("x1", 32 * kk), op, -0.5, A.add)
-
-        if t:
-            val(0)
-            val(1)
-            first(0)
-            val(2)
-            first(1)
-            second(0)
-            first(2)
-        else:
-            first(0)
-            first(1)
-            first(2)
-            second(0)
-        second(1)
-        bid(0)
-        second(2)
-        bid(1)
-        turn(0)
-        bid(2)
-        turn(1)
-        turn(2)
-        far(2, 0, 2, A.is_lt)
-        near(0)
-        far(0, 1, 3, A.is_le)
-        count(0)
-        near(1)
-        far(1, 0, 1, A.is_lt)
-        far(1, 2, 3, A.is_le)
-        count(1)
-        near(2)
-        count(2)
+            if t == 0:
+                mm(V("psS", 512 * kk, 512 * kk + 192), blk("xpq", 128, kk), blk("xps", 128, kk), V("pq", 0, 192), V("pz", 0, 192))
+            o = ("v", 256 * kk) if t else ("psS", 512 * kk)
+            P = 200 * kk + 8
+            top, sec, fw = col("pm", P + 191), col("qm", 192 * kk + 190), tmp(32)
+            scan(V("pm", P, P + 192), V(o[0], o[1], o[1] + 192), V(o[0], o[1], o[1] + 192) if t else neg(), u, u, -1e29 * sign)
+            scan(V("qm", 192 * kk, 192 * kk + 191), V(o[0], o[1] + 1, o[1] + 192), V("pm", P, P + 191), u, w, -1e29 * sign)
+            if t == 0:
+                axb(fw(), minus(), top, col(zero, 0))
+            elif kk < 2:
+                ac(col(fe, kk), four(), F.Relu, bias=low(), scale=top)
+                axb(fw(), one(), top, col(fe, kk))
+            else:
+                ts(fw(), far(), top, A.subtract, top, A.max)
+            ts(blk(x1, 32, kk), fw(), sec, A.subtract if t else A.add, -TINY, A.add)
+            axb(col(fe, 3 + kk), sec, sign, col(fw, 0))
+            tr(blk(r1, 32, kk), blk(x1, 32, kk))
+            count(col(g1, kk), V("pm", P - 1, P + 192), F.Sign, bias=top, scale=-1.0)
+            axb(col(kb, kk), col(g1, kk), KEY * sign, col(k, 4 + kk))
+            if t == 0:
+                times(V("v", 256 * kk, 256 * kk + 192), V("psS", 512 * kk, 512 * kk + 192), -1.0)
         for kk in range(3):
-            ts(col("g3", 4 + kk), col("g3", kk), 512.0, A.mult, col("k", KC + kk), A.add)
-        for kk in range(3):
-            ts(blk("m1", 32, kk), V("pat", 0, 32), col("a3", kk), A.is_equal, col("x1", 32 * kk), A.mult)
-            ts(blk("m1", 32, 3 + kk), V("pat", 0, 32), col("a3", kk), A.is_equal, col("g3", 4 + kk), A.mult)
-        for b in range(3):
-            ac(blk("hdv", 192, b), V("psD", 512 * b, 512 * b + 192), F.Copy, scale=0.5)
-        tr(V("t1", 0, 96), V("m1", 0, 96))
-        tr(V("t1", 96, 192), V("m1", 96, 192))
-        red(col("c8", 0), V("t1", 0, 96), A.add)
-        red(col("c8", 1), V("t1", 96, 192), A.add)
-        cp(V("c8", 2, 4, 1, 0, 64), V("c8", 0, 2, 1, 64, 128))
-        ac(V("c8", 2, 4, 1, 64, 128), V("c8", 0, 2, 1, 0, 64), F.Copy)
-        cp(V("c8", 4, 8, 1, 0, 32), V("c8", 0, 4, 1, 32, 64))
-        ac(V("c8", 4, 8, 1, 64, 96), V("c8", 0, 4, 1, 96, 128), F.Copy)
-        cp(V("c8", 4, 8, 1, 32, 64), V("c8", 0, 4, 1, 0, 32))
-        ac(V("c8", 4, 8, 1, 96, 128), V("c8", 0, 4, 1, 64, 96), F.Copy)
-        cp(V("x2"), ind(V("c8"), V("co", E_2, E_2 + 5)))
-        ac(blk("hdv", 192, 3), V("psD", 1536, 1536 + 192), F.Copy, scale=0.5)
-        tr(V("r2"), V("x2", 0, 64))
-        ts(V("d2", 0, 2), V("x2", 64, 66), 1.0 / 512, A.mult, MAGIC, A.add)
+            ee, th, x = tmp(96, "tb"), tmp(32), col(x1, 32 * kk)
+            axb(th(), od1(), x, col(zero, 0))
+            tt(blk(ee, 32, kk), blk(r1, 32, kk), th(), A.is_lt)
+            if kk > 0:
+                ts(ee(0, 32 * kk), r1(0, 32 * kk), x, A.is_le)
+            if kk < 2:
+                ts(ee(32 * kk + 32, 96), r1(32 * kk + 32, 96), x, A.is_lt)
+            total(col(a3, kk), ee())
+        c8, x2, kc, r2, c2 = tmp(2), tmp(64), tmp(2), tmp(64), tmp(2)
+        for f in range(2):
+            m1, t1 = tmp(96), tmp(96)
+            for kk in range(3):
+                ts(blk(m1, 32, kk), pat1(), col(a3, kk), A.is_equal, col(kb, kk) if f else col(fe, 3 + kk), A.mult)
+            tr(t1(), m1())
+            total(col(c8, f), t1())
         for b in range(2):
-            ac(blk("sg", 64, b), V("r2"), F.Sign, bias=col("x2", 32 * b), scale=-1.0)
-        ts(V("d2", 4, 6), V("d2", 0, 2), -MAGIC, A.add, -512.0, A.mult)
-        ts(V("d2", 2, 4), V("d2", 0, 2), -MAGIC, A.add)
+            for q in range(4):
+                axb(x2(32 * b, 32 * b + 32, 1, 32 * q, 32 * q + 32), one(0, 32, 1, 32 * q, 32 * q + 32),
+                    col(c8, 0, 64 * b, 64 * b + 32), col(c8, 0, 64 * b + 32, 64 * b + 64))
+            axb(col(kc, b, 0, 32), col(c8, 1, 64 * b, 64 * b + 32), 1.0, col(c8, 1, 64 * b + 32, 64 * b + 64))
+        cp2(kc(0, 2, 1, 32, 64), kc(0, 2, 1, 0, 32))
+        cp2(kc(0, 2, 1, 64, 128), kc(0, 2, 1, 0, 64))
+        tr(r2(), x2())
         for b in range(2):
-            tt(blk("ee", 64, b), blk("sg", 64, b), blk("od2", 64, b), A.add)
-            ac(blk("jk", 64, b), blk("ee", 64, b), F.Sign, acc=col("a3", 4 + b))
-        for b in range(2):
-            ts(col("d2", 6 + b), col("d2", 4 + b), col("x2", 64 + b), A.add, 192.0 + NB * me, A.add)
-        for b in range(2):
-            for f, fld in enumerate([col("x2", 32 * b), col("d2", 2 + b), col("d2", 6 + b)]):
-                ts(blk("m2", 32, 2 * f + b), V("pat", 32, 64), col("a3", 4 + b), A.is_equal, fld, A.mult)
-        for f in range(3):
-            tr(blk("t2", 64, f), blk("m2", 64, f))
-        for f in range(3):
-            red(col("land", L + 4 * me + f), blk("t2", 64, f), A.add)
-        mine = V("land", L + 4 * me, L + 4 * me + 4)
-        send(mine, lambda r: mine, "bids%d" % t)
-        ts(col("gl", 2 * t), col("land", L + 4 * me + 1), -1.0, A.add, 0.0, A.max)
-        ts(col("xl", 0), col("land", L + 4 * me + 2), -float(NB * me), A.add, 0.0, A.max)
-        for b in range(4):
-            ac(blk("gv", 16, b), ind(blk("hdv", 192, b), col("gl", 2 * t)), F.Copy)
-        for b in range(4):
-            tt(V("tn", b, 64, 4), ind(blk("hdx", NB, b), col("xl", 0)), blk("gv", 16, b), A.add)
-        quant(V(pq, OWN, PW), V(pz, OWN, PW), V("tn"))
-        send(b8(V(pq, OWN, OWN + NK)), lambda r: b8(V(pq, place(me, r), place(me, r) + NK)), "cols%d" % t)
-        send(V(pz, OWN, OWN + NK), lambda r: V(pz, place(me, r), place(me, r) + NK), "cols%d" % t)
+            ee, x = tmp(64, "tb"), col(x2, 32 * b)
+            ts(blk(ee, 32, 1 - b), blk(r2, 32, 1 - b), x, A.is_le if b else A.is_lt)
+            ts(blk(ee, 16, 2 * b), blk(r2, 16, 2 * b), x, A.is_le, h, A.mult)
+            ts(blk(ee, 16, 2 * b + 1), blk(r2, 16, 2 * b + 1), x, A.is_lt, col(k, 10), A.mult)
+            total(col(c2, b), ee())
+        for f in range(2):
+            m2, t2 = tmp(64), tmp(64)
+            for b in range(2):
+                ts(blk(m2, 32, b), pat2(), col(c2, b), A.is_equal, col(kc, b) if f else col(x2, 32 * b), A.mult)
+            tr(t2(), m2())
+            total(col("land", L + 4 * me + f), t2())
+        mine, key = V("land", L + 4 * me, L + 4 * me + 4), col("land", L + 4 * me + 1)
+        bids = [send(mine, mine, "bids%d" % t)]
         if t == 0:
-            later()
-            latest()
-        if t == 1:
+            ms(V("pm", 7, 600, 200), 1e29)
+            load(V("tw"), T.w[:], [key])
             quant(V("wq"), V("ws"), V("tw"))
-        ac(V("wm", 0, 384), V("wc", 0, 384), F.Copy)
-        arrive("bids%d" % t, 1, [V("land", L + 4 * r, L + 4 * r + 4) for r in peers])
-        lw, goal = V("land", L, L + 16), V("xs3", 64, 128, 32)
-        cp(V("xs3", 64, 128), ind(lw, V("co", E_S + 4, E_S + 8)))
-        ac(V("xs3", 0, 64), ind(lw, V("co", E_S, E_S + 4)), F.Copy)
-        ac(V("sm", 0, 2), goal, F.Copy, scale=-BIG)
-        tr(V("rs", 64, 128), V("xs3", 64, 128))
-        ts(V("sm", 4, 6), goal, -24.5, A.add, 1.0 / NI, A.mult)
-        tr(V("rs", 0, 64), V("xs3", 0, 64))
-        ts(V("sm", 8, 10), V("sm", 4, 6), MAGIC, A.add)
-        for b in range(2):
-            ac(blk("tt", 64, b), V("rs", 64, 128), F.Abs, bias=col("sm", b), scale=BIG)
-        for b in range(2):
-            ac(blk("jk", 64, b), V("rs", 0, 64), F.Sign, bias=col("xs3", 32 * b), scale=-1.0, acc=col("sm", 24 + b))
-        tt(blk("mb", 64, 0), V("rs", 0, 64), blk("tt", 64, 0), A.subtract)
-        ts(V("sm", 16, 18), V("sm", 8, 10), -MAGIC, A.add, 1.0 / 16, A.mult)
-        tt(blk("mb", 64, 1), V("rs", 0, 64), blk("tt", 64, 1), A.subtract)
-        for b in range(2):
-            ac(col("sm", 20 + b), col("xs3", 64 + 32 * b), F.Identity, bias=col("sm", 16 + b), scale=2.0 ** -20)
-        for b in range(2):
-            ac(col("sm", 36 + b), col("sm", 24 + b), F.Identity, bias=col("sm", 20 + b), scale=-2.0 ** -12)
-        for b in range(2):
-            scan(blk("pb", 64, b), blk("mb", 64, b), blk("mb", 64, b), A.max, A.max)
-            ac(blk("jk", 64, 4 + b), blk("pb", 64, b), F.Sign, bias=col("pb", 64 * b + 63), scale=-1.0, acc=col("sm", 32 + b))
-        ts(V("g4", 0, 7, 2), V("land", L + 1, L + 16, 4), -1.0, A.add, 0.0, A.max)
-        ts(V("sm", 6, 8), goal, -8.5, A.add, 1.0 / 16, A.mult)
-        ts(V("sm", 40, 42), V("sm", 16, 18), -2.0 ** -5, A.add)
+            mm(V("psY", 0, 192), V("wq"), V("ws"), V("pq", 0, 192), V("pz", 0, 192))
+            cp2(V("yo", 0, 192), V("psY", 0, 192))
+        gl, g4, xl, xk = tmp(2, "tu"), tmp(4, "tu"), tmp(1, "tu"), tmp(1)
+        ts(gl(), two(), key, A.add, 1 / KEY, A.mult)
+        ts(xk(), key, MID - KEY - NB * me, A.add)
+        ts(xl(), gl(0, 1), -KEY, A.mult, xk(), A.add)
+        if t:
+            lr, lc = tmp(32, "tb"), tmp(32, "tb")
+            cp2(lr(), ind(V("wm"), gl()))
+            tr(lc(), lr())
+            ts(g4(0, 1), col(lc, 0), 128.0, A.add)
+            for b in range(4):
+                cp2(blk("gv", 16, b), ind(blk("hdx", NB, b), xl()))
+                tt(V("tn", b, 64, 4), ind(blk("hdv", PW, b), g4(0, 1)), blk("gv", 16, b), A.add)
+        else:
+            ts(g4(), k(24, 28), key, A.add, 1 / KEY, A.mult)
+            cp2(V("gv"), ind(V("hdv"), g4()))
+            for b in range(4):
+                tt(V("tn", b, 64, 4), ind(blk("hdx", NB, b), xl()), blk("gv", 16, b), A.add)
+        quant(V(oq), V(oz), V("tn"))
+        own = (O + 16 * me, O + 16 * me + 16)
+        cols = [send(b8(V(oq, 0, 16)), b8(V("pq", *own)), "cols%d" % t), send(V(oz, 0, 16), V("pz", *own), "cols%d" % t)]
+        pick(V("pq", *own), V("pz", *own), V(oq), V(oz), l_i(0, 1))
+        vo = [tmp(64) for kk in range(3)]
+        if not last:
+            xo, ro, po = tmp(64), tmp(64), tmp(16)
+            for f in range(2):
+                axb(blk(xo, 32, f), zero(), 1.0, col("land", L + 4 * me + f))
+            tr(ro(), xo())
+            tt(po(), ind(V("pp"), gl(0, 1)), ro(0, 16), A.subtract)
+            for kk in range(3):
+                e, pk = tmp(16), tmp(16)
+                ts(e(), ro(32, 48), col(kb, kk), A.is_equal, HELD, A.mult)
+                tt(pk(), po(), e(), A.subtract)
+                mm(V("psS", 512 * kk, 512 * kk + 128), blk("xpq", 128, kk), blk("xps", 128, kk), V(oq), V(oz))
+                tt(blk(vo[kk], 16, me), pk(), V("psS", 512 * kk, 512 * kk + 16), A.subtract)
+        arrive("bids%d" % t, bids, [V("land", L + 4 * r, L + 4 * r + 4) for r in peers])
+        lw, keys = V("land", L, L + 16), V("land", L + 1, L + 16, 4)
+        xs, rs, sm, gs, pr, nn = tmp(128), tmp(128), tmp(64), tmp(4, "tu"), tmp(64), tmp(16)
+        for f in range(2):
+            cp2(blk(xs, 64, f), ind(lw, blk(l_s, 4, f)))
+            tr(blk(rs, 64, f), blk(xs, 64, f))
+        axb(sm(0, 4), keys, 1 / KEY, up())
+        axb(sm(4, 8), sm(0, 4), 1.0, down())
+        ts(blk("oi", 4, t), keys, 1 / (KEY * NI), A.mult, -24.5 / NI, A.add)
+        ts(sm(8, 12), blk("oi", 4, t), 256.0, A.mult)
+        axb(sm(12, 16), sm(4, 8), 2.0 ** -8, shift())
+        tt(sm(16, 20), sm(12, 16), sm(8, 12), A.add)
+        tt(sm(20, 24), sm(4, 8), k(20, 24), A.subtract)
+        ts(gs(), keys, 1 / KEY, A.mult, -1.0, A.add)
+        tt(pr(), ind(V("pp"), gs()), blk(rs, 64, 0), A.subtract)
+        for r in range(N):
+            nb, pen, z = col("land", L + 4 * r), tmp(64, "tb"), tmp(64, "tb")
+            if r > 0:
+                ts(bm(64 * r, 80 * r), rs(0, 16 * r), nb, A.is_le)
+            if r < N - 1:
+                ts(bm(80 * r + 16, 64 * r + 64), rs(16 * r + 16, 64), nb, A.is_lt)
+            ac(pen(), blk(rs, 64, 1), F.Abs, bias=col(sm, 4 + r), scale=-1 / KEY)
+            tt(z(), blk(bm, 64, r), pen(), A.subtract)
+            count(col(nn, 4 * r), z(), F.Relu, bias=lose(), scale=2.0 ** 18)
+            count(col(sm, 36 + r), blk(rs, 64, 0), F.Sign, bias=nb, scale=-1.0)
+        kw, xz, of, s3, sw = tmp(16), tmp(64), tmp(4, "tu"), tmp(16), tmp(64)
+        tt(s3(0, 16, 4), sm(36, 40), sm(16, 20), A.add)
+        cp2(sw(), ind(s3(0, 13), blk(l_s, 4, 0)))
+        tt(kw(0, 16, 4), nn(0, 16, 4), s3(0, 16, 4), A.add)
+        tt(xz(), ind(nn(0, 13), blk(l_s, 4, 0)), sw(), A.add)
+        tr(rz(0, 64), xz())
+        for r in range(N):
+            count(col(sm, 48 + r), rz(), F.Sign, bias=col(kw, 4 * r), scale=-1.0)
+            ts(cb(80 * r, 80 * r + 64), rz(0, 64), col(sm, 8 + r), A.is_lt, 2.0, A.mult)
+            total(col(sm, 52 + r), cb(80 * r, 80 * r + 65))
+            ts(col(sm, 56 + r), col(sm, 48 + r), col(sm, 52 + r), A.is_lt, col(sm, 20 + r), A.mult)
+        tt(of(), sm(56, 60), k(16, 20), A.add)
+        arrive("cols%d" % t, cols, [V(n, O + 16 * r, O + 16 * r + 16) for r in peers for n in ("pq", "pz")])
+        new = (V("pq", O - 64, O + 64), V("pz", O - 64, O + 64))
+        if not last:
+            for kk in range(3):
+                mm(V("psS", 512 * kk, 512 * kk + 128), blk("xpq", 128, kk), blk("xps", 128, kk), *new)
+                for a, b in ((0, 16 * me), (16 * me + 16, 64)):
+                    if a < b:
+                        tt(vo[kk](a, b), pr(a, b), V("psS", 512 * kk + 64 + a, 512 * kk + 64 + b), A.subtract)
+                cp(ind(blk("v", 256, kk), of()), vo[kk]())
+            decode(O - 64, 128, 64)
+        cp(ind(V("wm"), of()), wc(O, O + 64))
+        yn, hr = tmp(64), tmp(256)
+        mm(V("psY", 0, 128), V("wq"), V("ws"), *new)
+        cp2(yn(), V("psY", 64, 128))
+        cp(ind(V("yo"), of()), yn())
+        axb(blk(hr, 64, 0), blk(rs, 64, 1), 1 / KEY, up())
+        axb(blk(hr, 64, 1), blk(hr, 64, 0), 1.0, down())
+        axb(blk(hr, 64, 2), blk(hr, 64, 1), -KEY, mid())
+        tt(blk(hr, 64, 3), blk(hr, 64, 2), blk(rs, 64, 1), A.add)
+        cp(ind(V("pp"), of()), pr())
+        cp(ind(V("hp"), of()), blk(hr, 64, 3))
+        store("a" if last else "s", T.pr[t:t + 1, :], V("pp", NI * me, NI * me + NI, 1, 0, 1))
+        store("a" if last else "s", T.ho[t:t + 1, :], V("hp", NI * me, NI * me + NI, 1, 0, 1))
 
-        def offer(u):
-            tt(V(pp, place(u, me), place(u, me) + 16), ind(V(pp, 0, 192), col("g4", 2 * u)), blk("rs", 16, u), A.add)
-
-        for b in range(2):
-            ts(blk("xz", 32, b), blk("ce", 32, b), col("sm", 32 + b), A.not_equal, col("sm", 36 + b), A.add)
-        ts(V("sm", 10, 12), V("sm", 6, 8), MAGIC, A.add)
-        tr(V("rz"), V("xz"))
-        for b in range(2):
-            ac(blk("jk", 64, b), V("rz"), F.Sign, bias=col("xz", 32 * b), scale=-1.0, acc=col("sm", 48 + b))
-            ac(blk("jk", 64, 4 + b), V("rz"), F.Sign, bias=col("sm", 40 + b), scale=-1.0, acc=col("sm", 52 + b))
-        ac(V("xh"), ind(lw, V("co", E_H, E_H + 12)), F.Copy)
-        ts(V("sm", 12, 14), V("sm", 10, 12), -MAGIC, A.add, 16.0, A.mult)
-        tt(V("sm", 14, 16), goal, V("k", GD, GD + 2), A.add)
-        for b in range(2):
-            ts(col("sm", 56 + b), col("sm", 32 + b), col("k", CP + b), A.is_equal, 2.0 * NM, A.mult)
-        tt(V("sm", 44, 46), V("sm", 12, 14), V("sm", 14, 16), A.add)
-        for b in range(2):
-            ts(col("sm", 60 + b), col("sm", 48 + b), col("sm", 52 + b), A.subtract, col("sm", 56 + b), A.is_lt)
-        for b in range(2):
-            ts(col("of", b), col("sm", 60 + b), col("sm", 44 + b), A.mult, col("k", DM + b), A.add)
-        offer(0)
-        cp(ind(V("wm", 0, 416), V("of")), V("mv"))
-        offer(1)
-        cp(ind(V("wm", 16, 432), V("of")), V("mv"))
-        offer(2)
-        tr(V("tm"), V("wm", 0, 384))
-        offer(3)
-        tt(V("mx"), V("tm", 0, 384, 32), V("tm", 16, 384, 32), A.max)
-        lst = V("ml", 16 * t, 16 * t + 12)
-        ts(lst, V("mx"), 128.0, A.add)
-        arrive("cols%d" % t, 2, [V(n, place(r, me), place(r, me) + NK) for r in peers for n in (pq, pz)])
-        pick(V(nq, 0, 192), V(nz, 0, 192), V(pq), V(pz), lst)
-        tr(V(hp, 192, 384), V("xh"))
-        own = (NI * me, NI * me + NI)
-        if t == NR - 1:
-            mm(V("psY", 0, 192), V("wq"), V("ws"), V(nq), V(nz))
-            store("s", T.oc[:], b8(V(nq, *own)))
-            cp(V("yo"), V("psY", 0, 192))
-            for u in range(4):
-                store("s" if u < 2 else "a", T.osc[4 * u:4 * u + 4, :], V(nz, own[0], own[1], 1, 32 * u, 32 * u + 4))
-            store("s", T.y[:], V("yo"))
-        ac(V(np_, 0, 192), ind(V(pp), lst), F.Copy)
-        ac(V(nh, 0, 192), ind(V(hp), lst), F.Copy)
-        q = "s" if t < NR - 1 else "a"
-        store(q, T.pr[t:t + 1, :], V(np_, own[0], own[1], 1, 0, 1))
-        store(q, T.ho[t:t + 1, :], V(nh, own[0], own[1], 1, 0, 1))
-        if t < NR - 1:
-            n = 16 * (2 * t + 1)
-            for kk in range(3):
-                ac(V("fu", 48 * kk, 48 * kk + n), ind(V(nh, 0, 192), V("gl", 0, 2 * t + 1)), F.Abs, bias=col("k", NG + kk))
-            for kk in range(3):
-                ac(V("fj", 48 * kk, 48 * kk + n), V("fu", 48 * kk, 48 * kk + n), F.Sign, acc=col("fm", kk))
-            for kk in range(3):
-                ac(blk("fe", 32, kk), V("cb"), F.Identity, bias=col("k", 40 + t), scale=col("fm", kk))
+    store("s", T.y[:], V("yo", 0, 192))
+    wd, tm, lst = tmp(96, "tb"), tmp(96, "tb"), tmp(3, "tu")
+    cp2(wd(), ind(V("wm"), l_d()))
+    tr(tm(), wd())
+    ts(lst(), tm(0, 96, 32), 128.0, A.add)
+    pick(V("nq"), V("nz"), V("pq"), V("pz"), lst())
+    store("s", T.oc[:], b8(V("nq")))
+    for u in range(4):
+        store("s" if u < 2 else "a", T.osc[4 * u:4 * u + 4, :], V("nz", 0, NI, 1, 32 * u, 32 * u + 4))
 
     emit(g, T, ops, sent[0])
 
 
 def clash(a, b):
-    return a[0] == b[0] and a[1] < b[2] and b[1] < a[2] and not a[3].isdisjoint(b[3])
+    return a[1] < b[2] and b[1] < a[2] and a[3] <= b[4] and b[3] <= a[4] and not a[5].isdisjoint(b[5])
 
 
 def emit(g, T, ops, sent):
     n = len(ops)
-    hist, known, waits, done = {}, {}, [], []
+    hist, deps = {}, []
     for i, o in enumerate(ops):
-        deps = set()
+        d = set()
         if o["kind"] != "x":
             for z in o["r"]:
-                deps.update(j for j, y, w in hist.get(z[0], []) if w and clash(z, y))
+                d.update(j for j, y, w in hist.get(z[0], []) if w and clash(z, y))
             for z in o["w"]:
-                deps.update(j for j, y, w in hist.get(z[0], []) if clash(z, y) and ops[j]["kind"] != "r")
+                d.update(j for j, y, w in hist.get(z[0], []) if clash(z, y) and ops[j]["kind"] != "r")
         for z in o["r"]:
             hist.setdefault(z[0], []).append((i, z, False))
         for z in o["w"]:
             hist.setdefault(z[0], []).append((i, z, True))
-        kn = known.setdefault(o["q"], set())
+        d.discard(i)
+        deps.append(d)
+    sends = [i for i in range(n) if ops[i]["kind"] == "r"]
+    after = [set(deps[i]) | set(ops[i]["ext"][2] if ops[i]["kind"] == "x" else []) for i in range(n)]
+    for a, b in zip(sends, sends[1:]):
+        after[b].add(a)
+    tail = [LOCAL if o["kind"] in "do" else 0.0 for o in ops]
+    aft = [sorted(x) for x in after]
+    span = [min(a[2] for a in ops[i]["alts"]) + tail[i] + WAKE for i in range(n)]
+
+    def plan(fac, lean):
+        rank = [0.0] * n
+        for i in range(n - 1, -1, -1):
+            rank[i] += span[i] * fac[i]
+            for j in aft[i]:
+                if rank[j] < rank[i]:
+                    rank[j] = rank[i]
+        busy, start, end, way = {}, [0.0] * n, [0.0] * n, [None] * n
+        for i in sorted(range(n), key=lambda i: (-rank[i], i)):
+            ready = max([end[j] + WAKE for j in aft[i]] + [0.0])
+            best = None
+            for c, a in enumerate(ops[i]["alts"]):
+                s, at = ready, 0
+                if a[0] is not None:
+                    line = busy.setdefault(a[0], [])
+                    at = len(line)
+                    while at > 0 and line[at - 1][1] > s:
+                        at -= 1
+                    while at < len(line) and s + a[2] > line[at][0]:
+                        s = max(s, line[at][1])
+                        at += 1
+                e = s + a[2] + (lean[i] if c else 0.0)
+                if best is None or e < best[0] - 1e-9:
+                    best = (e, s, a, at)
+            start[i], way[i] = best[1], best[2]
+            end[i] = start[i] + way[i][2] + tail[i]
+            if way[i][0] is not None:
+                busy[way[i][0]].insert(best[3], (start[i], start[i] + way[i][2]))
+        order = sorted(range(n), key=lambda i: (start[i], i))
+        score = max(end)
+        for wake, slow, fly in OTHER:
+            free, fin = {}, [0.0] * n
+            for i in order:
+                q = way[i][0]
+                s = max([fin[j] + wake for j in aft[i]] + [free.get(q, 0.0)])
+                c = way[i][2] * (slow if q else fly)
+                if q:
+                    free[q] = s + c
+                fin[i] = s + c + tail[i]
+            score += max(fin)
+        return score, start, end, way
+
+    seed = [1]
+
+    def draw():
+        seed[0] = (seed[0] * 1103515245 + 12345) % 2147483648
+        return seed[0] / 2147483648.0
+
+    fac, lean = [1.0] * n, [0.0] * n
+    held = plan(fac, lean)
+    for trial in range(TRIES):
+        f2, l2 = list(fac), list(lean)
+        a = int(draw() * n)
+        for u in range(MUT):
+            i = min(n - 1, a + int(draw() * 60))
+            f2[i] = 0.2 + 2.8 * draw() ** 2
+            l2[i] = 0.4 * draw() - 0.2
+        new = plan(f2, l2)
+        if new[0] <= held[0]:
+            held, fac, lean = new, f2, l2
+    start, end, way = held[1:]
+    order = sorted(range(n), key=lambda i: (start[i], i))
+    known, waits, done = {}, {}, {}
+    for i in order:
+        kn = known.setdefault(way[i][0], set())
         ws = []
-        for j in sorted(deps, reverse=True):
-            if j != i and j not in kn:
+        for j in sorted(deps[i], key=lambda j: -end[j]):
+            if j not in kn:
                 ws.append(j)
                 kn.add(j)
                 kn.update(done[j])
-        waits.append(ws)
-        done.append(set(kn) if o["kind"] != "x" else set())
-    need = set(j for ws in waits for j in ws)
-    last = [i for i in range(n) if ops[i]["kind"] == "o" and i not in need]
+        waits[i] = ws
+        done[i] = set(kn) if ops[i]["kind"] != "x" else set()
+    need = set(j for i in order for j in waits[i])
+    last = [i for i in order if ops[i]["kind"] == "o" and i not in need]
     need.update(i for i in range(n) if ops[i]["kind"] in "do")
     queue = {"v": g.vector, "a": g.scalar, "p": g.tensor, "g": g, "s": g.sync}
     user, count, sig = {}, {}, {}
-    for i, o in enumerate(ops):
+    for i in order:
+        o, q = ops[i], way[i][0]
         if o["kind"] == "x":
             sig[i] = o["ext"]
             continue
-        for j in waits[i]:
-            queue[o["q"]].wait_ge(T.sem[sig[j][0]], sig[j][1])
-        ins = o["fn"]()
+        s = None
         if i in need:
             dma = o["kind"] in "do"
-            pool = o["q"] + "d" if dma else o["q"]
-            s = [pool + str(u) for u in range(POOLS[pool]) if user.get(pool + str(u), -1) in done[i] or pool + str(u) not in user][0]
+            pool = q + "d" if dma else q
+            names = [pool + str(u) for u in range(POOLS[pool])]
+            free = [u for u in names if u not in user or user[u] in done[i]]
+            s = free[0] if free else min(names, key=lambda u: start[user[u]])
+            if not free:
+                waits[i].append(user[s])
+        for j in waits[i]:
+            queue[q].wait_ge(T.sem[sig[j][0]], sig[j][1])
+        ins = way[i][1]()
+        if s is not None:
             user[s] = i
             count[s] = count.get(s, 0) + (16 if dma else 1)
             sig[i] = (s, count[s])
             ins.then_inc(T.sem[s], 16 if dma else 1)
     for i in last:
-        queue[ops[i]["q"]].wait_ge(T.sem[sig[i][0]], sig[i][1])
+        queue[way[i][0]].wait_ge(T.sem[sig[i][0]], sig[i][1])
     g.wait_ge(T.sem.sent, sent)

@@ -21,7 +21,7 @@ SCRATCH = {
     "pint": _s(8, I32), "bint": _s(8, I32), "bits": _s(8, F32), "r128": _s(128, BF), "oi": _s(16, I32),
     "land": _s(48, F32), "v": _s(768, F32), "pm": _s(600, F32), "qm": _s(576, F32), "yo": _s(256, F32),
     "pp": _s(256, F32), "hp": _s(256, F32), "wm": _s(256, BF),
-    "tf": _s(12288, F32), "tb": _s(16384, BF), "tu": _s(512, U16),
+    "tf": _s(16384, F32), "tb": _s(16384, BF), "tu": _s(512, U16),
 }
 POOLS = {"v": 56, "a": 44, "p": 10, "g": 8, "sd": 14, "ad": 8}
 SEMAPHORES = [q + str(i) for q in POOLS for i in range(POOLS[q])] + ["sent", "items"] + \
@@ -30,9 +30,10 @@ MAGIC = 12582912.0
 HELD = 2.0 ** 88
 TINY = 2.0 ** -120
 KEY, MID = 2048.0, 768.0
-CYC, WAKE, GATH, SCAT, FLY, ROWS, LOCAL = 0.00085, 0.2, 1.5, 3.5, 1.2, 0.9, 1.5
-OTHER = [(0.12, 1.0, 0.9), (0.2, 1.3, 1.2)]
-TRIES, MUT = 2000, 10
+CYC, WAKE, GATH, SCAT, FLY, ROWS, LOCAL = 0.00085, 0.2, 1.5, 3.8, 0.95, 1.0, 1.5
+OTHER = [(0.19, 1.0, 0.9, 0.75, 1.0), (0.22, 1.25, 1.2, 1.6, 1.3), (0.21, 1.3, 1.0, 0.9, 1.5)]
+TRIES, MUT, MOVES, HEAT = 3000, 10, 22000, 0.05
+KEPT = {}
 
 
 def rank_program(g, core, T, topo):
@@ -88,9 +89,8 @@ def rank_program(g, core, T, topo):
 
     def rec(alts, wr, rd, kind="c", ext=None):
         r = [z for x in rd if isinstance(x, tuple) for z in x[1]] + [z for x in wr for z in x[1][1:]]
-        w = [x[1][0] for x in wr]
-        w = w + [z for z in r if SCRATCH[z[0]][0] == "psum"]
-        ops.append({"alts": alts, "w": w, "r": r, "kind": kind, "ext": ext})
+        ops.append({"alts": alts, "w": [x[1][0] for x in wr], "r": r, "x": [z for z in r if SCRATCH[z[0]][0] == "psum"], "kind": kind, "ext": ext,
+                    "ind": any(isinstance(x, tuple) and x[3] == "i" for x in list(wr) + list(rd))})
         return len(ops) - 1
 
     def cost(o, i, mul=None, base=0.05):
@@ -119,8 +119,8 @@ def rank_program(g, core, T, topo):
             kw["accum_out"] = acc[0]
         return ("a", lambda: act.activation(o[0], i[0], f, **kw), cost(o, i, 1.0, 0.065) + (0.02 if acc is not None else 0))
 
-    def ts(o, i, s1, op0, s2=None, op1=None):
-        rec([vts(o, i, s1, op0, s2, op1)], [o], [i, s1, s2])
+    def ts(o, i, s1, op0, s2=None, op1=None, behind=None):
+        rec([vts(o, i, s1, op0, s2, op1)], [o], [i, s1, s2, behind])
 
     def ac(o, i, f, bias=None, scale=None, acc=None):
         rec([aac(o, i, f, bias, scale, acc)], [o] + ([acc] if acc is not None else []), [i, bias, scale])
@@ -134,8 +134,8 @@ def rank_program(g, core, T, topo):
     def times(o, i, c):
         rec([aac(o, i, F.Copy, None, c), vts(o, i, c, A.mult)], [o], [i])
 
-    def tt(o, a, b, op):
-        rec([("v", lambda: vec.tensor_tensor(o[0], a[0], b[0], op), cost(o, a, 1.0 if "p" in (a[3], b[3]) else 2.0))], [o], [a, b])
+    def tt(o, a, b, op, behind=None):
+        rec([("v", lambda: vec.tensor_tensor(o[0], a[0], b[0], op), cost(o, a, 1.0 if "p" in (a[3], b[3]) else 2.0))], [o], [a, b, behind])
 
     def cp(o, i):
         rec([("v", lambda: vec.tensor_copy(o[0], i[0]), cost(o, i))], [o], [i])
@@ -146,8 +146,8 @@ def rank_program(g, core, T, topo):
     def ms(o, c):
         rec([("v", lambda: vec.memset(o[0], c), cost(o, o))], [o], [])
 
-    def tr(o, i):
-        rec([("v", lambda: vec.transpose(o[0], i[0]), cost(o, i))], [o], [i])
+    def tr(o, i, behind=None):
+        rec([("v", lambda: vec.transpose(o[0], i[0]), cost(o, i))], [o], [i, behind])
 
     def total(o, i):
         j = tmp(i[2])()
@@ -167,16 +167,16 @@ def rank_program(g, core, T, topo):
         rec([("g", lambda: g.iota(o[0], pattern, base, cm, **kw), 0.13 + 2 * CYC * o[2])], [o], [])
 
     def load(o, src, behind=()):
-        rec([("s", lambda: g.sync.dma_start(o[0], src), 0.05)], [o], list(behind), kind="d")
+        rec([("s", lambda: g.sync.dma_start(o[0], src), 0.08)], [o], list(behind), kind="d", ext=o[2] / 800.0 - 0.6)
 
-    def store(q, dst, i):
+    def store(q, dst, i, more=0.0):
         e = g.sync if q == "s" else act
-        rec([(q, lambda: e.dma_start(dst, i[0]), 0.05)], [], [i], kind="o")
+        rec([(q, lambda: e.dma_start(dst, i[0]), 0.08)], [], [i], kind="o", ext=more)
 
     sent = [0]
 
     def send(s, d, sem):
-        trs = [RemoteDMATransfer(dst_ids=ids, dma_engine_mask=sum(1 << e for e in engs), remote_sem=T.sem[sem], srcs=[s[0]], dsts=[d[0] for r in peers])]
+        trs = [RemoteDMATransfer(dst_ids=ids, dma_engine_mask=sum(1 << e for e in engs), remote_sem=T.sem[sem], srcs=[s[0]], dsts=[d(r)[0] for r in peers])]
         sent[0] += len(engs)
         return rec([("g", lambda: g.remote_dma_fused(trs, local_sem=T.sem.sent), 0.3)], [], [s], kind="r")
 
@@ -204,25 +204,25 @@ def rank_program(g, core, T, topo):
     iota(row(), [[1, 96]], 0, 0)
     iota(V("r128"), [[1, 128]], 0, 0)
     iota(ep(), [[32, 3], [96, 4], [16, 2]], 0, 0)
-    iota(dup(), [[16, 3], [0, 2]], NI * me, 0)
-    iota(wc(), [[1, PW]], -128, 0)
     ms(V("ti", 192, 512), 0.0)
     ms(V("te"), 0.0)
     for j, (sh, m) in enumerate([(4, 1), (4, 1), (5, 1), (0, 15), (0, 31), (0, 127)]):
         ts(col("bint", j), col("pint", 0), sh, A.logical_shift_right, m, A.bitwise_and)
     cp(V("bits", 0, 6), V("bint", 0, 6))
-    h, hh, q0, s16, s32, pf = col("bits", 0), V("bits", 0, 2), col("bits", 2), col("bits", 3), col("bits", 4), col("bits", 5)
+    hh, q0, s16, s32, pf = V("bits", 0, 2), col("bits", 2), col("bits", 3), col("bits", 4), col("bits", 5)
     l_i, l_p, l_d, l_s = tmp(3, "tu"), tmp(24, "tu"), tmp(6, "tu"), tmp(8, "tu")
     ts(l_i(), row(0, 48, 16), s16, A.add)
     ts(l_p(), ep(), s16, A.add)
-    ts(l_d(), dup(), s16, A.add)
     for b in range(2):
         for f in range(2):
             ts(l_s(4 * f + 2 * b, 4 * f + 2 * b + 2), hh, 4.0, A.mult, float(8 * b + f), A.add)
     ts(V("te", 2, 514, 4), V("r128"), pf, A.is_equal)
     ts(V("te", 523, 1035, 4), V("r128"), pf, A.is_equal)
     quant(V("iq"), V("isc"), V("ti"))
-    first = [send(b8(V("iq", 0, NI)), b8(blk("pq", NI, me)), "items"), send(V("isc", 0, NI), blk("pz", NI, me), "items")]
+    first = [send(b8(V("iq", 0, NI)), lambda r: b8(blk("pq", NI, me)), "items"), send(V("isc", 0, NI), lambda r: blk("pz", NI, me), "items")]
+    iota(dup(), [[16, 3], [0, 2]], NI * me, 0)
+    iota(wc(), [[1, PW]], -128, 0)
+    ts(l_d(), dup(), s16, A.add)
     for b, a in enumerate([2, 522, 0, 520]):
         quant(blk("eq", 128, b), blk("es", 128, b), V("te", a, a + 512))
     pick(blk("pq", NI, me), blk("pz", NI, me), V("iq"), V("isc"), l_i())
@@ -233,27 +233,28 @@ def rank_program(g, core, T, topo):
         times(blk("hdx", NB, b), V("psD", 512 * b, 512 * b + NB), 0.5)
     neg, zero, one, four, low = const(192, -1e29), const(32, 0.0), const(32, 1.0), const(1, -4.0), const(1, -HELD / 8)
     up, down, lose, two = const(1, MAGIC), const(1, -MAGIC), const(1, -2.0 ** 17), const(2, -KEY)
-    mid, shift, far, minus = const(1, MID), const(1, 128.0), const(32, -HELD / 2), const(32, -1.0)
-    k, od0, od1, pat1, pat2, bm, rz, cb = tmp(48), tmp(32), tmp(32), tmp(32), tmp(32), tmp(256, "tb"), tmp(80), tmp(320, "tb")
+    mid, shift, far, minus, tiny = const(1, MID), const(1, 128.0), const(32, -HELD / 2), const(32, -1.0), const(1, TINY)
+    k, od3, od2, pat1, pat2, bm, rz, cb = tmp(48), tmp(128), tmp(128), tmp(32), tmp(32), tmp(256, "tb"), tmp(80), tmp(640, "tb")
     ts(col(k, 0), pf, s32, A.subtract, 3.0, A.mult)
     ts(col(k, 1), col(k, 0), s32, A.add, NB * me - MID, A.add)
     ts(k(4, 7), row(0, 96, 32), col(k, 1), A.add)
-    ts(od0(), row(0, 32), s32, A.is_lt, -2.0 ** -24, A.mult)
-    ts(od1(), od0(), 1.0, A.add)
+    ts(col(k, 13), s32, 32.0, A.add)
+    for b in range(2):
+        ts(blk(od3, 64, b), row(0, 64), col(k, 13) if b else s32, A.is_lt, -2.0 ** -24, A.mult)
+    ts(od2(), od3(), 1.0, A.add)
     ts(col(k, 8), q0, 1000.0, A.mult)
     ts(col(k, 9), q0, -1000.0, A.mult, 1000.0, A.add)
     for j in range(2):
         ts(blk(pat1, 16, j), row(0, 16), col(k, 8 + j), A.add)
-        ts(pat2(16 * j, 16 * j + NK), row(0, NK), s16, A.subtract)
+        cp2(pat2(16 * j, 16 * j + NK), row(0, NK))
         ms(pat2(16 * j + NK, 16 * j + 16), 999.0)
-    ts(col(k, 10), h, -1.0, A.mult, 1.0, A.add)
     ts(col(k, 11), s16, float(NK), A.is_lt)
     ts(k(16, 20), row(0, 64, 16), s16, A.add, 192.0, A.add)
-    ts(k(20, 24), k(16, 20), 1.0, A.add, col(k, 11), A.mult)
+    ts(col(k, 12), col(k, 11), -1000.0, A.mult, 999.0, A.add)
     ts(k(24, 28), row(0, 4), PW * KEY, A.mult, -KEY, A.add)
     for r in range(N):
         ts(bm(80 * r, 80 * r + 16), row(0, 16), s16, A.is_lt)
-    ms(cb(64, 320, 80), -64.0)
+    ms(cb(136, 640, 160), -1024.0 * (NM - 0.5))
     ms(rz(64, 80), 8192.0)
     ms(V("pm", 7, 600, 200), -1e29)
     ms(V("tn"), 0.0)
@@ -268,11 +269,12 @@ def rank_program(g, core, T, topo):
     ms(V("yo", 192, 256), 0.0)
     arrive("items", first, [blk(n, NI, r) for n in ("pq", "pz") for r in peers])
     decode(0, 192, 0)
+    turn = [(me + 1, N, 0), (0, me + 1, N - me - 1)] if me < N - 1 else [(0, me, 0), (me, N, me)]
 
     for t in range(NR):
         last = t == NR - 1
         oq, oz, L, O = "oq%d" % t, "oz%d" % t, 16 * t, 192 + 64 * t
-        g1, x1, r1, a3, kb, fe = tmp(3), tmp(96), tmp(96), tmp(3), tmp(3), tmp(6)
+        g1, x1, r1, a3, kb, fe = tmp(3), tmp(96), tmp(96), tmp(3), tmp(3), tmp(3)
         u, w, sign = (A.min, A.max, -1.0) if t else (A.max, A.min, 1.0)
         for kk in range(3):
             if t == 0:
@@ -290,7 +292,6 @@ def rank_program(g, core, T, topo):
             else:
                 ts(fw(), far(), top, A.subtract, top, A.max)
             ts(blk(x1, 32, kk), fw(), sec, A.subtract if t else A.add, -TINY, A.add)
-            axb(col(fe, 3 + kk), sec, sign, col(fw, 0))
             tr(blk(r1, 32, kk), blk(x1, 32, kk))
             count(col(g1, kk), V("pm", P - 1, P + 192), F.Sign, bias=top, scale=-1.0)
             axb(col(kb, kk), col(g1, kk), KEY * sign, col(k, 4 + kk))
@@ -298,18 +299,18 @@ def rank_program(g, core, T, topo):
                 times(V("v", 256 * kk, 256 * kk + 192), V("psS", 512 * kk, 512 * kk + 192), -1.0)
         for kk in range(3):
             ee, th, x = tmp(96, "tb"), tmp(32), col(x1, 32 * kk)
-            axb(th(), od1(), x, col(zero, 0))
+            axb(th(), od2(0, 32), x, col(zero, 0))
             tt(blk(ee, 32, kk), blk(r1, 32, kk), th(), A.is_lt)
             if kk > 0:
                 ts(ee(0, 32 * kk), r1(0, 32 * kk), x, A.is_le)
             if kk < 2:
                 ts(ee(32 * kk + 32, 96), r1(32 * kk + 32, 96), x, A.is_lt)
             total(col(a3, kk), ee())
-        c8, x2, kc, r2, c2 = tmp(2), tmp(64), tmp(2), tmp(64), tmp(2)
+        c8, x2, kc, r2, c2, xe = tmp(2), tmp(64), tmp(2), tmp(64), tmp(2), tmp(2)
         for f in range(2):
             m1, t1 = tmp(96), tmp(96)
             for kk in range(3):
-                ts(blk(m1, 32, kk), pat1(), col(a3, kk), A.is_equal, col(kb, kk) if f else col(fe, 3 + kk), A.mult)
+                ts(blk(m1, 32, kk), pat1(), col(a3, kk), A.is_equal, col(kb, kk) if f else col(x1, 32 * kk), A.mult)
             tr(t1(), m1())
             total(col(c8, f), t1())
         for b in range(2):
@@ -320,20 +321,20 @@ def rank_program(g, core, T, topo):
         cp2(kc(0, 2, 1, 32, 64), kc(0, 2, 1, 0, 32))
         cp2(kc(0, 2, 1, 64, 128), kc(0, 2, 1, 0, 64))
         tr(r2(), x2())
+        axb(xe(), x2(0, 64, 32), 1.0, tiny())
         for b in range(2):
-            ee, x = tmp(64, "tb"), col(x2, 32 * b)
-            ts(blk(ee, 32, 1 - b), blk(r2, 32, 1 - b), x, A.is_le if b else A.is_lt)
-            ts(blk(ee, 16, 2 * b), blk(r2, 16, 2 * b), x, A.is_le, h, A.mult)
-            ts(blk(ee, 16, 2 * b + 1), blk(r2, 16, 2 * b + 1), x, A.is_lt, col(k, 10), A.mult)
+            ee, th = tmp(64, "tb"), tmp(64)
+            axb(th(), blk(od2, 64, b), col(x2, 32 * b), col(zero, 0))
+            tt(ee(), r2(), th(), A.is_lt)
             total(col(c2, b), ee())
         for f in range(2):
             m2, t2 = tmp(64), tmp(64)
             for b in range(2):
-                ts(blk(m2, 32, b), pat2(), col(c2, b), A.is_equal, col(kc, b) if f else col(x2, 32 * b), A.mult)
+                ts(blk(m2, 32, b), pat2(), col(c2, b), A.is_equal, col(kc, b) if f else col(xe, b), A.mult)
             tr(t2(), m2())
             total(col("land", L + 4 * me + f), t2())
         mine, key = V("land", L + 4 * me, L + 4 * me + 4), col("land", L + 4 * me + 1)
-        bids = [send(mine, mine, "bids%d" % t)]
+        bids = [send(mine, lambda r: mine, "bids%d" % t)]
         if t == 0:
             ms(V("pm", 7, 600, 200), 1e29)
             load(V("tw"), T.w[:], [key])
@@ -358,25 +359,25 @@ def rank_program(g, core, T, topo):
             for b in range(4):
                 tt(V("tn", b, 64, 4), ind(blk("hdx", NB, b), xl()), blk("gv", 16, b), A.add)
         quant(V(oq), V(oz), V("tn"))
-        own = (O + 16 * me, O + 16 * me + 16)
-        cols = [send(b8(V(oq, 0, 16)), b8(V("pq", *own)), "cols%d" % t), send(V(oz, 0, 16), V("pz", *own), "cols%d" % t)]
-        pick(V("pq", *own), V("pz", *own), V(oq), V(oz), l_i(0, 1))
+        cols = [send(b8(V(oq, 0, 16)), lambda r: b8(blk("pq", 16, O // 16 + (me - r - 1) % N)), "cols%d" % t),
+                send(V(oz, 0, 16), lambda r: blk("pz", 16, O // 16 + (me - r - 1) % N), "cols%d" % t)]
+        pick(V("pq", O + 48, O + 64), V("pz", O + 48, O + 64), V(oq), V(oz), l_i(0, 1))
         vo = [tmp(64) for kk in range(3)]
         if not last:
             xo, ro, po = tmp(64), tmp(64), tmp(16)
             for f in range(2):
                 axb(blk(xo, 32, f), zero(), 1.0, col("land", L + 4 * me + f))
-            tr(ro(), xo())
+            tr(ro(), xo(), V("tn", 0, 64))
             tt(po(), ind(V("pp"), gl(0, 1)), ro(0, 16), A.subtract)
             for kk in range(3):
                 e, pk = tmp(16), tmp(16)
                 ts(e(), ro(32, 48), col(kb, kk), A.is_equal, HELD, A.mult)
                 tt(pk(), po(), e(), A.subtract)
                 mm(V("psS", 512 * kk, 512 * kk + 128), blk("xpq", 128, kk), blk("xps", 128, kk), V(oq), V(oz))
-                tt(blk(vo[kk], 16, me), pk(), V("psS", 512 * kk, 512 * kk + 16), A.subtract)
+                tt(blk(vo[kk], 16, 3), pk(), V("psS", 512 * kk, 512 * kk + 16), A.subtract)
         arrive("bids%d" % t, bids, [V("land", L + 4 * r, L + 4 * r + 4) for r in peers])
         lw, keys = V("land", L, L + 16), V("land", L + 1, L + 16, 4)
-        xs, rs, sm, gs, pr, nn = tmp(128), tmp(128), tmp(64), tmp(4, "tu"), tmp(64), tmp(16)
+        xs, rs, sm, pr, nn = tmp(128), tmp(128), tmp(64), tmp(64), tmp(16)
         for f in range(2):
             cp2(blk(xs, 64, f), ind(lw, blk(l_s, 4, f)))
             tr(blk(rs, 64, f), blk(xs, 64, f))
@@ -386,9 +387,11 @@ def rank_program(g, core, T, topo):
         ts(sm(8, 12), blk("oi", 4, t), 256.0, A.mult)
         axb(sm(12, 16), sm(4, 8), 2.0 ** -8, shift())
         tt(sm(16, 20), sm(12, 16), sm(8, 12), A.add)
-        tt(sm(20, 24), sm(4, 8), k(20, 24), A.subtract)
-        ts(gs(), keys, 1 / KEY, A.mult, -1.0, A.add)
-        tt(pr(), ind(V("pp"), gs()), blk(rs, 64, 0), A.subtract)
+        axb(sm(20, 24), sm(4, 8), 1.0, col(k, 12))
+        for a, b, c in turn:
+            gs = tmp(b - a, "tu")
+            ts(gs(), V("land", L + 4 * a + 1, L + 4 * b, 4), 1 / KEY, A.mult, -1.0, A.add, keys)
+            tt(pr(16 * c, 16 * (c + b - a)), ind(V("pp"), gs()), rs(16 * a, 16 * b), A.subtract)
         for r in range(N):
             nb, pen, z = col("land", L + 4 * r), tmp(64, "tb"), tmp(64, "tb")
             if r > 0:
@@ -406,19 +409,22 @@ def rank_program(g, core, T, topo):
         tt(xz(), ind(nn(0, 13), blk(l_s, 4, 0)), sw(), A.add)
         tr(rz(0, 64), xz())
         for r in range(N):
-            count(col(sm, 48 + r), rz(), F.Sign, bias=col(kw, 4 * r), scale=-1.0)
-            ts(cb(80 * r, 80 * r + 64), rz(0, 64), col(sm, 8 + r), A.is_lt, 2.0, A.mult)
-            total(col(sm, 52 + r), cb(80 * r, 80 * r + 65))
-            ts(col(sm, 56 + r), col(sm, 48 + r), col(sm, 52 + r), A.is_lt, col(sm, 20 + r), A.mult)
-        tt(of(), sm(56, 60), k(16, 20), A.add)
-        arrive("cols%d" % t, cols, [V(n, O + 16 * r, O + 16 * r + 16) for r in peers for n in ("pq", "pz")])
+            if r < 2:
+                count(col(sm, 56 + r), rz(0, 64), F.Sign, bias=col(sm, 8 + r), scale=-1.0)
+                count(col(sm, 48 + r), rz(), F.Sign, bias=col(kw, 4 * r), scale=-1.0)
+                ts(col(sm, 52 + r), col(sm, 48 + r), col(sm, 56 + r), A.subtract, 512.0, A.mult)
+            else:
+                ts(cb(160 * r, 160 * r + 64), rz(0, 64), col(sm, 8 + r), A.is_lt, -1024.0, A.mult)
+                ts(cb(160 * r + 64, 160 * r + 136), rz(0, 72), col(kw, 4 * r), A.is_lt, 1024.0, A.mult)
+                total(col(sm, 52 + r), cb(160 * r, 160 * r + 137))
+            c = (r - me - 1) % N
+            ts(col(of, c), col(sm, 52 + r), col(sm, 20 + r), A.max, col(k, 16 + r), A.min)
+        arrive("cols%d" % t, cols, [V(n, O, O + 48) for n in ("pq", "pz")])
         new = (V("pq", O - 64, O + 64), V("pz", O - 64, O + 64))
         if not last:
             for kk in range(3):
                 mm(V("psS", 512 * kk, 512 * kk + 128), blk("xpq", 128, kk), blk("xps", 128, kk), *new)
-                for a, b in ((0, 16 * me), (16 * me + 16, 64)):
-                    if a < b:
-                        tt(vo[kk](a, b), pr(a, b), V("psS", 512 * kk + 64 + a, 512 * kk + 64 + b), A.subtract)
+                tt(vo[kk](0, 48), pr(0, 48), V("psS", 512 * kk + 64, 512 * kk + 112), A.subtract, pr())
                 cp(ind(blk("v", 256, kk), of()), vo[kk]())
             decode(O - 64, 128, 64)
         cp(ind(V("wm"), of()), wc(O, O + 64))
@@ -429,21 +435,22 @@ def rank_program(g, core, T, topo):
         axb(blk(hr, 64, 0), blk(rs, 64, 1), 1 / KEY, up())
         axb(blk(hr, 64, 1), blk(hr, 64, 0), 1.0, down())
         axb(blk(hr, 64, 2), blk(hr, 64, 1), -KEY, mid())
-        tt(blk(hr, 64, 3), blk(hr, 64, 2), blk(rs, 64, 1), A.add)
+        for a, b, c in turn:
+            tt(hr(192 + 16 * c, 192 + 16 * (c + b - a)), hr(128 + 16 * a, 128 + 16 * b), rs(64 + 16 * a, 64 + 16 * b), A.add)
         cp(ind(V("pp"), of()), pr())
         cp(ind(V("hp"), of()), blk(hr, 64, 3))
-        store("a" if last else "s", T.pr[t:t + 1, :], V("pp", NI * me, NI * me + NI, 1, 0, 1))
+        store("a", T.pr[t:t + 1, :], V("pp", NI * me, NI * me + NI, 1, 0, 1))
         store("a" if last else "s", T.ho[t:t + 1, :], V("hp", NI * me, NI * me + NI, 1, 0, 1))
 
-    store("s", T.y[:], V("yo", 0, 192))
+    store("s", T.y[:], V("yo", 0, 192), 0.5)
     wd, tm, lst = tmp(96, "tb"), tmp(96, "tb"), tmp(3, "tu")
     cp2(wd(), ind(V("wm"), l_d()))
     tr(tm(), wd())
     ts(lst(), tm(0, 96, 32), 128.0, A.add)
     pick(V("nq"), V("nz"), V("pq"), V("pz"), lst())
-    store("s", T.oc[:], b8(V("nq")))
+    store("s", T.oc[:], b8(V("nq")), 0.3)
     for u in range(4):
-        store("s" if u < 2 else "a", T.osc[4 * u:4 * u + 4, :], V("nz", 0, NI, 1, 32 * u, 32 * u + 4))
+        store("s" if u < 1 else "a", T.osc[4 * u:4 * u + 4, :], V("nz", 0, NI, 1, 32 * u, 32 * u + 4))
 
     emit(g, T, ops, sent[0])
 
@@ -462,6 +469,9 @@ def emit(g, T, ops, sent):
                 d.update(j for j, y, w in hist.get(z[0], []) if w and clash(z, y))
             for z in o["w"]:
                 d.update(j for j, y, w in hist.get(z[0], []) if clash(z, y) and ops[j]["kind"] != "r")
+            for z in o["x"]:
+                d.update(j for j, y, w in hist.get(z[0], []) if clash(z, y)
+                         and not (len(o["alts"]) == len(ops[j]["alts"]) == 1 and o["alts"][0][0] == ops[j]["alts"][0][0]))
         for z in o["r"]:
             hist.setdefault(z[0], []).append((i, z, False))
         for z in o["w"]:
@@ -472,9 +482,52 @@ def emit(g, T, ops, sent):
     after = [set(deps[i]) | set(ops[i]["ext"][2] if ops[i]["kind"] == "x" else []) for i in range(n)]
     for a, b in zip(sends, sends[1:]):
         after[b].add(a)
-    tail = [LOCAL if o["kind"] in "do" else 0.0 for o in ops]
-    aft = [sorted(x) for x in after]
+    for i in range(n):
+        if ops[i]["alts"][0][0] == "g" and ops[i]["kind"] == "c":
+            if i < sends[0]:
+                after[sends[0]].add(i)
+            else:
+                after[i].add(sends[1])
+    tail = [LOCAL + o["ext"] if o["kind"] in "do" else 0.0 for o in ops]
+    below, aft, nxt = [], [], [[] for i in range(n)]
+    for i in range(n):
+        m = 0
+        for j in after[i]:
+            m |= below[j]
+        aft.append(sorted(j for j in after[i] if not m >> j & 1))
+        for j in after[i]:
+            m |= 1 << j
+        below.append(m)
+        for j in aft[i]:
+            nxt[j].append(i)
     span = [min(a[2] for a in ops[i]["alts"]) + tail[i] + WAKE for i in range(n)]
+    listed = [o["ind"] for o in ops]
+
+    def play(order, way):
+        score, pairs = 0.0, []
+        for wake, slow, fly, rows, jump in OTHER + [(WAKE, 1.0, FLY, ROWS, 1.0)]:
+            free, fin, why = {}, [0.0] * n, [-1] * n
+            for i in order:
+                q, s, c = way[i][0], 0.0, -1
+                for j in aft[i]:
+                    if fin[j] + wake > s:
+                        s, c = fin[j] + wake, j
+                if q:
+                    f = free.get(q)
+                    if f and f[0] > s:
+                        s, c = f
+                    e = s + way[i][2] * slow * (jump if listed[i] else 1.0)
+                    free[q] = (e, i)
+                else:
+                    e = s + fly + rows * len(ops[i]["ext"][2])
+                fin[i], why[i] = e + tail[i], c
+            i = max(range(n), key=lambda i: fin[i])
+            score += fin[i]
+            while why[i] >= 0:
+                if why[i] not in aft[i]:
+                    pairs.append((why[i], i))
+                i = why[i]
+        return score, pairs, fin
 
     def plan(fac, lean):
         rank = [0.0] * n
@@ -505,18 +558,7 @@ def emit(g, T, ops, sent):
             if way[i][0] is not None:
                 busy[way[i][0]].insert(best[3], (start[i], start[i] + way[i][2]))
         order = sorted(range(n), key=lambda i: (start[i], i))
-        score = max(end)
-        for wake, slow, fly in OTHER:
-            free, fin = {}, [0.0] * n
-            for i in order:
-                q = way[i][0]
-                s = max([fin[j] + wake for j in aft[i]] + [free.get(q, 0.0)])
-                c = way[i][2] * (slow if q else fly)
-                if q:
-                    free[q] = s + c
-                fin[i] = s + c + tail[i]
-            score += max(fin)
-        return score, start, end, way
+        return play(order, way)[0], order, way
 
     seed = [1]
 
@@ -524,20 +566,57 @@ def emit(g, T, ops, sent):
         seed[0] = (seed[0] * 1103515245 + 12345) % 2147483648
         return seed[0] / 2147483648.0
 
-    fac, lean = [1.0] * n, [0.0] * n
-    held = plan(fac, lean)
-    for trial in range(TRIES):
-        f2, l2 = list(fac), list(lean)
-        a = int(draw() * n)
-        for u in range(MUT):
-            i = min(n - 1, a + int(draw() * 60))
-            f2[i] = 0.2 + 2.8 * draw() ** 2
-            l2[i] = 0.4 * draw() - 0.2
-        new = plan(f2, l2)
-        if new[0] <= held[0]:
-            held, fac, lean = new, f2, l2
-    start, end, way = held[1:]
-    order = sorted(range(n), key=lambda i: (start[i], i))
+    shape = tuple(map(tuple, aft))
+    if shape not in KEPT:
+        fac, lean = [1.0] * n, [0.0] * n
+        held = plan(fac, lean)
+        for trial in range(TRIES):
+            f2, l2 = list(fac), list(lean)
+            a = int(draw() * n)
+            for u in range(MUT):
+                i = min(n - 1, a + int(draw() * 60))
+                f2[i] = 0.2 + 2.8 * draw() ** 2
+                l2[i] = 0.4 * draw() - 0.2
+            new = plan(f2, l2)
+            if new[0] <= held[0]:
+                held, fac, lean = new, f2, l2
+        best = held
+        order, way = held[1:]
+        now = play(order, way)
+        for trial in range(MOVES):
+            j, i = now[1][int(draw() * len(now[1]))]
+            o2, w2, kind = list(order), way, draw()
+            a, b = order.index(j), order.index(i)
+            if kind < 0.2:
+                c = i if draw() < 0.5 else j
+                if len(ops[c]["alts"]) < 2:
+                    continue
+                w2 = list(way)
+                w2[c] = ops[c]["alts"][1] if way[c] is ops[c]["alts"][0] else ops[c]["alts"][0]
+            elif kind < 0.6:
+                a = max(0, a - int(draw() ** 3 * 12))
+                take = set([i])
+                for u in reversed(order[a:b]):
+                    if any(x in take for x in nxt[u]):
+                        take.add(u)
+                o2[a:b + 1] = [u for u in order[a:b + 1] if u in take] + [u for u in order[a:b + 1] if u not in take]
+            else:
+                b = min(n - 1, b + int(draw() ** 3 * 30))
+                take = set([j])
+                for u in order[a + 1:b + 1]:
+                    if any(x in take for x in aft[u]):
+                        take.add(u)
+                o2[a:b + 1] = [u for u in order[a:b + 1] if u not in take] + [u for u in order[a:b + 1] if u in take]
+            new = play(o2, w2)
+            if new[0] <= now[0] + HEAT * (1 - trial / MOVES) * draw():
+                now, order, way = new, o2, w2
+                if now[0] < best[0]:
+                    best = (now[0], order, way)
+        KEPT[shape] = (best[1], [0 if best[2][i] is ops[i]["alts"][0] else 1 for i in range(n)], best[0])
+    order = KEPT[shape][0]
+    way = [ops[i]["alts"][KEPT[shape][1][i]] for i in range(n)]
+    end = play(order, way)[2]
+    place = dict((i, c) for c, i in enumerate(order))
     known, waits, done = {}, {}, {}
     for i in order:
         kn = known.setdefault(way[i][0], set())
@@ -565,7 +644,7 @@ def emit(g, T, ops, sent):
             pool = q + "d" if dma else q
             names = [pool + str(u) for u in range(POOLS[pool])]
             free = [u for u in names if u not in user or user[u] in done[i]]
-            s = free[0] if free else min(names, key=lambda u: start[user[u]])
+            s = free[0] if free else min(names, key=lambda u: place[user[u]])
             if not free:
                 waits[i].append(user[s])
         for j in waits[i]:

@@ -20,19 +20,19 @@ SCRATCH = {
     "psS": ("psum", [128, 1536], F32), "psD": ("psum", [128, 2048], F32), "psY": ("psum", [128, 512], F32),
     "pint": _s(8, I32), "bint": _s(8, I32), "bits": _s(8, F32), "r128": _s(128, BF), "oi": _s(16, I32),
     "land": _s(48, F32), "v": _s(768, F32), "pm": _s(600, F32), "qm": _s(576, F32), "yo": _s(256, F32),
-    "pp": _s(256, F32), "hp": _s(256, F32), "wm": _s(256, BF),
+    "pp": _s(256, F32), "hp": _s(256, F32), "wm": _s(272, BF), "fin": _s(272, F32),
     "tf": _s(16384, F32), "tb": _s(16384, BF), "tu": _s(512, U16),
 }
 POOLS = {"v": 56, "a": 44, "p": 10, "g": 8, "sd": 14, "ad": 8}
 SEMAPHORES = [q + str(i) for q in POOLS for i in range(POOLS[q])] + ["sent", "items"] + \
     ["bids%d" % t for t in range(NR)] + ["cols%d" % t for t in range(NR)]
-MAGIC = 12582912.0
 HELD = 2.0 ** 88
 TINY = 2.0 ** -120
-KEY, MID = 2048.0, 768.0
+KEY, MID = 8192.0, 768.0
 CYC, WAKE, GATH, SCAT, FLY, ROWS, LOCAL = 0.00085, 0.2, 1.5, 3.8, 0.95, 1.0, 1.5
 OTHER = [(0.19, 1.0, 0.9, 0.75, 1.0), (0.22, 1.25, 1.2, 1.6, 1.3), (0.21, 1.3, 1.0, 0.9, 1.5)]
-TRIES, MUT, MOVES, HEAT = 3000, 10, 22000, 0.05
+TRIES, MUT, MOVES, HEAT = 600, 10, 60000, 0.1
+NA = 1
 KEPT = {}
 
 
@@ -132,13 +132,13 @@ def rank_program(g, core, T, topo):
         rec([aac(o, i, F.Identity, b, a), vts(o, i, a, A.mult, b, A.add)], [o], [i, a, b])
 
     def times(o, i, c):
-        rec([aac(o, i, F.Copy, None, c), vts(o, i, c, A.mult)], [o], [i])
+        rec([aac(o, i, F.Copy, None, c), vts(o, i, c, A.mult)], [o], [i, c])
 
     def tt(o, a, b, op, behind=None):
         rec([("v", lambda: vec.tensor_tensor(o[0], a[0], b[0], op), cost(o, a, 1.0 if "p" in (a[3], b[3]) else 2.0))], [o], [a, b, behind])
 
-    def cp(o, i):
-        rec([("v", lambda: vec.tensor_copy(o[0], i[0]), cost(o, i))], [o], [i])
+    def cp(o, i, behind=None):
+        rec([("v", lambda: vec.tensor_copy(o[0], i[0]), cost(o, i))], [o], [i, behind])
 
     def cp2(o, i):
         rec([aac(o, i, F.Copy), ("v", lambda: vec.tensor_copy(o[0], i[0]), cost(o, i))], [o], [i])
@@ -155,6 +155,11 @@ def rank_program(g, core, T, topo):
 
     def scan(o, a, b, op0, op1, init):
         rec([("v", lambda: vec.tensor_tensor_scan(o[0], a[0], b[0], init, op0, op1), cost(o, a))], [o], [a, b])
+
+    def fold(w, a, n, pool):
+        o = tmp(n, pool)
+        scan(o(), w(a, a + n), w(a + n, a + 2 * n), A.add, A.add, 0.0)
+        return col(o, n - 1)
 
     def quant(q, s, i):
         rec([("v", lambda: vec.quantize_mx(q[0], s[0], i[0]), 0.012 + 0.00022 * i[2])], [q, s], [i])
@@ -199,30 +204,41 @@ def rank_program(g, core, T, topo):
 
     load(V("ti", 0, 192), T.it[:])
     load(V("tx"), T.x[:])
-    row, ep, dup, wc = tmp(96), tmp(24), tmp(6), tmp(PW, "tb")
+    row, ep, hk, wc, ki = tmp(64), tmp(24), tmp(NI), tmp(PW + 16, "tb"), tmp(16)
+    k, od3, od2, pat, rz, cb = tmp(48), tmp(32), tmp(33), tmp(32), tmp(80), tmp(640, "tb")
     iota(col("pint", 0), [[0, 1]], 0, 1)
-    iota(row(), [[1, 96]], 0, 0)
-    iota(V("r128"), [[1, 128]], 0, 0)
-    iota(ep(), [[32, 3], [96, 4], [16, 2]], 0, 0)
+    iota(row(), [[1, 64]], 0, 0)
+    for kk in range(3):
+        iota(blk(ep, 8, kk), [[96, 2], [192, 2], [16, 2]], 32 * kk, 0)
+    iota(ki(0, 8), [[1, 2], [8, 2], [0, 2]], 0, 0)
     ms(V("ti", 192, 512), 0.0)
-    ms(V("te"), 0.0)
-    for j, (sh, m) in enumerate([(4, 1), (4, 1), (5, 1), (0, 15), (0, 31), (0, 127)]):
+    for j, (sh, m) in enumerate([(4, 1), (5, 1), (0, 15), (0, 31), (6, 1)]):
         ts(col("bint", j), col("pint", 0), sh, A.logical_shift_right, m, A.bitwise_and)
-    cp(V("bits", 0, 6), V("bint", 0, 6))
-    hh, q0, s16, s32, pf = V("bits", 0, 2), col("bits", 2), col("bits", 3), col("bits", 4), col("bits", 5)
-    l_i, l_p, l_d, l_s = tmp(3, "tu"), tmp(24, "tu"), tmp(6, "tu"), tmp(8, "tu")
+    cp(V("bits", 0, 5), V("bint", 0, 5))
+    hh, q0, s16, s32, q1 = [col("bits", j) for j in range(5)]
+    l_i, l_p, l_h, l_s = tmp(3, "tu"), tmp(24, "tu"), tmp(1, "tu"), tmp(8, "tu")
     ts(l_i(), row(0, 48, 16), s16, A.add)
     ts(l_p(), ep(), s16, A.add)
-    for b in range(2):
-        for f in range(2):
-            ts(l_s(4 * f + 2 * b, 4 * f + 2 * b + 2), hh, 4.0, A.mult, float(8 * b + f), A.add)
-    ts(V("te", 2, 514, 4), V("r128"), pf, A.is_equal)
-    ts(V("te", 523, 1035, 4), V("r128"), pf, A.is_equal)
+    times(col(k, 2), hh, 4.0)
+    ts(l_s(), ki(0, 8), col(k, 2), A.add)
     quant(V("iq"), V("isc"), V("ti"))
     first = [send(b8(V("iq", 0, NI)), lambda r: b8(blk("pq", NI, me)), "items"), send(V("isc", 0, NI), lambda r: blk("pz", NI, me), "items")]
-    iota(dup(), [[16, 3], [0, 2]], NI * me, 0)
-    iota(wc(), [[1, PW]], -128, 0)
-    ts(l_d(), dup(), s16, A.add)
+    iota(V("r128"), [[1, 128]], 0, -1)
+    ms(V("te"), 0.0)
+    ts(V("te", 2, 514, 4), V("r128"), 0.0, A.is_equal)
+    ts(V("te", 523, 1035, 4), V("r128"), 0.0, A.is_equal)
+    iota(wc(), [[1, PW + 16]], -144, 0)
+    iota(V("hp", 0, 192), [[int(KEY), 192]], int(KEY - MID - 1), 0)
+    iota(hk(), [[int(KEY), NI]], int(KEY * (NI * me + 1) - MID), 0)
+    iota(ki(8, 11), [[32, 3]], int(NB * me - MID), 0)
+    iota(ki(12, 16), [[16, 4]], 192, 0)
+    iota(V("tn", 64, 512), [[0, 448]], 0, 0)
+    iota(V("pp", 0, 192), [[0, 192]], 0, 0)
+    iota(rz(64, 80), [[0, 16]], 8192, 0)
+    for r in range(2, N):
+        iota(cb(160 * r + 136, 160 * r + 138), [[1024 * NM - 512, 2]], 512 - 1024 * NM, 0)
+    for t in range(NR):
+        iota(V("land", 16 * t + 14, 16 * t + 16), [[0, 2]], 0, 0)
     for b, a in enumerate([2, 522, 0, 520]):
         quant(blk("eq", 128, b), blk("es", 128, b), V("te", a, a + 512))
     pick(blk("pq", NI, me), blk("pz", NI, me), V("iq"), V("isc"), l_i())
@@ -231,50 +247,41 @@ def rank_program(g, core, T, topo):
     for b in range(4):
         mm(V("psD", 512 * b, 512 * b + NB), blk("eq", 128, b), blk("es", 128, b), V("xq"), V("xs"))
         times(blk("hdx", NB, b), V("psD", 512 * b, 512 * b + NB), 0.5)
-    neg, zero, one, four, low = const(192, -1e29), const(32, 0.0), const(32, 1.0), const(1, -4.0), const(1, -HELD / 8)
-    up, down, lose, two = const(1, MAGIC), const(1, -MAGIC), const(1, -2.0 ** 17), const(2, -KEY)
-    mid, shift, far, minus, tiny = const(1, MID), const(1, 128.0), const(32, -HELD / 2), const(32, -1.0), const(1, TINY)
-    k, od3, od2, pat1, pat2, bm, rz, cb = tmp(48), tmp(128), tmp(128), tmp(32), tmp(32), tmp(256, "tb"), tmp(80), tmp(640, "tb")
-    ts(col(k, 0), pf, s32, A.subtract, 3.0, A.mult)
-    ts(col(k, 1), col(k, 0), s32, A.add, NB * me - MID, A.add)
-    ts(k(4, 7), row(0, 96, 32), col(k, 1), A.add)
-    ts(col(k, 13), s32, 32.0, A.add)
-    for b in range(2):
-        ts(blk(od3, 64, b), row(0, 64), col(k, 13) if b else s32, A.is_lt, -2.0 ** -24, A.mult)
-    ts(od2(), od3(), 1.0, A.add)
-    ts(col(k, 8), q0, 1000.0, A.mult)
-    ts(col(k, 9), q0, -1000.0, A.mult, 1000.0, A.add)
+    neg, one, two, far, minus = tmp(192), tmp(32), tmp(2), tmp(32), tmp(32)
+    axb(neg(), V("ti", 0, 192), 0.0, -1e29)
+    for w, c in ((one, 1.0), (two, -KEY), (far, -HELD / 2), (minus, -1.0), (pat, 999.0)):
+        axb(w(), row(0, w()[2]), 0.0, c)
+    axb(col(k, 0), q0, 192.0, s32)
+    axb(col(k, 1), q1, 96.0, col(k, 0))
+    axb(k(4, 7), ki(8, 11), 1.0, col(k, 1))
+    ts(od3(), row(0, 32), s32, A.is_lt, -2.0 ** -24, A.mult)
+    axb(od2(0, 32), od3(), 1.0, 1.0)
+    axb(col(od2, 32), q1, -2.0 ** -24, 1.0)
+    axb(col(k, 8), q0, -2.0, 1.0)
+    times(col(k, 9), q0, NK - 1.0)
     for j in range(2):
-        ts(blk(pat1, 16, j), row(0, 16), col(k, 8 + j), A.add)
-        cp2(pat2(16 * j, 16 * j + NK), row(0, NK))
-        ms(pat2(16 * j + NK, 16 * j + 16), 999.0)
+        axb(pat(16 * j, 16 * j + NK), row(0, NK), col(k, 8), col(k, 9))
     ts(col(k, 11), s16, float(NK), A.is_lt)
-    ts(k(16, 20), row(0, 64, 16), s16, A.add, 192.0, A.add)
-    ts(col(k, 12), col(k, 11), -1000.0, A.mult, 999.0, A.add)
-    ts(k(24, 28), row(0, 4), PW * KEY, A.mult, -KEY, A.add)
-    for r in range(N):
-        ts(bm(80 * r, 80 * r + 16), row(0, 16), s16, A.is_lt)
-    ms(cb(136, 640, 160), -1024.0 * (NM - 0.5))
-    ms(rz(64, 80), 8192.0)
+    axb(k(16, 20), ki(12, 16), 1.0, s16)
+    axb(col(k, 12), col(k, 11), -1000.0, 999.0)
+    wl = tmp(64)
+    axb(col(k, 32), hh, -1.0, 1.0)
+    times(wl(), wc(PW - 48, PW + 16), col(k, 32))
+    ts(col(k, 33), s16, col(k, 32), A.add, 3.0, A.min)
+    times(col(k, 34), col(k, 33), 64.0)
+    ts(col(k, 35), col(k, 33), 2.0, A.is_ge, -96.0, A.mult)
+    ts(l_h(), col(k, 34), col(k, 35), A.add)
+    axb(k(24, 28), row(0, 4), PW * KEY, -KEY)
     ms(V("pm", 7, 600, 200), -1e29)
-    ms(V("tn"), 0.0)
-    ms(V("hdv"), 0.0)
-    ms(V("land", 4 * me + 2, 48, 16), 0.0)
-    ms(V("land", 4 * me + 3, 48, 16), 0.0)
-    ms(V("pp"), 0.0)
-    ms(V("hp"), -1.0)
-    cp2(V("wm"), wc(0, 256))
-    for kk in range(3):
-        ms(V("v", 256 * kk + 192, 256 * kk + 256), 0.0)
-    ms(V("yo", 192, 256), 0.0)
+    ms(V("hdv", PW - 1, 4 * PW, PW), 0.0)
+    cp2(V("wm"), wc(0, 272))
     arrive("items", first, [blk(n, NI, r) for n in ("pq", "pz") for r in peers])
     decode(0, 192, 0)
-    turn = [(me + 1, N, 0), (0, me + 1, N - me - 1)] if me < N - 1 else [(0, me, 0), (me, N, me)]
 
     for t in range(NR):
         last = t == NR - 1
         oq, oz, L, O = "oq%d" % t, "oz%d" % t, 16 * t, 192 + 64 * t
-        g1, x1, r1, a3, kb, fe = tmp(3), tmp(96), tmp(96), tmp(3), tmp(3), tmp(3)
+        g1, x1, r1, a3, kb, fe = tmp(3), tmp(96), tmp(192), tmp(3), tmp(3), tmp(3)
         u, w, sign = (A.min, A.max, -1.0) if t else (A.max, A.min, 1.0)
         for kk in range(3):
             if t == 0:
@@ -285,56 +292,51 @@ def rank_program(g, core, T, topo):
             scan(V("pm", P, P + 192), V(o[0], o[1], o[1] + 192), V(o[0], o[1], o[1] + 192) if t else neg(), u, u, -1e29 * sign)
             scan(V("qm", 192 * kk, 192 * kk + 191), V(o[0], o[1] + 1, o[1] + 192), V("pm", P, P + 191), u, w, -1e29 * sign)
             if t == 0:
-                axb(fw(), minus(), top, col(zero, 0))
+                times(fw(), minus(), top)
             elif kk < 2:
-                ac(col(fe, kk), four(), F.Relu, bias=low(), scale=top)
+                ac(col(fe, kk), top, F.Relu, -HELD / 8, -4.0)
                 axb(fw(), one(), top, col(fe, kk))
             else:
                 ts(fw(), far(), top, A.subtract, top, A.max)
             ts(blk(x1, 32, kk), fw(), sec, A.subtract if t else A.add, -TINY, A.add)
-            tr(blk(r1, 32, kk), blk(x1, 32, kk))
             count(col(g1, kk), V("pm", P - 1, P + 192), F.Sign, bias=top, scale=-1.0)
             axb(col(kb, kk), col(g1, kk), KEY * sign, col(k, 4 + kk))
             if t == 0:
                 times(V("v", 256 * kk, 256 * kk + 192), V("psS", 512 * kk, 512 * kk + 192), -1.0)
+        an = []
+        tr(r1(0, 96), x1())
+        tr(r1(96, 192, 1, 0, 64), x1(0, 96, 1, 64, 128))
+        tr(r1(96, 192, 1, 64, 128), x1(0, 96, 1, 0, 64))
         for kk in range(3):
-            ee, th, x = tmp(96, "tb"), tmp(32), col(x1, 32 * kk)
-            axb(th(), od2(0, 32), x, col(zero, 0))
-            tt(blk(ee, 32, kk), blk(r1, 32, kk), th(), A.is_lt)
+            ee, th, x = tmp(192, "tb"), tmp(33), col(x1, 32 * kk)
+            times(th(), od2(), x)
+            tt(blk(ee, 32, kk), blk(r1, 32, kk), th(0, 32), A.is_lt)
             if kk > 0:
                 ts(ee(0, 32 * kk), r1(0, 32 * kk), x, A.is_le)
             if kk < 2:
                 ts(ee(32 * kk + 32, 96), r1(32 * kk + 32, 96), x, A.is_lt)
-            total(col(a3, kk), ee())
-        c8, x2, kc, r2, c2, xe = tmp(2), tmp(64), tmp(2), tmp(64), tmp(2), tmp(2)
+            if kk < NA:
+                ac(ee(96, 192), r1(96, 192), F.Sign, col(th, 32), -1.0)
+                count(col(a3, kk), ee(), F.Relu)
+                an.append(col(a3, kk))
+            else:
+                ts(ee(96, 192), r1(96, 192), col(th, 32), A.is_lt)
+                an.append(fold(ee, 0, 96, "tf"))
+        cs, uw = tmp(192), tmp(2)
         for f in range(2):
             m1, t1 = tmp(96), tmp(96)
             for kk in range(3):
-                ts(blk(m1, 32, kk), pat1(), col(a3, kk), A.is_equal, col(kb, kk) if f else col(x1, 32 * kk), A.mult)
+                ts(blk(m1, 32, kk), pat(), an[kk], A.is_equal, col(kb, kk) if f else col(x1, 32 * kk), A.mult)
             tr(t1(), m1())
-            total(col(c8, f), t1())
-        for b in range(2):
-            for q in range(4):
-                axb(x2(32 * b, 32 * b + 32, 1, 32 * q, 32 * q + 32), one(0, 32, 1, 32 * q, 32 * q + 32),
-                    col(c8, 0, 64 * b, 64 * b + 32), col(c8, 0, 64 * b + 32, 64 * b + 64))
-            axb(col(kc, b, 0, 32), col(c8, 1, 64 * b, 64 * b + 32), 1.0, col(c8, 1, 64 * b + 32, 64 * b + 64))
-        cp2(kc(0, 2, 1, 32, 64), kc(0, 2, 1, 0, 32))
-        cp2(kc(0, 2, 1, 64, 128), kc(0, 2, 1, 0, 64))
-        tr(r2(), x2())
-        axb(xe(), x2(0, 64, 32), 1.0, tiny())
-        for b in range(2):
-            ee, th = tmp(64, "tb"), tmp(64)
-            axb(th(), blk(od2, 64, b), col(x2, 32 * b), col(zero, 0))
-            tt(ee(), r2(), th(), A.is_lt)
-            total(col(c2, b), ee())
-        for f in range(2):
-            m2, t2 = tmp(64), tmp(64)
-            for b in range(2):
-                ts(blk(m2, 32, b), pat2(), col(c2, b), A.is_equal, col(kc, b) if f else col(xe, b), A.mult)
-            tr(t2(), m2())
-            total(col("land", L + 4 * me + f), t2())
-        mine, key = V("land", L + 4 * me, L + 4 * me + 4), col("land", L + 4 * me + 1)
-        bids = [send(mine, lambda r: mine, "bids%d" % t)]
+            scan(cs(96 * f, 96 * f + 96, 1, 0, 64), t1(0, 96, 1, 0, 64), t1(0, 96, 1, 64, 128), A.add, A.add, 0.0)
+        xa, xb = col(cs, 95, 0, 32), col(cs, 95, 32, 64)
+        ts(col(uw, 0, 0, 32), xa, xb, A.is_le, col(cs, 191, 0, 32), A.mult)
+        ts(col(uw, 1, 0, 32), xb, xa, A.is_lt, col(cs, 191, 32, 64), A.mult)
+        for q in range(4):
+            axb(col("land", L + 13, 32 * q, 32 * q + 32), col(uw, 0, 0, 32), 1.0, col(uw, 1, 0, 32))
+            ts(col("land", L + 12, 32 * q, 32 * q + 32), xa, xb, A.min, TINY, A.add)
+        mine, key = V("land", L + 12, L + 16), col("land", L + 13)
+        bids = [send(mine, lambda r: blk("land", 4, L // 4 + (me - r - 1) % N), "bids%d" % t)]
         if t == 0:
             ms(V("pm", 7, 600, 200), 1e29)
             load(V("tw"), T.w[:], [key])
@@ -347,7 +349,7 @@ def rank_program(g, core, T, topo):
         ts(xl(), gl(0, 1), -KEY, A.mult, xk(), A.add)
         if t:
             lr, lc = tmp(32, "tb"), tmp(32, "tb")
-            cp2(lr(), ind(V("wm"), gl()))
+            cp2(lr(), ind(V("wm", 16, 272), gl()))
             tr(lc(), lr())
             ts(g4(0, 1), col(lc, 0), 128.0, A.add)
             for b in range(4):
@@ -366,7 +368,7 @@ def rank_program(g, core, T, topo):
         if not last:
             xo, ro, po = tmp(64), tmp(64), tmp(16)
             for f in range(2):
-                axb(blk(xo, 32, f), zero(), 1.0, col("land", L + 4 * me + f))
+                times(blk(xo, 32, f), one(), col("land", L + 12 + f))
             tr(ro(), xo(), V("tn", 0, 64))
             tt(po(), ind(V("pp"), gl(0, 1)), ro(0, 16), A.subtract)
             for kk in range(3):
@@ -375,33 +377,27 @@ def rank_program(g, core, T, topo):
                 tt(pk(), po(), e(), A.subtract)
                 mm(V("psS", 512 * kk, 512 * kk + 128), blk("xpq", 128, kk), blk("xps", 128, kk), V(oq), V(oz))
                 tt(blk(vo[kk], 16, 3), pk(), V("psS", 512 * kk, 512 * kk + 16), A.subtract)
-        arrive("bids%d" % t, bids, [V("land", L + 4 * r, L + 4 * r + 4) for r in peers])
+        arrive("bids%d" % t, bids, [V("land", L, L + 12)])
         lw, keys = V("land", L, L + 16), V("land", L + 1, L + 16, 4)
         xs, rs, sm, pr, nn = tmp(128), tmp(128), tmp(64), tmp(64), tmp(16)
         for f in range(2):
             cp2(blk(xs, 64, f), ind(lw, blk(l_s, 4, f)))
             tr(blk(rs, 64, f), blk(xs, 64, f))
-        axb(sm(0, 4), keys, 1 / KEY, up())
-        axb(sm(4, 8), sm(0, 4), 1.0, down())
         ts(blk("oi", 4, t), keys, 1 / (KEY * NI), A.mult, -24.5 / NI, A.add)
         ts(sm(8, 12), blk("oi", 4, t), 256.0, A.mult)
-        axb(sm(12, 16), sm(4, 8), 2.0 ** -8, shift())
+        axb(sm(12, 16), keys, 2.0 ** -8 / KEY, 128.0)
         tt(sm(16, 20), sm(12, 16), sm(8, 12), A.add)
-        axb(sm(20, 24), sm(4, 8), 1.0, col(k, 12))
-        for a, b, c in turn:
-            gs = tmp(b - a, "tu")
-            ts(gs(), V("land", L + 4 * a + 1, L + 4 * b, 4), 1 / KEY, A.mult, -1.0, A.add, keys)
-            tt(pr(16 * c, 16 * (c + b - a)), ind(V("pp"), gs()), rs(16 * a, 16 * b), A.subtract)
+        axb(sm(20, 24), keys, 1 / KEY, col(k, 12))
+        gs = tmp(4, "tu")
+        ts(gs(), keys, 1 / KEY, A.mult, -1.0, A.add)
+        tt(pr(), ind(V("pp"), gs()), blk(rs, 64, 0), A.subtract)
+        axb(sm(24, 28), keys, 2 / KEY, -0.25)
         for r in range(N):
-            nb, pen, z = col("land", L + 4 * r), tmp(64, "tb"), tmp(64, "tb")
-            if r > 0:
-                ts(bm(64 * r, 80 * r), rs(0, 16 * r), nb, A.is_le)
-            if r < N - 1:
-                ts(bm(80 * r + 16, 64 * r + 64), rs(16 * r + 16, 64), nb, A.is_lt)
-            ac(pen(), blk(rs, 64, 1), F.Abs, bias=col(sm, 4 + r), scale=-1 / KEY)
-            tt(z(), blk(bm, 64, r), pen(), A.subtract)
-            count(col(nn, 4 * r), z(), F.Relu, bias=lose(), scale=2.0 ** 18)
-            count(col(sm, 36 + r), blk(rs, 64, 0), F.Sign, bias=nb, scale=-1.0)
+            sg, pen, z = tmp(64, "tb"), tmp(64), tmp(64)
+            ac(sg(), blk(rs, 64, 0), F.Sign, col("land", L + 4 * r), -1.0, col(sm, 36 + r))
+            ac(pen(), blk(rs, 64, 1), F.Square, bias=col(sm, 24 + r), scale=-2 / KEY)
+            tt(z(), sg(), pen(), A.subtract)
+            count(col(nn, 4 * r), z(), F.Relu, bias=2.0 ** 24 - 2.0 ** 14, scale=2.0 ** 28)
         kw, xz, of, s3, sw = tmp(16), tmp(64), tmp(4, "tu"), tmp(16), tmp(64)
         tt(s3(0, 16, 4), sm(36, 40), sm(16, 20), A.add)
         cp2(sw(), ind(s3(0, 13), blk(l_s, 4, 0)))
@@ -416,9 +412,7 @@ def rank_program(g, core, T, topo):
             else:
                 ts(cb(160 * r, 160 * r + 64), rz(0, 64), col(sm, 8 + r), A.is_lt, -1024.0, A.mult)
                 ts(cb(160 * r + 64, 160 * r + 136), rz(0, 72), col(kw, 4 * r), A.is_lt, 1024.0, A.mult)
-                total(col(sm, 52 + r), cb(160 * r, 160 * r + 137))
-            c = (r - me - 1) % N
-            ts(col(of, c), col(sm, 52 + r), col(sm, 20 + r), A.max, col(k, 16 + r), A.min)
+            ts(col(of, r), col(sm, 52 + r) if r < 2 else fold(cb, 160 * r, 69, "tb"), col(sm, 20 + r), A.max, col(k, 16 + r), A.min)
         arrive("cols%d" % t, cols, [V(n, O, O + 48) for n in ("pq", "pz")])
         new = (V("pq", O - 64, O + 64), V("pz", O - 64, O + 64))
         if not last:
@@ -427,27 +421,39 @@ def rank_program(g, core, T, topo):
                 tt(vo[kk](0, 48), pr(0, 48), V("psS", 512 * kk + 64, 512 * kk + 112), A.subtract, pr())
                 cp(ind(blk("v", 256, kk), of()), vo[kk]())
             decode(O - 64, 128, 64)
-        cp(ind(V("wm"), of()), wc(O, O + 64))
-        yn, hr = tmp(64), tmp(256)
+            cp(ind(V("wm", 16, 272), of()), wc(O + 16, O + 80))
+        yn = tmp(64)
         mm(V("psY", 0, 128), V("wq"), V("ws"), *new)
         cp2(yn(), V("psY", 64, 128))
         cp(ind(V("yo"), of()), yn())
-        axb(blk(hr, 64, 0), blk(rs, 64, 1), 1 / KEY, up())
-        axb(blk(hr, 64, 1), blk(hr, 64, 0), 1.0, down())
-        axb(blk(hr, 64, 2), blk(hr, 64, 1), -KEY, mid())
-        for a, b, c in turn:
-            tt(hr(192 + 16 * c, 192 + 16 * (c + b - a)), hr(128 + 16 * a, 128 + 16 * b), rs(64 + 16 * a, 64 + 16 * b), A.add)
-        cp(ind(V("pp"), of()), pr())
-        cp(ind(V("hp"), of()), blk(hr, 64, 3))
-        store("a", T.pr[t:t + 1, :], V("pp", NI * me, NI * me + NI, 1, 0, 1))
-        store("a" if last else "s", T.ho[t:t + 1, :], V("hp", NI * me, NI * me + NI, 1, 0, 1))
+        a, ho = NI * me, tmp(NI)
+        if last:
+            fa, fb = tmp(128), tmp(192)
+            times(fa(0, 80), V("wm", a, a + 80), col(k, 32))
+            for p, u, w in ((0, "pp", pr(0, 64, 1, 0, 64)), (64, "hp", rs(64, 128, 1, 64, 128))):
+                times(fb(0, 48, 1, p, p + 64), V(u, a, a + NI, 1, p, p + 64), col("bits", 0, p, p + 64))
+                times(fb(64, 128, 1, p, p + 64), w, col("bits", 0, p, p + 64))
+            cp2(V("fin", a, a + 16), fa(0, 16))
+            cp2(V("fin", a + 64, a + 80), fa(64, 80))
+            tt(V("fin", a + 16, a + 64), fa(16, 64), fb(0, 48), A.add)
+            tt(fb(128, 192), fb(64, 128), wl(), A.add)
+            cp(ind(V("fin", 16, 272), of()), fb(128, 192), V("fin"))
+            tt(ho(0, NI, 1, 64, 96), V("fin", a + 16, a + 64, 1, 64, 96), hk(0, NI, 1, 64, 96), A.subtract)
+            store("a", T.pr[t:t + 1, :], V("fin", a + 16, a + 64, 1, 16, 17))
+            store("a", T.ho[t:t + 1, :], ho(0, NI, 1, 80, 81))
+        else:
+            cp(ind(V("pp"), of()), pr())
+            cp(ind(V("hp"), of()), blk(rs, 64, 1))
+            tt(ho(0, NI, 1, 0, 32), V("hp", a, a + NI, 1, 0, 32), hk(0, NI, 1, 0, 32), A.subtract)
+            store("a", T.pr[t:t + 1, :], V("pp", a, a + NI, 1, 0, 1))
+            store("s", T.ho[t:t + 1, :], ho(0, NI, 1, 0, 1))
 
     store("s", T.y[:], V("yo", 0, 192), 0.5)
-    wd, tm, lst = tmp(96, "tb"), tmp(96, "tb"), tmp(3, "tu")
-    cp2(wd(), ind(V("wm"), l_d()))
-    tr(tm(), wd())
-    ts(lst(), tm(0, 96, 32), 128.0, A.add)
-    pick(V("nq"), V("nz"), V("pq"), V("pz"), lst())
+    tm, lst = tmp(128), tmp(16, "tu")
+    for j in range(2):
+        tr(blk(tm, 64, j), V("fin", a + 16 * j, a + 16 * j + 64))
+    ts(lst(), ind(tm(), l_h()), 128.0, A.add)
+    pick(V("nq"), V("nz"), V("pq"), V("pz"), lst(0, 3))
     store("s", T.oc[:], b8(V("nq")), 0.3)
     for u in range(4):
         store("s" if u < 1 else "a", T.osc[4 * u:4 * u + 4, :], V("nz", 0, NI, 1, 32 * u, 32 * u + 4))
@@ -503,31 +509,40 @@ def emit(g, T, ops, sent):
     span = [min(a[2] for a in ops[i]["alts"]) + tail[i] + WAKE for i in range(n)]
     listed = [o["ind"] for o in ops]
 
-    def play(order, way):
-        score, pairs = 0.0, []
-        for wake, slow, fly, rows, jump in OTHER + [(WAKE, 1.0, FLY, ROWS, 1.0)]:
-            free, fin, why = {}, [0.0] * n, [-1] * n
-            for i in order:
-                q, s, c = way[i][0], 0.0, -1
-                for j in aft[i]:
-                    if fin[j] + wake > s:
-                        s, c = fin[j] + wake, j
+    guesses = OTHER + [(WAKE, 1.0, FLY, ROWS, 1.0)]
+    scale = [[u[1] * (u[4] if listed[i] else 1.0) for i in range(n)] for u in guesses]
+    plus = [[tail[i] + u[0] + (u[2] + u[3] * len(ops[i]["ext"][2]) if ops[i]["kind"] == "x" else 0.0) for i in range(n)] for u in guesses]
+    ends = [i for i in range(n) if not nxt[i]]
+
+    def play(order, way, old=None, at=0):
+        score, pairs, kept, lastq = 0.0, [], [], {}
+        for i in order[:at]:
+            lastq[way[i][0]] = i
+        rest = [(i, way[i][0], way[i][2] if way[i][0] else 0.0, aft[i]) for i in order[at:]]
+        for m in range(len(guesses)):
+            sc, pl = scale[m], plus[m]
+            fin, why = (list(old[m][0]), list(old[m][1])) if old else ([0.0] * n, [-1] * n)
+            free = dict((q, (fin[i] - pl[i], i)) for q, i in lastq.items())
+            for i, q, d, js in rest:
+                s, c = 0.0, -1
+                for j in js:
+                    if fin[j] > s:
+                        s, c = fin[j], j
                 if q:
                     f = free.get(q)
                     if f and f[0] > s:
                         s, c = f
-                    e = s + way[i][2] * slow * (jump if listed[i] else 1.0)
-                    free[q] = (e, i)
-                else:
-                    e = s + fly + rows * len(ops[i]["ext"][2])
-                fin[i], why[i] = e + tail[i], c
-            i = max(range(n), key=lambda i: fin[i])
-            score += fin[i]
+                    s += d * sc[i]
+                    free[q] = (s, i)
+                fin[i], why[i] = s + pl[i], c
+            i = max(ends, key=lambda u: fin[u])
+            score += fin[i] - guesses[m][0]
             while why[i] >= 0:
                 if why[i] not in aft[i]:
                     pairs.append((why[i], i))
                 i = why[i]
-        return score, pairs, fin
+            kept.append((fin, why))
+        return score, pairs, [u - WAKE for u in fin], kept
 
     def plan(fac, lean):
         rank = [0.0] * n
@@ -607,7 +622,7 @@ def emit(g, T, ops, sent):
                     if any(x in take for x in aft[u]):
                         take.add(u)
                 o2[a:b + 1] = [u for u in order[a:b + 1] if u not in take] + [u for u in order[a:b + 1] if u in take]
-            new = play(o2, w2)
+            new = play(o2, w2, now[3], a)
             if new[0] <= now[0] + HEAT * (1 - trial / MOVES) * draw():
                 now, order, way = new, o2, w2
                 if now[0] < best[0]:

from concourse.bass import DstId, RemoteDMATransfer
from concourse.mybir import dt, AluOpType, AxisListType, ActivationFunctionType

NI, NB, NK, NM, NR = 48, 384, 12, 8, 3
C4, U8, F32, BF, U16, I32 = "float8_e4m3fn_x4", "uint8", "float32", "bfloat16", "uint16", "int32"
PW = 384


def _s(n, d):
    return ("sbuf", [128, n], d)


SCRATCH = {
    "ti": _s(512, BF), "tx": _s(1536, BF), "tw": _s(512, BF), "te": _s(1040, BF), "tn": _s(512, BF),
    "iq": _s(128, C4), "isc": _s(128, U8), "xq": _s(384, C4), "xs": _s(384, U8), "xpq": _s(384, C4), "xps": _s(384, U8),
    "wq": _s(128, C4), "ws": _s(128, U8), "eq": _s(512, C4), "es": _s(512, U8),
    "pq": _s(PW, C4), "pz": _s(PW, U8), "nq": _s(48, C4), "nz": _s(48, U8),
    "oq0": _s(128, C4), "oz0": _s(128, U8), "oq1": _s(128, C4), "oz1": _s(128, U8), "oq2": _s(128, C4), "oz2": _s(128, U8),
    "hdx": _s(1536, BF), "hdv": _s(4 * PW, BF), "gv": _s(64, F32),
    "psS": ("psum", [128, 1536], F32), "psD": ("psum", [128, 2048], F32), "psY": ("psum", [128, 512], F32),
    "pint": _s(8, I32), "bint": _s(8, I32), "bits": _s(8, F32), "r128": _s(128, BF), "oi": _s(16, I32),
    "land": _s(48, F32), "v": _s(768, F32), "pm": _s(600, F32), "qm": _s(576, F32), "yo": _s(256, F32),
    "pp": _s(256, F32), "hp": _s(256, F32), "wm": _s(272, BF), "fin": _s(272, F32),
    "tf": _s(16384, F32), "tb": _s(16384, BF), "tu": _s(512, U16),
}
POOLS = {"v": 56, "a": 44, "p": 10, "g": 8, "sd": 14, "ad": 8}
SEMAPHORES = [q + str(i) for q in POOLS for i in range(POOLS[q])] + ["sent", "items"] + \
    ["bids%d" % t for t in range(NR)] + ["cols%d" % t for t in range(NR)]
HELD = 2.0 ** 88
TINY = 2.0 ** -120
KEY, MID = 8192.0, 768.0
CYC, WAKE, GATH, SCAT, FLY, ROWS, LOCAL = 0.00085, 0.2, 1.5, 3.8, 0.95, 1.0, 1.5
OTHER = [(0.19, 1.0, 0.9, 0.75, 1.0), (0.22, 1.25, 1.2, 1.6, 1.3), (0.21, 1.3, 1.0, 0.9, 1.5)]
TRIES, MUT, MOVES, HEAT = 600, 10, 60000, 0.1
NA = 1
KEPT = {}


def rank_program(g, core, T, topo):
    me = T.rank_of(core)
    if me is None:
        return
    N = len(T.cores)
    A, F = AluOpType, ActivationFunctionType
    peers = [r for r in range(N) if r != me]
    engs = [e for e in topo.engines(core, T.cores[peers[0]]) if all(e in topo.engines(core, T.cores[r]) for r in peers)]
    ids = [DstId(rid=topo.addr(T.cores[r])[0], pnc=topo.addr(T.cores[r])[1]) for r in peers]
    ops = []

    def V(name, a=0, b=None, step=1, p0=0, p1=128):
        b = SCRATCH[name][1][1] if b is None else b
        cols = range(a, b, step)
        if SCRATCH[name][0] == "psum":
            reg = (name, 0, 128, a // 512, a // 512, frozenset([a // 512]))
        else:
            reg = (name, p0, p1, a, b - 1, frozenset(cols))
        kind = "p" if SCRATCH[name][0] == "psum" else "h" if SCRATCH[name][2] in (BF, U16) else "s"
        return (T[name][p0:p1, a:b:step] if step > 1 else T[name][p0:p1, a:b], [reg], len(cols), kind)

    used = {"tf": 0, "tb": 0, "tu": 0}

    def tmp(n, pool="tf"):
        base = used[pool]
        al = 2 if pool == "tu" else 16
        used[pool] += (n + al - 1) // al * al
        assert used[pool] <= SCRATCH[pool][1][1]

        def view(a=0, b=None, step=1, p0=0, p1=128):
            return V(pool, base + a, base + (n if b is None else b), step, p0, p1)
        return view

    def col(w, a, p0=0, p1=128):
        return V(w, a, a + 1, 1, p0, p1) if isinstance(w, str) else w(a, a + 1, 1, p0, p1)

    def blk(w, n, j):
        return V(w, n * j, n * j + n) if isinstance(w, str) else w(n * j, n * j + n)

    def ind(w, o):
        return (w[0].indirect(o[0]), w[1] + o[1], 16 * o[2], "i")

    def b8(w):
        return (w[0].bitcast(dt.uint8),) + w[1:]

    def b32(w):
        return (w[0].bitcast(dt.uint32),) + w[1:]

    def ap(x):
        return x[0] if isinstance(x, tuple) else x

    def rec(alts, wr, rd, kind="c", ext=None):
        r = [z for x in rd if isinstance(x, tuple) for z in x[1]] + [z for x in wr for z in x[1][1:]]
        ops.append({"alts": alts, "w": [x[1][0] for x in wr], "r": r, "x": [z for z in r if SCRATCH[z[0]][0] == "psum"], "kind": kind, "ext": ext,
                    "ind": any(isinstance(x, tuple) and x[3] == "i" for x in list(wr) + list(rd))})
        return len(ops) - 1

    def cost(o, i, mul=None, base=0.05):
        if o[3] == "i":
            return base + SCAT * CYC * o[2]
        if i[3] == "i":
            return base + GATH * CYC * o[2]
        if mul is None:
            mul = 0.5 if o[3] == i[3] == "h" else 1.0
        return CYC * max(64, mul * i[2])

    vec, act, pe = g.vector, g.scalar, g.tensor

    def vts(o, i, s1, op0, s2=None, op1=None):
        if op1 is None:
            return ("v", lambda: vec.tensor_scalar(o[0], i[0], ap(s1), None, op0), cost(o, i))
        return ("v", lambda: vec.tensor_scalar(o[0], i[0], ap(s1), ap(s2), op0, op1), cost(o, i))

    def aac(o, i, f, bias=None, scale=None, acc=None):
        kw = {}
        if bias is not None:
            kw["bias"] = ap(bias)
        if scale is not None:
            kw["scale"] = ap(scale)
        if acc is not None:
            kw["accum_out"] = acc[0]
        return ("a", lambda: act.activation(o[0], i[0], f, **kw), cost(o, i, 1.0, 0.065) + (0.02 if acc is not None else 0))

    def ts(o, i, s1, op0, s2=None, op1=None, behind=None):
        rec([vts(o, i, s1, op0, s2, op1)], [o], [i, s1, s2, behind])

    def ac(o, i, f, bias=None, scale=None, acc=None):
        rec([aac(o, i, f, bias, scale, acc)], [o] + ([acc] if acc is not None else []), [i, bias, scale])

    def count(acc, i, f, bias=None, scale=None):
        ac(tmp(i[2], "tb")(), i, f, bias, scale, acc)

    def axb(o, i, a, b):
        rec([aac(o, i, F.Identity, b, a), vts(o, i, a, A.mult, b, A.add)], [o], [i, a, b])

    def times(o, i, c):
        rec([aac(o, i, F.Copy, None, c), vts(o, i, c, A.mult)], [o], [i, c])

    def tt(o, a, b, op, behind=None):
        rec([("v", lambda: vec.tensor_tensor(o[0], a[0], b[0], op), cost(o, a, 1.0 if "p" in (a[3], b[3]) else 2.0))], [o], [a, b, behind])

    def cp(o, i, behind=None):
        rec([("v", lambda: vec.tensor_copy(o[0], i[0]), cost(o, i))], [o], [i, behind])

    def cp2(o, i):
        rec([aac(o, i, F.Copy), ("v", lambda: vec.tensor_copy(o[0], i[0]), cost(o, i))], [o], [i])

    def ms(o, c):
        rec([("v", lambda: vec.memset(o[0], c), cost(o, o))], [o], [])

    def tr(o, i, behind=None):
        rec([("v", lambda: vec.transpose(o[0], i[0]), cost(o, i))], [o], [i, behind])

    def total(o, i):
        j = tmp(i[2])()
        rec([("v", lambda: vec.tensor_reduce(o[0], i[0], AxisListType.X, A.add), cost(o, i, 1.0)), aac(j, i, F.Identity, None, None, o)], [o, j], [i])

    def scan(o, a, b, op0, op1, init):
        rec([("v", lambda: vec.tensor_tensor_scan(o[0], a[0], b[0], init, op0, op1), cost(o, a))], [o], [a, b])

    def fold(w, a, n, pool):
        o = tmp(n, pool)
        scan(o(), w(a, a + n), w(a + n, a + 2 * n), A.add, A.add, 0.0)
        return col(o, n - 1)

    def quant(q, s, i):
        rec([("v", lambda: vec.quantize_mx(q[0], s[0], i[0]), 0.012 + 0.00022 * i[2])], [q, s], [i])

    def mm(o, lq, ls, rq, rs):
        rec([("p", lambda: pe.matmul_mx(o[0], lq[0], ls[0], rq[0], rs[0], True, True), 1.5 * CYC * (rq[2] + 16))], [o], [lq, ls, rq, rs])

    def iota(o, pattern, base, cm):
        kw = {} if o[1][0][0] == "pint" else {"allow_small_or_imprecise_dtypes": True}
        rec([("g", lambda: g.iota(o[0], pattern, base, cm, **kw), 0.13 + 2 * CYC * o[2])], [o], [])

    def load(o, src, behind=()):
        rec([("s", lambda: g.sync.dma_start(o[0], src), 0.08)], [o], list(behind), kind="d", ext=o[2] / 800.0 - 0.6)

    def store(q, dst, i, more=0.0):
        e = g.sync if q == "s" else act
        rec([(q, lambda: e.dma_start(dst, i[0]), 0.08)], [], [i], kind="o", ext=more)

    sent = [0]

    def send(s, d, sem):
        trs = [RemoteDMATransfer(dst_ids=ids, dma_engine_mask=sum(1 << e for e in engs), remote_sem=T.sem[sem], srcs=[s[0]], dsts=[d(r)[0] for r in peers])]
        sent[0] += len(engs)
        return rec([("g", lambda: g.remote_dma_fused(trs, local_sem=T.sem.sent), 0.3)], [], [s], kind="r")

    def arrive(sem, calls, views):
        rec([(None, None, FLY + ROWS * len(calls))], views, [], kind="x", ext=(sem, len(calls) * len(engs) * len(peers), calls))

    def pick(oq, oz, wq, wz, lst):
        ac(oz, ind(wz, lst), F.Copy)
        cp(b32(oq), ind(b32(wq), lst))

    def const(n, c, pool="tf"):
        w = tmp(n, pool)
        ms(w(), c)
        return w

    def decode(a, n, skip):
        for b in range(4):
            mm(V("psD", 512 * b, 512 * b + n), blk("eq", 128, b), blk("es", 128, b), V("pq", a, a + n), V("pz", a, a + n))
            times(V("hdv", PW * b + a + skip, PW * b + a + n), V("psD", 512 * b + skip, 512 * b + n), 0.5)

    load(V("ti", 0, 192), T.it[:])
    load(V("tx"), T.x[:])
    row, ep, hk, wc, ki = tmp(64), tmp(24), tmp(NI), tmp(PW + 16, "tb"), tmp(16)
    k, od3, od2, pat, rz, cb = tmp(48), tmp(32), tmp(33), tmp(32), tmp(80), tmp(640, "tb")
    iota(col("pint", 0), [[0, 1]], 0, 1)
    iota(row(), [[1, 64]], 0, 0)
    for kk in range(3):
        iota(blk(ep, 8, kk), [[96, 2], [192, 2], [16, 2]], 32 * kk, 0)
    iota(ki(0, 8), [[1, 2], [8, 2], [0, 2]], 0, 0)
    ms(V("ti", 192, 512), 0.0)
    for j, (sh, m) in enumerate([(4, 1), (5, 1), (0, 15), (0, 31), (6, 1)]):
        ts(col("bint", j), col("pint", 0), sh, A.logical_shift_right, m, A.bitwise_and)
    cp(V("bits", 0, 5), V("bint", 0, 5))
    hh, q0, s16, s32, q1 = [col("bits", j) for j in range(5)]
    l_i, l_p, l_h, l_s = tmp(3, "tu"), tmp(24, "tu"), tmp(1, "tu"), tmp(8, "tu")
    ts(l_i(), row(0, 48, 16), s16, A.add)
    ts(l_p(), ep(), s16, A.add)
    times(col(k, 2), hh, 4.0)
    ts(l_s(), ki(0, 8), col(k, 2), A.add)
    quant(V("iq"), V("isc"), V("ti"))
    first = [send(b8(V("iq", 0, NI)), lambda r: b8(blk("pq", NI, me)), "items"), send(V("isc", 0, NI), lambda r: blk("pz", NI, me), "items")]
    iota(V("r128"), [[1, 128]], 0, -1)
    ms(V("te"), 0.0)
    ts(V("te", 2, 514, 4), V("r128"), 0.0, A.is_equal)
    ts(V("te", 523, 1035, 4), V("r128"), 0.0, A.is_equal)
    iota(wc(), [[1, PW + 16]], -144, 0)
    iota(V("hp", 0, 192), [[int(KEY), 192]], int(KEY - MID - 1), 0)
    iota(hk(), [[int(KEY), NI]], int(KEY * (NI * me + 1) - MID), 0)
    iota(ki(8, 11), [[32, 3]], int(NB * me - MID), 0)
    iota(ki(12, 16), [[16, 4]], 192, 0)
    iota(V("tn", 64, 512), [[0, 448]], 0, 0)
    iota(V("pp", 0, 192), [[0, 192]], 0, 0)
    iota(rz(64, 80), [[0, 16]], 8192, 0)
    for r in range(2, N):
        iota(cb(160 * r + 136, 160 * r + 138), [[1024 * NM - 512, 2]], 512 - 1024 * NM, 0)
    for t in range(NR):
        iota(V("land", 16 * t + 14, 16 * t + 16), [[0, 2]], 0, 0)
    for b, a in enumerate([2, 522, 0, 520]):
        quant(blk("eq", 128, b), blk("es", 128, b), V("te", a, a + 512))
    pick(blk("pq", NI, me), blk("pz", NI, me), V("iq"), V("isc"), l_i())
    quant(V("xq"), V("xs"), V("tx"))
    pick(V("xpq"), V("xps"), V("xq"), V("xs"), l_p())
    for b in range(4):
        mm(V("psD", 512 * b, 512 * b + NB), blk("eq", 128, b), blk("es", 128, b), V("xq"), V("xs"))
        times(blk("hdx", NB, b), V("psD", 512 * b, 512 * b + NB), 0.5)
    neg, one, two, far, minus = tmp(192), tmp(32), tmp(2), tmp(32), tmp(32)
    axb(neg(), V("ti", 0, 192), 0.0, -1e29)
    for w, c in ((one, 1.0), (two, -KEY), (far, -HELD / 2), (minus, -1.0), (pat, 999.0)):
        axb(w(), row(0, w()[2]), 0.0, c)
    axb(col(k, 0), q0, 192.0, s32)
    axb(col(k, 1), q1, 96.0, col(k, 0))
    axb(k(4, 7), ki(8, 11), 1.0, col(k, 1))
    ts(od3(), row(0, 32), s32, A.is_lt, -2.0 ** -24, A.mult)
    axb(od2(0, 32), od3(), 1.0, 1.0)
    axb(col(od2, 32), q1, -2.0 ** -24, 1.0)
    axb(col(k, 8), q0, -2.0, 1.0)
    times(col(k, 9), q0, NK - 1.0)
    for j in range(2):
        axb(pat(16 * j, 16 * j + NK), row(0, NK), col(k, 8), col(k, 9))
    ts(col(k, 11), s16, float(NK), A.is_lt)
    axb(k(16, 20), ki(12, 16), 1.0, s16)
    axb(col(k, 12), col(k, 11), -1000.0, 999.0)
    wl = tmp(64)
    axb(col(k, 32), hh, -1.0, 1.0)
    times(wl(), wc(PW - 48, PW + 16), col(k, 32))
    ts(col(k, 33), s16, col(k, 32), A.add, 3.0, A.min)
    times(col(k, 34), col(k, 33), 64.0)
    ts(col(k, 35), col(k, 33), 2.0, A.is_ge, -96.0, A.mult)
    ts(l_h(), col(k, 34), col(k, 35), A.add)
    axb(k(24, 28), row(0, 4), PW * KEY, -KEY)
    ms(V("pm", 7, 600, 200), -1e29)
    ms(V("hdv", PW - 1, 4 * PW, PW), 0.0)
    cp2(V("wm"), wc(0, 272))
    arrive("items", first, [blk(n, NI, r) for n in ("pq", "pz") for r in peers])
    decode(0, 192, 0)

    for t in range(NR):
        last = t == NR - 1
        oq, oz, L, O = "oq%d" % t, "oz%d" % t, 16 * t, 192 + 64 * t
        g1, x1, r1, a3, kb, fe = tmp(3), tmp(96), tmp(192), tmp(3), tmp(3), tmp(3)
        u, w, sign = (A.min, A.max, -1.0) if t else (A.max, A.min, 1.0)
        for kk in range(3):
            if t == 0:
                mm(V("psS", 512 * kk, 512 * kk + 192), blk("xpq", 128, kk), blk("xps", 128, kk), V("pq", 0, 192), V("pz", 0, 192))
            o = ("v", 256 * kk) if t else ("psS", 512 * kk)
            P = 200 * kk + 8
            top, sec, fw = col("pm", P + 191), col("qm", 192 * kk + 190), tmp(32)
            scan(V("pm", P, P + 192), V(o[0], o[1], o[1] + 192), V(o[0], o[1], o[1] + 192) if t else neg(), u, u, -1e29 * sign)
            scan(V("qm", 192 * kk, 192 * kk + 191), V(o[0], o[1] + 1, o[1] + 192), V("pm", P, P + 191), u, w, -1e29 * sign)
            if t == 0:
                times(fw(), minus(), top)
            elif kk < 2:
                ac(col(fe, kk), top, F.Relu, -HELD / 8, -4.0)
                axb(fw(), one(), top, col(fe, kk))
            else:
                ts(fw(), far(), top, A.subtract, top, A.max)
            ts(blk(x1, 32, kk), fw(), sec, A.subtract if t else A.add, -TINY, A.add)
            count(col(g1, kk), V("pm", P - 1, P + 192), F.Sign, bias=top, scale=-1.0)
            axb(col(kb, kk), col(g1, kk), KEY * sign, col(k, 4 + kk))
            if t == 0:
                times(V("v", 256 * kk, 256 * kk + 192), V("psS", 512 * kk, 512 * kk + 192), -1.0)
        an = []
        tr(r1(0, 96), x1())
        tr(r1(96, 192, 1, 0, 64), x1(0, 96, 1, 64, 128))
        tr(r1(96, 192, 1, 64, 128), x1(0, 96, 1, 0, 64))
        for kk in range(3):
            ee, th, x = tmp(192, "tb"), tmp(33), col(x1, 32 * kk)
            times(th(), od2(), x)
            tt(blk(ee, 32, kk), blk(r1, 32, kk), th(0, 32), A.is_lt)
            if kk > 0:
                ts(ee(0, 32 * kk), r1(0, 32 * kk), x, A.is_le)
            if kk < 2:
                ts(ee(32 * kk + 32, 96), r1(32 * kk + 32, 96), x, A.is_lt)
            if kk < NA:
                ac(ee(96, 192), r1(96, 192), F.Sign, col(th, 32), -1.0)
                count(col(a3, kk), ee(), F.Relu)
                an.append(col(a3, kk))
            else:
                ts(ee(96, 192), r1(96, 192), col(th, 32), A.is_lt)
                an.append(fold(ee, 0, 96, "tf"))
        cs, uw = tmp(192), tmp(2)
        for f in range(2):
            m1, t1 = tmp(96), tmp(96)
            for kk in range(3):
                ts(blk(m1, 32, kk), pat(), an[kk], A.is_equal, col(kb, kk) if f else col(x1, 32 * kk), A.mult)
            tr(t1(), m1())
            scan(cs(96 * f, 96 * f + 96, 1, 0, 64), t1(0, 96, 1, 0, 64), t1(0, 96, 1, 64, 128), A.add, A.add, 0.0)
        xa, xb = col(cs, 95, 0, 32), col(cs, 95, 32, 64)
        ts(col(uw, 0, 0, 32), xa, xb, A.is_le, col(cs, 191, 0, 32), A.mult)
        ts(col(uw, 1, 0, 32), xb, xa, A.is_lt, col(cs, 191, 32, 64), A.mult)
        for q in range(4):
            axb(col("land", L + 13, 32 * q, 32 * q + 32), col(uw, 0, 0, 32), 1.0, col(uw, 1, 0, 32))
            ts(col("land", L + 12, 32 * q, 32 * q + 32), xa, xb, A.min, TINY, A.add)
        mine, key = V("land", L + 12, L + 16), col("land", L + 13)
        bids = [send(mine, lambda r: blk("land", 4, L // 4 + (me - r - 1) % N), "bids%d" % t)]
        if t == 0:
            ms(V("pm", 7, 600, 200), 1e29)
            load(V("tw"), T.w[:], [key])
            quant(V("wq"), V("ws"), V("tw"))
            mm(V("psY", 0, 192), V("wq"), V("ws"), V("pq", 0, 192), V("pz", 0, 192))
            cp2(V("yo", 0, 192), V("psY", 0, 192))
        gl, g4, xl, xk = tmp(2, "tu"), tmp(4, "tu"), tmp(1, "tu"), tmp(1)
        ts(gl(), two(), key, A.add, 1 / KEY, A.mult)
        ts(xk(), key, MID - KEY - NB * me, A.add)
        ts(xl(), gl(0, 1), -KEY, A.mult, xk(), A.add)
        if t:
            lr, lc = tmp(32, "tb"), tmp(32, "tb")
            cp2(lr(), ind(V("wm", 16, 272), gl()))
            tr(lc(), lr())
            ts(g4(0, 1), col(lc, 0), 128.0, A.add)
            for b in range(4):
                cp2(blk("gv", 16, b), ind(blk("hdx", NB, b), xl()))
                tt(V("tn", b, 64, 4), ind(blk("hdv", PW, b), g4(0, 1)), blk("gv", 16, b), A.add)
        else:
            ts(g4(), k(24, 28), key, A.add, 1 / KEY, A.mult)
            cp2(V("gv"), ind(V("hdv"), g4()))
            for b in range(4):
                tt(V("tn", b, 64, 4), ind(blk("hdx", NB, b), xl()), blk("gv", 16, b), A.add)
        quant(V(oq), V(oz), V("tn"))
        cols = [send(b8(V(oq, 0, 16)), lambda r: b8(blk("pq", 16, O // 16 + (me - r - 1) % N)), "cols%d" % t),
                send(V(oz, 0, 16), lambda r: blk("pz", 16, O // 16 + (me - r - 1) % N), "cols%d" % t)]
        pick(V("pq", O + 48, O + 64), V("pz", O + 48, O + 64), V(oq), V(oz), l_i(0, 1))
        vo = [tmp(64) for kk in range(3)]
        if not last:
            xo, ro, po = tmp(64), tmp(64), tmp(16)
            for f in range(2):
                times(blk(xo, 32, f), one(), col("land", L + 12 + f))
            tr(ro(), xo(), V("tn", 0, 64))
            tt(po(), ind(V("pp"), gl(0, 1)), ro(0, 16), A.subtract)
            for kk in range(3):
                e, pk = tmp(16), tmp(16)
                ts(e(), ro(32, 48), col(kb, kk), A.is_equal, HELD, A.mult)
                tt(pk(), po(), e(), A.subtract)
                mm(V("psS", 512 * kk, 512 * kk + 128), blk("xpq", 128, kk), blk("xps", 128, kk), V(oq), V(oz))
                tt(blk(vo[kk], 16, 3), pk(), V("psS", 512 * kk, 512 * kk + 16), A.subtract)
        arrive("bids%d" % t, bids, [V("land", L, L + 12)])
        lw, keys = V("land", L, L + 16), V("land", L + 1, L + 16, 4)
        xs, rs, sm, pr, nn = tmp(128), tmp(128), tmp(64), tmp(64), tmp(16)
        for f in range(2):
            cp2(blk(xs, 64, f), ind(lw, blk(l_s, 4, f)))
            tr(blk(rs, 64, f), blk(xs, 64, f))
        ts(blk("oi", 4, t), keys, 1 / (KEY * NI), A.mult, -24.5 / NI, A.add)
        ts(sm(8, 12), blk("oi", 4, t), 256.0, A.mult)
        axb(sm(12, 16), keys, 2.0 ** -8 / KEY, 128.0)
        tt(sm(16, 20), sm(12, 16), sm(8, 12), A.add)
        axb(sm(20, 24), keys, 1 / KEY, col(k, 12))
        gs = tmp(4, "tu")
        ts(gs(), keys, 1 / KEY, A.mult, -1.0, A.add)
        tt(pr(), ind(V("pp"), gs()), blk(rs, 64, 0), A.subtract)
        axb(sm(24, 28), keys, 2 / KEY, -0.25)
        for r in range(N):
            sg, pen, z = tmp(64, "tb"), tmp(64), tmp(64)
            ac(sg(), blk(rs, 64, 0), F.Sign, col("land", L + 4 * r), -1.0, col(sm, 36 + r))
            ac(pen(), blk(rs, 64, 1), F.Square, bias=col(sm, 24 + r), scale=-2 / KEY)
            tt(z(), sg(), pen(), A.subtract)
            count(col(nn, 4 * r), z(), F.Relu, bias=2.0 ** 24 - 2.0 ** 14, scale=2.0 ** 28)
        kw, xz, of, s3, sw = tmp(16), tmp(64), tmp(4, "tu"), tmp(16), tmp(64)
        tt(s3(0, 16, 4), sm(36, 40), sm(16, 20), A.add)
        cp2(sw(), ind(s3(0, 13), blk(l_s, 4, 0)))
        tt(kw(0, 16, 4), nn(0, 16, 4), s3(0, 16, 4), A.add)
        tt(xz(), ind(nn(0, 13), blk(l_s, 4, 0)), sw(), A.add)
        tr(rz(0, 64), xz())
        for r in range(N):
            if r < 2:
                count(col(sm, 56 + r), rz(0, 64), F.Sign, bias=col(sm, 8 + r), scale=-1.0)
                count(col(sm, 48 + r), rz(), F.Sign, bias=col(kw, 4 * r), scale=-1.0)
                ts(col(sm, 52 + r), col(sm, 48 + r), col(sm, 56 + r), A.subtract, 512.0, A.mult)
            else:
                ts(cb(160 * r, 160 * r + 64), rz(0, 64), col(sm, 8 + r), A.is_lt, -1024.0, A.mult)
                ts(cb(160 * r + 64, 160 * r + 136), rz(0, 72), col(kw, 4 * r), A.is_lt, 1024.0, A.mult)
            ts(col(of, r), col(sm, 52 + r) if r < 2 else fold(cb, 160 * r, 69, "tb"), col(sm, 20 + r), A.max, col(k, 16 + r), A.min)
        arrive("cols%d" % t, cols, [V(n, O, O + 48) for n in ("pq", "pz")])
        new = (V("pq", O - 64, O + 64), V("pz", O - 64, O + 64))
        if not last:
            for kk in range(3):
                mm(V("psS", 512 * kk, 512 * kk + 128), blk("xpq", 128, kk), blk("xps", 128, kk), *new)
                tt(vo[kk](0, 48), pr(0, 48), V("psS", 512 * kk + 64, 512 * kk + 112), A.subtract, pr())
                cp(ind(blk("v", 256, kk), of()), vo[kk]())
            decode(O - 64, 128, 64)
            cp(ind(V("wm", 16, 272), of()), wc(O + 16, O + 80))
        yn = tmp(64)
        mm(V("psY", 0, 128), V("wq"), V("ws"), *new)
        cp2(yn(), V("psY", 64, 128))
        cp(ind(V("yo"), of()), yn())
        a, ho = NI * me, tmp(NI)
        if last:
            fa, fb = tmp(128), tmp(192)
            times(fa(0, 80), V("wm", a, a + 80), col(k, 32))
            for p, u, w in ((0, "pp", pr(0, 64, 1, 0, 64)), (64, "hp", rs(64, 128, 1, 64, 128))):
                times(fb(0, 48, 1, p, p + 64), V(u, a, a + NI, 1, p, p + 64), col("bits", 0, p, p + 64))
                times(fb(64, 128, 1, p, p + 64), w, col("bits", 0, p, p + 64))
            cp2(V("fin", a, a + 16), fa(0, 16))
            cp2(V("fin", a + 64, a + 80), fa(64, 80))
            tt(V("fin", a + 16, a + 64), fa(16, 64), fb(0, 48), A.add)
            tt(fb(128, 192), fb(64, 128), wl(), A.add)
            cp(ind(V("fin", 16, 272), of()), fb(128, 192), V("fin"))
            tt(ho(0, NI, 1, 64, 96), V("fin", a + 16, a + 64, 1, 64, 96), hk(0, NI, 1, 64, 96), A.subtract)
            store("a", T.pr[t:t + 1, :], V("fin", a + 16, a + 64, 1, 16, 17))
            store("a", T.ho[t:t + 1, :], ho(0, NI, 1, 80, 81))
        else:
            cp(ind(V("pp"), of()), pr())
            cp(ind(V("hp"), of()), blk(rs, 64, 1))
            tt(ho(0, NI, 1, 0, 32), V("hp", a, a + NI, 1, 0, 32), hk(0, NI, 1, 0, 32), A.subtract)
            store("a", T.pr[t:t + 1, :], V("pp", a, a + NI, 1, 0, 1))
            store("s", T.ho[t:t + 1, :], ho(0, NI, 1, 0, 1))

    store("s", T.y[:], V("yo", 0, 192), 0.5)
    tm, lst = tmp(128), tmp(16, "tu")
    for j in range(2):
        tr(blk(tm, 64, j), V("fin", a + 16 * j, a + 16 * j + 64))
    ts(lst(), ind(tm(), l_h()), 128.0, A.add)
    pick(V("nq"), V("nz"), V("pq"), V("pz"), lst(0, 3))
    store("s", T.oc[:], b8(V("nq")), 0.3)
    for u in range(4):
        store("s" if u < 1 else "a", T.osc[4 * u:4 * u + 4, :], V("nz", 0, NI, 1, 32 * u, 32 * u + 4))

    emit(g, T, ops, sent[0])


def clash(a, b):
    return a[1] < b[2] and b[1] < a[2] and a[3] <= b[4] and b[3] <= a[4] and not a[5].isdisjoint(b[5])


def emit(g, T, ops, sent):
    n = len(ops)
    hist, deps = {}, []
    for i, o in enumerate(ops):
        d = set()
        if o["kind"] != "x":
            for z in o["r"]:
                d.update(j for j, y, w in hist.get(z[0], []) if w and clash(z, y))
            for z in o["w"]:
                d.update(j for j, y, w in hist.get(z[0], []) if clash(z, y) and ops[j]["kind"] != "r")
            for z in o["x"]:
                d.update(j for j, y, w in hist.get(z[0], []) if clash(z, y)
                         and not (len(o["alts"]) == len(ops[j]["alts"]) == 1 and o["alts"][0][0] == ops[j]["alts"][0][0]))
        for z in o["r"]:
            hist.setdefault(z[0], []).append((i, z, False))
        for z in o["w"]:
            hist.setdefault(z[0], []).append((i, z, True))
        d.discard(i)
        deps.append(d)
    sends = [i for i in range(n) if ops[i]["kind"] == "r"]
    after = [set(deps[i]) | set(ops[i]["ext"][2] if ops[i]["kind"] == "x" else []) for i in range(n)]
    for a, b in zip(sends, sends[1:]):
        after[b].add(a)
    for i in range(n):
        if ops[i]["alts"][0][0] == "g" and ops[i]["kind"] == "c":
            if i < sends[0]:
                after[sends[0]].add(i)
            else:
                after[i].add(sends[1])
    tail = [LOCAL + o["ext"] if o["kind"] in "do" else 0.0 for o in ops]
    below, aft, nxt = [], [], [[] for i in range(n)]
    for i in range(n):
        m = 0
        for j in after[i]:
            m |= below[j]
        aft.append(sorted(j for j in after[i] if not m >> j & 1))
        for j in after[i]:
            m |= 1 << j
        below.append(m)
        for j in aft[i]:
            nxt[j].append(i)
    span = [min(a[2] for a in ops[i]["alts"]) + tail[i] + WAKE for i in range(n)]
    listed = [o["ind"] for o in ops]

    guesses = OTHER + [(WAKE, 1.0, FLY, ROWS, 1.0)]
    scale = [[u[1] * (u[4] if listed[i] else 1.0) for i in range(n)] for u in guesses]
    plus = [[tail[i] + u[0] + (u[2] + u[3] * len(ops[i]["ext"][2]) if ops[i]["kind"] == "x" else 0.0) for i in range(n)] for u in guesses]
    ends = [i for i in range(n) if not nxt[i]]

    def play(order, way, old=None, at=0):
        score, pairs, kept, lastq = 0.0, [], [], {}
        for i in order[:at]:
            lastq[way[i][0]] = i
        rest = [(i, way[i][0], way[i][2] if way[i][0] else 0.0, aft[i]) for i in order[at:]]
        for m in range(len(guesses)):
            sc, pl = scale[m], plus[m]
            fin, why = (list(old[m][0]), list(old[m][1])) if old else ([0.0] * n, [-1] * n)
            free = dict((q, (fin[i] - pl[i], i)) for q, i in lastq.items())
            for i, q, d, js in rest:
                s, c = 0.0, -1
                for j in js:
                    if fin[j] > s:
                        s, c = fin[j], j
                if q:
                    f = free.get(q)
                    if f and f[0] > s:
                        s, c = f
                    s += d * sc[i]
                    free[q] = (s, i)
                fin[i], why[i] = s + pl[i], c
            i = max(ends, key=lambda u: fin[u])
            score += fin[i] - guesses[m][0]
            while why[i] >= 0:
                if why[i] not in aft[i]:
                    pairs.append((why[i], i))
                i = why[i]
            kept.append((fin, why))
        return score, pairs, [u - WAKE for u in fin], kept

    def plan(fac, lean):
        rank = [0.0] * n
        for i in range(n - 1, -1, -1):
            rank[i] += span[i] * fac[i]
            for j in aft[i]:
                if rank[j] < rank[i]:
                    rank[j] = rank[i]
        busy, start, end, way = {}, [0.0] * n, [0.0] * n, [None] * n
        for i in sorted(range(n), key=lambda i: (-rank[i], i)):
            ready = max([end[j] + WAKE for j in aft[i]] + [0.0])
            best = None
            for c, a in enumerate(ops[i]["alts"]):
                s, at = ready, 0
                if a[0] is not None:
                    line = busy.setdefault(a[0], [])
                    at = len(line)
                    while at > 0 and line[at - 1][1] > s:
                        at -= 1
                    while at < len(line) and s + a[2] > line[at][0]:
                        s = max(s, line[at][1])
                        at += 1
                e = s + a[2] + (lean[i] if c else 0.0)
                if best is None or e < best[0] - 1e-9:
                    best = (e, s, a, at)
            start[i], way[i] = best[1], best[2]
            end[i] = start[i] + way[i][2] + tail[i]
            if way[i][0] is not None:
                busy[way[i][0]].insert(best[3], (start[i], start[i] + way[i][2]))
        order = sorted(range(n), key=lambda i: (start[i], i))
        return play(order, way)[0], order, way

    seed = [1]

    def draw():
        seed[0] = (seed[0] * 1103515245 + 12345) % 2147483648
        return seed[0] / 2147483648.0

    shape = tuple(map(tuple, aft))
    if shape not in KEPT:
        fac, lean = [1.0] * n, [0.0] * n
        held = plan(fac, lean)
        for trial in range(TRIES):
            f2, l2 = list(fac), list(lean)
            a = int(draw() * n)
            for u in range(MUT):
                i = min(n - 1, a + int(draw() * 60))
                f2[i] = 0.2 + 2.8 * draw() ** 2
                l2[i] = 0.4 * draw() - 0.2
            new = plan(f2, l2)
            if new[0] <= held[0]:
                held, fac, lean = new, f2, l2
        best = held
        order, way = held[1:]
        now = play(order, way)
        for trial in range(MOVES):
            j, i = now[1][int(draw() * len(now[1]))]
            o2, w2, kind = list(order), way, draw()
            a, b = order.index(j), order.index(i)
            if kind < 0.2:
                c = i if draw() < 0.5 else j
                if len(ops[c]["alts"]) < 2:
                    continue
                w2 = list(way)
                w2[c] = ops[c]["alts"][1] if way[c] is ops[c]["alts"][0] else ops[c]["alts"][0]
            elif kind < 0.6:
                a = max(0, a - int(draw() ** 3 * 12))
                take = set([i])
                for u in reversed(order[a:b]):
                    if any(x in take for x in nxt[u]):
                        take.add(u)
                o2[a:b + 1] = [u for u in order[a:b + 1] if u in take] + [u for u in order[a:b + 1] if u not in take]
            else:
                b = min(n - 1, b + int(draw() ** 3 * 30))
                take = set([j])
                for u in order[a + 1:b + 1]:
                    if any(x in take for x in aft[u]):
                        take.add(u)
                o2[a:b + 1] = [u for u in order[a:b + 1] if u not in take] + [u for u in order[a:b + 1] if u in take]
            new = play(o2, w2, now[3], a)
            if new[0] <= now[0] + HEAT * (1 - trial / MOVES) * draw():
                now, order, way = new, o2, w2
                if now[0] < best[0]:
                    best = (now[0], order, way)
        KEPT[shape] = (best[1], [0 if best[2][i] is ops[i]["alts"][0] else 1 for i in range(n)], best[0])
    order = KEPT[shape][0]
    way = [ops[i]["alts"][KEPT[shape][1][i]] for i in range(n)]
    end = play(order, way)[2]
    place = dict((i, c) for c, i in enumerate(order))
    known, waits, done = {}, {}, {}
    for i in order:
        kn = known.setdefault(way[i][0], set())
        ws = []
        for j in sorted(deps[i], key=lambda j: -end[j]):
            if j not in kn:
                ws.append(j)
                kn.add(j)
                kn.update(done[j])
        waits[i] = ws
        done[i] = set(kn) if ops[i]["kind"] != "x" else set()
    need = set(j for i in order for j in waits[i])
    last = [i for i in order if ops[i]["kind"] == "o" and i not in need]
    need.update(i for i in range(n) if ops[i]["kind"] in "do")
    queue = {"v": g.vector, "a": g.scalar, "p": g.tensor, "g": g, "s": g.sync}
    user, count, sig = {}, {}, {}
    for i in order:
        o, q = ops[i], way[i][0]
        if o["kind"] == "x":
            sig[i] = o["ext"]
            continue
        s = None
        if i in need:
            dma = o["kind"] in "do"
            pool = q + "d" if dma else q
            names = [pool + str(u) for u in range(POOLS[pool])]
            free = [u for u in names if u not in user or user[u] in done[i]]
            s = free[0] if free else min(names, key=lambda u: place[user[u]])
            if not free:
                waits[i].append(user[s])
        for j in waits[i]:
            queue[q].wait_ge(T.sem[sig[j][0]], sig[j][1])
        ins = way[i][1]()
        if s is not None:
            user[s] = i
            count[s] = count.get(s, 0) + (16 if dma else 1)
            sig[i] = (s, count[s])
            ins.then_inc(T.sem[s], 16 if dma else 1)
    for i in last:
        queue[way[i][0]].wait_ge(T.sem[sig[i][0]], sig[i][1])
    g.wait_ge(T.sem.sent, sent)
